import numpy as np
import ml_dtypes


def mxq(x, axis, fmt="e4m3"):
    dtype, down = {"e4m3": (ml_dtypes.float8_e4m3fn, 7), "e5m2": (ml_dtypes.float8_e5m2, 14)}[fmt]
    v = np.moveaxis(np.asarray(x, np.float32).astype(ml_dtypes.bfloat16).astype(np.float64), axis, -1)
    blocks = v.reshape(v.shape[:-1] + (-1, 32))
    amax = np.abs(blocks).max(-1, keepdims=True)
    byte = np.maximum(np.where(amax > 0, np.frexp(amax)[1] - 1 + 127, 0) - down, 1)
    scale = np.exp2(byte - 127.0)
    codes = (blocks / scale).astype(np.float32).astype(dtype).astype(np.float64)
    return np.moveaxis((codes * scale).reshape(v.shape), -1, axis)


WIDE = False


def mx_kscale(k):
    if not WIDE:
        return np.ones(k)
    levels = np.array([10, -10, 5, -5, 0])
    if k % 512:
        return np.exp2(np.random.permutation(np.resize(levels, k // 32))).repeat(32)
    a = np.empty((k // 512, 16))
    for p in range(k // 512):
        a[p, :8] = np.random.permutation(np.resize(levels, 8))
        for g in range(8):
            far = levels[np.abs(levels - a[p, g]) >= 10]
            a[p, g + 8] = far[np.random.randint(len(far))]
    return np.exp2(a.ravel()).repeat(32)


def f64(x):
    return np.asarray(x).astype(np.float64)


def striped(idx):
    return np.tile(idx.reshape(-1, 16).T, (8, 1)).astype(np.uint16)


def unstriped(offs):
    return offs[:16].T.reshape(-1).astype(np.int64)


E2M1 = np.array([0.0, 0.5, 1.0, 1.5, 2.0, 3.0, 4.0, 6.0, -0.0, -0.5, -1.0, -1.5, -2.0, -3.0, -4.0, -6.0])


def pack_weight(w, fmt):
    k, n = w.shape
    w = f64(np.asarray(w, np.float32).astype(ml_dtypes.bfloat16)).reshape(k // 32, 32, n)
    amax = np.abs(w).max(1)
    if fmt == "e4m3":
        byte = np.frexp(amax)[1] - 1 + 127 - 7
    else:
        mant, ex = np.frexp(amax / 6.0)
        byte = np.where(mant > 0.5, ex, ex - 1) + 127
    byte = np.clip(np.where(amax > 0, byte, 1), 1, 254)
    scaled = (w * np.exp2(127.0 - byte)[:, None, :]).reshape(k, n).astype(np.float32)
    by_word = np.ascontiguousarray(scaled.reshape(k // 512, 128, 4, n).transpose(0, 1, 3, 2))
    if fmt == "e4m3":
        words = by_word.astype(ml_dtypes.float8_e4m3fn).view(np.uint8)
    else:
        c = by_word.astype(ml_dtypes.float4_e2m1fn).view(np.uint8) & 0xF
        words = (c[..., 0::2] | (c[..., 1::2] << 4)).reshape(k // 512, 128, 2 * n)
    return np.ascontiguousarray(words), np.ascontiguousarray(byte.astype(np.uint8).reshape(k // 512, 16, n))


def unpack_weight(words, scales, fmt):
    g, _, n = scales.shape
    words = np.ascontiguousarray(words).reshape(g, 128, n, -1)
    if fmt == "e4m3":
        vals = words.view(ml_dtypes.float8_e4m3fn).astype(np.float64)
    else:
        nib = np.empty((g, 128, n, 4), np.uint8)
        nib[..., 0::2] = words & 0xF
        nib[..., 1::2] = words >> 4
        vals = E2M1[nib]
    vals = vals * np.repeat(np.exp2(scales.astype(np.float64) - 127.0), 8, axis=1)[..., None]
    return vals.transpose(0, 1, 3, 2).reshape(g * 512, n)


def gelu(v):
    return 0.5 * v * (1.0 + np.tanh(np.sqrt(2.0 / np.pi) * (v + 0.044715 * v**3)))


def striped8(idx):
    return np.concatenate([v.reshape(-1, 16).T for v in idx]).astype(np.uint16)


def unstriped8(offs):
    return np.stack([offs[16 * g:16 * g + 16].T.reshape(-1) for g in range(8)]).astype(np.int64)


def runs(v, idx8):
    k = np.arange(v.shape[0])
    return v[k[:, None], idx8[k % 512 // 64]]


K, T, S, H, N = 1024, 2048, 1024, 1024, 512


def setup_inputs():
    n = np.random.standard_normal
    s = mx_kscale(K)[:, None]
    u = mx_kscale(H)[:, None]
    tab_words, tab_scales = pack_weight(n((K, T)) * s, "e4m3")
    offs = striped8(np.stack([np.random.permutation(T)[:S] for _ in range(8)]))
    wb = n((K, H)) / np.sqrt(K) / s * u.T
    wf_words, wf_scales = pack_weight(n((K, H)) / np.sqrt(K) / s * u.T, "e2m1")
    wx_words, wx_scales = pack_weight(2.0 * n((H, N)) / np.sqrt(H) / u, "e4m3")
    return {
        "tab_words": tab_words, "tab_scales": tab_scales,
        "offs": offs,
        "wb": wb.astype(np.float32),
        "wf_words": wf_words, "wf_scales": wf_scales,
        "wx_words": wx_words, "wx_scales": wx_scales,
        "wind": n((N, S)).astype(np.float32),
    }


def reference(tab_words, tab_scales, offs, wb, wf_words, wf_scales, wx_words, wx_scales, wind):
    v = runs(unpack_weight(tab_words, tab_scales, "e4m3"), unstriped8(offs))
    back = mxq(f64(wb), 0, "e4m3").T @ v
    fwd = unpack_weight(wf_words, wf_scales, "e2m1").T @ v
    rising = np.maximum(0.0, np.minimum(back, fwd))
    falling = np.minimum(0.0, np.maximum(back, fwd))
    h = rising + falling
    face = unpack_weight(wx_words, wx_scales, "e4m3").T @ mxq(h, 0, "e4m3")
    return f64(wind) * face

@@ -1,0 +1,307 @@
+from contextlib import ExitStack
+
+import concourse.mybir as mybir
+from concourse.masks import make_identity
+
+K, T, S, H, N = 1024, 2048, 1024, 1024, 512
+FLOPS = 2 * K * H * S * 2 + 2 * H * N * S
+
+F32 = mybir.dt.float32
+BF16 = mybir.dt.bfloat16
+I32 = mybir.dt.int32
+U32 = mybir.dt.uint32
+U16 = mybir.dt.uint16
+U8 = mybir.dt.uint8
+E4M3 = mybir.dt.float8_e4m3fn_x4
+E2M1 = mybir.dt.float4_e2m1fn_x4
+ALU = mybir.AluOpType
+
+P = 128
+PASS = 512
+
+
+def tile_list_minmod_neighbour_fluxes_kernel(
+    tc, tab_words, tab_scales, offs, wb, wf_words, wf_scales, wx_words, wx_scales, wind, out
+):
+    nc = tc.nc
+    with ExitStack() as ctx:
+        keep = ctx.enter_context(tc.tile_pool(name="keep", bufs=1))
+        shared = ctx.enter_context(tc.tile_pool(name="shared", bufs=1))
+        ring = ctx.enter_context(tc.tile_pool(name="ring", bufs=3))
+        ps_b = ctx.enter_context(tc.psum_pool(name="ps_b", bufs=3))
+        ps_f = ctx.enter_context(tc.psum_pool(name="ps_f", bufs=2))
+        ps_t = ctx.enter_context(tc.psum_pool(name="ps_t", bufs=1))
+        ps_o = ctx.enter_context(tc.psum_pool(name="ps_o", bufs=2))
+
+        def held(name, shape, dtype, slot=None):
+            return keep.tile(shape, dtype, name=name, tag=slot or name, align_bytes=64)
+
+        offsets = keep.tile([P, S // 16], U16, name="offsets")
+        nc.sync.dma_start(offsets[:], offs)
+
+        win = shared.tile([P, T], U8, name="win", align_bytes=64, offset=3072)
+        for a in range(2):
+            nc.sync.dma_start(
+                win[:].bitcast(I32)[a:P:2, :],
+                tab_scales[a].bitcast(I32).unsqueeze(1).to_broadcast([16, 4, T // 4]),
+            )
+        tab = [held("tab%d" % a, [P, T], I32, "big%d" % a) for a in range(2)]
+        for a in range(2):
+            nc.sync.dma_start(tab[a][:], tab_words[a].rearrange("p t i -> p (t i)").bitcast(I32))
+
+        raw = {}
+
+        def load_wb(a, c0, width, into):
+            raw[a, c0] = into
+            nc.sync.dma_start(
+                into, wb[PASS * a : PASS * (a + 1), c0 : c0 + width].rearrange("(p i) c -> p i c", i=4)
+            )
+
+        raw00 = held("raw00", [P, 4, 256], F32)
+        load_wb(0, 0, 256, raw00[:])
+
+        wfs = held("wfs", [P, 2, H], U8)
+        nc.vector.memset(wfs[:].bitcast(I32), 0)
+        for d in range(4):
+            nc.gpsimd.dma_start(
+                wfs[:].bitcast(I32)[32 * d : 32 * d + 4],
+                wf_scales.bitcast(I32)[:, 4 * d : 4 * d + 4, :].rearrange("a r c -> r a c"),
+            )
+        vs = [held("vs%d" % a, [P, S], U8) for a in range(2)]
+        for a in range(2):
+            nc.vector.memset(vs[a][:].bitcast(I32), 0)
+        wxs = held("wxs", [P, 2, N], U8)
+        nc.vector.memset(wxs[:].bitcast(I32), 0)
+        for d in range(4):
+            nc.gpsimd.dma_start(
+                wxs[:].bitcast(I32)[32 * d : 32 * d + 4],
+                wx_scales.bitcast(I32)[:, 4 * d : 4 * d + 4, :].rearrange("a r c -> r a c"),
+            )
+        ident = held("ident", [P, P], F32)
+        make_identity(nc, ident[:])
+
+        gs = held("gs", [P, S], U8)
+        nc.vector.tensor_copy(gs[:], win[:].indirect(offsets[:]))
+
+        def move(a, r):
+            nc.sync.dma_start(vs[a][:].bitcast(I32)[r:P:32, :], gs[:].bitcast(I32)[8 * r + a : P : 32, :])
+
+        late = shared.tile([P, 3072], F32, name="late", align_bytes=64, offset=4096)
+        wf = shared.tile([P, 4 * H], U8, name="wf", align_bytes=64, offset=0)
+
+        def late_raw(x):
+            return late[:, 1024 * x : 1024 * (x + 1)].rearrange("p (i c) -> p i c", i=4)
+
+        moves = [(a, r) for a in range(2) for r in range(4)]
+        for a, r in moves[:6]:
+            move(a, r)
+        load_wb(1, 0, 256, late_raw(0))
+        nc.sync.dma_start(
+            wf[:].bitcast(I32).rearrange("p (a c) -> p a c", a=2),
+            wf_words.bitcast(I32).rearrange("a p c -> p a c"),
+        )
+        for a, r in moves[6:]:
+            move(a, r)
+        load_wb(0, 256, 256, late_raw(1))
+        load_wb(1, 256, 256, late_raw(2))
+
+        v = {}
+
+        def gather_words(a, half):
+            v[a, half] = held("v%d_%d" % (a, half), [P, 512], I32)
+            nc.vector.tensor_copy(
+                v[a, half][:].bitcast(U32), tab[a][:].bitcast(U32).indirect(offsets[:, 32 * half : 32 * (half + 1)])
+            )
+
+        def v_codes(a, jt):
+            return v[a, jt // 4][:, 128 * (jt % 4) : 128 * (jt % 4 + 1)].bitcast(E4M3)
+
+        def v_scales(a, jt):
+            return vs[a][:, 128 * jt : 128 * (jt + 1)]
+
+        grouped, wbq, wbs = {}, {}, {}
+
+        def cast_wb(a, c0, width):
+            grouped[a, c0] = held("grp%d_%d" % (a, c0), [P, 4 * width], BF16)
+            dst = grouped[a, c0][:].rearrange("p (u m e i) -> p m i u e", u=2, e=2, i=4)
+            src = raw[a, c0].rearrange("p i (m u e) -> p m i u e", u=2, e=2)
+            for m0 in range(0, width // 4, 64):
+                nc.scalar.copy(dst[:, m0 : m0 + 64], src[:, m0 : m0 + 64])
+
+        def quant_wb(a, c0, width):
+            wbq[a, c0] = held("wbq%d_%d" % (a, c0), [P, width], I32)
+            wbs[a, c0] = held("wbs%d_%d" % (a, c0), [P, width], U8)
+            nc.vector.quantize_mx(out=wbq[a, c0][:].bitcast(E4M3), scales=wbs[a, c0][:], in_=grouped[a, c0][:])
+
+        f_sb = {(s, b): held("f%d_%d" % (s, b), [P, 4, 256], F32) for s in range(2) for b in range(4)}
+        h_sb = {(s, b): held("h%d_%d" % (s, b), [P, 4, 256], BF16) for s in range(2) for b in range(4)}
+
+        def forward(s, jt):
+            bank = ps_f.tile([P, 512], F32, name="fbank")
+            for a in range(2):
+                nc.tensor.matmul_mx(
+                    out=bank[:],
+                    lhsT=v_codes(a, jt),
+                    lhsT_scale=v_scales(a, jt),
+                    rhs=wf[:, 2048 * a + 1024 * s : 2048 * a + 1024 * (s + 1)].bitcast(E2M1),
+                    rhs_scale=wfs[:, a, 512 * s : 512 * (s + 1)],
+                    start=(a == 0),
+                    stop=(a == 1),
+                )
+            jj = jt % 2
+            nc.scalar.copy(
+                f_sb[s, jt // 2][:, 2 * jj : 2 * jj + 2, :].rearrange("p u (m e) -> p u m e", e=2),
+                bank[:].rearrange("p (m u e) -> p u m e", u=2, e=2),
+            )
+
+        def backward(c0, width, jts):
+            bank = ps_b.tile([P, 512], F32, name="bbank")
+            for x, jt in enumerate(jts):
+                for a in range(2):
+                    nc.tensor.matmul_mx(
+                        out=bank[:, width * x : width * (x + 1)],
+                        lhsT=v_codes(a, jt),
+                        lhsT_scale=v_scales(a, jt),
+                        rhs=wbq[a, c0][:].bitcast(E4M3),
+                        rhs_scale=wbs[a, c0][:],
+                        start=(a == 0),
+                        stop=(a == 1),
+                    )
+            return bank
+
+        def place(tiles, c0, width, jts):
+            s, b = c0 // 512, jts[0] // 2
+            first, run = 2 * (jts[0] % 2), width // 2
+            col = (c0 % 512) // 2
+            return tiles[s, b][:, first : first + 2 * len(jts), col : col + run]
+
+        def lower(unit):
+            bank = backward(*unit)
+            run = unit[1] // 2
+            t1 = ring.tile([P, 512], F32, name="t1")
+            nc.vector.scalar_tensor_tensor(
+                out=t1[:].rearrange("p (x c) -> p x c", c=run),
+                in0=bank[:].rearrange("p (x c) -> p x c", c=run),
+                scalar=0.0,
+                in1=place(f_sb, *unit),
+                op0=ALU.min,
+                op1=ALU.max,
+            )
+            return bank, t1
+
+        def upper(unit, bank, t1):
+            run = unit[1] // 2
+            nc.vector.scalar_tensor_tensor(
+                out=place(h_sb, *unit),
+                in0=bank[:].rearrange("p (x c) -> p x c", c=run),
+                scalar=0.0,
+                in1=t1[:].rearrange("p (x c) -> p x c", c=run),
+                op0=ALU.max,
+                op1=ALU.min,
+            )
+
+        h_t = {}
+        hq = [held("hq%d" % s, [P, S], I32) for s in range(2)]
+        hs = [held("hs%d" % s, [P, S], U8) for s in range(2)]
+
+        def turn(s, b):
+            bank = ps_t.tile([P, 4, P], F32, name="tbank")
+            for x in range(4):
+                nc.tensor.transpose(bank[:, x, :], h_sb[s, b][:, x, :].bitcast(F32), ident[:])
+            h_t[s, b] = held("ht%d_%d" % (s, b), [P, 1024], BF16)
+            nc.scalar.copy(
+                h_t[s, b][:].bitcast(F32).rearrange("p (y j u) -> p y j u", y=2, u=2),
+                bank[:].rearrange("p (y u) j -> p y j u", u=2),
+            )
+
+        def quant_h(s, b):
+            cols = slice(256 * b, 256 * (b + 1))
+            nc.vector.quantize_mx(out=hq[s][:, cols].bitcast(E4M3), scales=hs[s][:, cols], in_=h_t[s, b][:])
+
+        faces = {}
+        wx = []
+
+        def face(b):
+            cols = slice(256 * b, 256 * (b + 1))
+            for g in range(2):
+                bank = ps_o.tile([P, 2, 256], F32, name="obank")
+                for y in range(2):
+                    rows = slice(128 * (2 * g + y), 128 * (2 * g + y + 1))
+                    for s in range(2):
+                        nc.tensor.matmul_mx(
+                            out=bank[:, y, :],
+                            lhsT=wx[0][:, s, rows].bitcast(E4M3),
+                            lhsT_scale=wxs[:, s, rows],
+                            rhs=hq[s][:, cols].bitcast(E4M3),
+                            rhs_scale=hs[s][:, cols],
+                            start=(s == 0),
+                            stop=(s == 1),
+                        )
+                faces[b, g] = bank
+
+        def flux(b, g):
+            res = held("res%d_%d" % (b, g), [P, 2, 256], F32)
+            nc.vector.tensor_tensor(res[:], faces[b, g][:], winds[b // 2][:, 2 * g : 2 * g + 2, 256 * (b % 2) : 256 * (b % 2 + 1)], ALU.mult)
+            nc.sync.dma_start(
+                out[256 * g : 256 * (g + 1), 256 * b : 256 * (b + 1)].rearrange("(y p) j -> p y j", p=P), res[:]
+            )
+
+        gather_words(0, 0)
+        gather_words(1, 0)
+        for a in range(2):
+            cast_wb(a, 0, 256)
+            quant_wb(a, 0, 256)
+        forward(0, 0)
+        forward(0, 1)
+        gather_words(0, 1)
+        gather_words(1, 1)
+        for a in range(2):
+            wide = held("raw%d_512" % a, [P, 4, 512], F32, "big%d" % a)
+            load_wb(a, 512, 512, wide[:])
+
+        winds = {}
+
+        def load_wind(x):
+            winds[x] = held("wind%d" % x, [P, 4, 512], F32, "big%d" % x)
+            nc.sync.dma_start(winds[x][:], wind[:, 512 * x : 512 * (x + 1)].rearrange("(m p) j -> p m j", p=P))
+
+        def load_wx():
+            wx.append(held("wx", [P, 2, N], I32, "grp0_256"))
+            nc.sync.dma_start(wx[0][:], wx_words.rearrange("a p c i -> p a (c i)").bitcast(I32))
+
+        units = []
+        for half in range(2):
+            for c0 in (0, 256):
+                for b in (2 * half, 2 * half + 1):
+                    units.append((c0, 256, (2 * b, 2 * b + 1)))
+        for jt in range(8):
+            units.append((512, 512, (jt,)))
+
+        before = {i: [] for i in range(len(units) + 4)}
+        before[1] += [lambda: forward(0, 2), lambda: forward(0, 3)]
+        before[1] += [lambda: cast_wb(0, 256, 256), lambda: cast_wb(1, 256, 256)]
+        before[2] += [lambda: quant_wb(0, 256, 256), lambda: quant_wb(1, 256, 256), load_wx]
+        before[3] += [lambda: forward(0, 4), lambda: forward(0, 5)]
+        before[4] += [lambda: forward(0, 6), lambda: forward(0, 7), lambda: turn(0, 0)]
+        before[5] += [lambda: cast_wb(0, 512, 512), lambda: turn(0, 1)]
+        before[6] += [lambda: cast_wb(1, 512, 512), lambda: quant_wb(0, 512, 512), lambda: quant_h(0, 0)]
+        before[7] += [lambda: forward(1, 0), lambda: quant_wb(1, 512, 512), lambda: quant_h(0, 1)]
+        before[8] += [lambda: turn(0, 2), lambda: load_wind(0), lambda: load_wind(1)]
+        before[9] += [lambda: turn(0, 3)]
+        before[10] += [lambda: quant_h(0, 2)]
+        before[11] += [lambda: quant_h(0, 3)]
+        for jt in range(1, 8):
+            before[7 + jt].append(lambda jt=jt: forward(1, jt))
+        for b in range(4):
+            before[11 + 2 * b].append(lambda b=b: turn(1, b))
+            before[12 + 2 * b] += [lambda b=b: quant_h(1, b), lambda b=b: face(b)]
+            before[13 + 2 * b] += [lambda b=b: flux(b, 0), lambda b=b: flux(b, 1)]
+
+        pending = None
+        for i in range(len(units) + 4):
+            for step in before[i]:
+                step()
+            made = lower(units[i]) if i < len(units) else None
+            if pending is not None:
+                upper(units[i - 1], *pending)
+            pending = made

@@ -39,26 +39,39 @@ def tile_list_minmod_neighbour_fluxes_kernel(
         offsets = keep.tile([P, S // 16], U16, name="offsets")
         nc.sync.dma_start(offsets[:], offs)
 
-        win = shared.tile([P, T], U8, name="win", align_bytes=64, offset=3072)
+        def placed(name, shape, dtype, kib):
+            return shared.tile(shape, dtype, name=name, align_bytes=64, offset=1024 * kib)
+
+        win = placed("win", [P, T], U8, 27)
         for a in range(2):
-            nc.sync.dma_start(
-                win[:].bitcast(I32)[a:P:2, :],
-                tab_scales[a].bitcast(I32).unsqueeze(1).to_broadcast([16, 4, T // 4]),
-            )
-        tab = [held("tab%d" % a, [P, T], I32, "big%d" % a) for a in range(2)]
-        for a in range(2):
-            nc.sync.dma_start(tab[a][:], tab_words[a].rearrange("p t i -> p (t i)").bitcast(I32))
+            for e in range(2):
+                nc.sync.dma_start(
+                    win[:].bitcast(I32)[2 * a + e : P : 4, :],
+                    tab_scales[a].bitcast(I32)[e::2].unsqueeze(1).to_broadcast([8, 4, T // 4]),
+                )
+        tab = [placed("tab0", [P, T], I32, 0), placed("tab1", [P, T], I32, 12)]
+        nc.sync.dma_start(tab[0][:], tab_words[0].rearrange("p t i -> p (t i)").bitcast(I32))
+        nc.sync.dma_start(tab[1][:], tab_words[1].rearrange("p t i -> p (t i)").bitcast(I32))
 
         raw = {}
 
         def load_wb(a, c0, width, into):
             raw[a, c0] = into
             nc.sync.dma_start(
-                into, wb[PASS * a : PASS * (a + 1), c0 : c0 + width].rearrange("(p i) c -> p i c", i=4)
+                into[:], wb[PASS * a : PASS * (a + 1), c0 : c0 + width].rearrange("(p i) c -> p i c", i=4)
             )
 
-        raw00 = held("raw00", [P, 4, 256], F32)
-        load_wb(0, 0, 256, raw00[:])
+        wf = {}
+
+        def load_wf(s, into):
+            wf[s] = into
+            nc.sync.dma_start(
+                into[:].bitcast(I32),
+                wf_words.bitcast(I32)[:, :, 256 * s : 256 * (s + 1)].rearrange("a p c -> p a c"),
+            )
+
+        load_wf(0, held("wf0", [P, 2, H], U8))
+        load_wb(0, 0, 256, held("raw00", [P, 4, 256], F32))
 
         wfs = held("wfs", [P, 2, H], U8)
         nc.vector.memset(wfs[:].bitcast(I32), 0)
@@ -68,42 +81,18 @@ def tile_list_minmod_neighbour_fluxes_kernel(
                 wf_scales.bitcast(I32)[:, 4 * d : 4 * d + 4, :].rearrange("a r c -> r a c"),
             )
         vs = [held("vs%d" % a, [P, S], U8) for a in range(2)]
-        for a in range(2):
-            nc.vector.memset(vs[a][:].bitcast(I32), 0)
-        wxs = held("wxs", [P, 2, N], U8)
-        nc.vector.memset(wxs[:].bitcast(I32), 0)
-        for d in range(4):
-            nc.gpsimd.dma_start(
-                wxs[:].bitcast(I32)[32 * d : 32 * d + 4],
-                wx_scales.bitcast(I32)[:, 4 * d : 4 * d + 4, :].rearrange("a r c -> r a c"),
-            )
-        ident = held("ident", [P, P], F32)
-        make_identity(nc, ident[:])
+        nc.vector.memset(vs[1][:].bitcast(I32), 0)
 
         gs = held("gs", [P, S], U8)
         nc.vector.tensor_copy(gs[:], win[:].indirect(offsets[:]))
-
-        def move(a, r):
-            nc.sync.dma_start(vs[a][:].bitcast(I32)[r:P:32, :], gs[:].bitcast(I32)[8 * r + a : P : 32, :])
-
-        late = shared.tile([P, 3072], F32, name="late", align_bytes=64, offset=4096)
-        wf = shared.tile([P, 4 * H], U8, name="wf", align_bytes=64, offset=0)
-
-        def late_raw(x):
-            return late[:, 1024 * x : 1024 * (x + 1)].rearrange("p (i c) -> p i c", i=4)
-
-        moves = [(a, r) for a in range(2) for r in range(4)]
-        for a, r in moves[:6]:
-            move(a, r)
-        load_wb(1, 0, 256, late_raw(0))
-        nc.sync.dma_start(
-            wf[:].bitcast(I32).rearrange("p (a c) -> p a c", a=2),
-            wf_words.bitcast(I32).rearrange("a p c -> p a c"),
-        )
-        for a, r in moves[6:]:
-            move(a, r)
-        load_wb(0, 256, 256, late_raw(1))
-        load_wb(1, 256, 256, late_raw(2))
+        nc.vector.tensor_copy(vs[0][:].bitcast(I32), gs[:].bitcast(I32))
+        for a, r in [(1, 0), (1, 1), (1, 2), (1, 3), (0, 2), (0, 3)]:
+            first = 16 * (r // 2) + 2 * a + r % 2
+            queue = nc.gpsimd if (a, r) == (0, 3) else nc.sync
+            queue.dma_start(vs[a][:].bitcast(I32)[r:P:32, :], gs[:].bitcast(I32)[first:P:32, :])
+        load_wb(1, 0, 256, placed("raw10", [P, 4, 256], F32, 28))
+        ident = held("ident", [P, P], F32)
+        make_identity(nc, ident[:])
 
         v = {}
 
@@ -124,9 +113,10 @@ def tile_list_minmod_neighbour_fluxes_kernel(
         def cast_wb(a, c0, width):
             grouped[a, c0] = held("grp%d_%d" % (a, c0), [P, 4 * width], BF16)
             dst = grouped[a, c0][:].rearrange("p (u m e i) -> p m i u e", u=2, e=2, i=4)
-            src = raw[a, c0].rearrange("p i (m u e) -> p m i u e", u=2, e=2)
+            src = raw[a, c0][:].rearrange("p i (m u e) -> p m i u e", u=2, e=2)
             for m0 in range(0, width // 4, 64):
-                nc.scalar.copy(dst[:, m0 : m0 + 64], src[:, m0 : m0 + 64])
+                copy = nc.vector.tensor_copy if (a, c0) in [(1, 0), (1, 256)] else nc.scalar.copy
+                copy(dst[:, m0 : m0 + 64], src[:, m0 : m0 + 64])
 
         def quant_wb(a, c0, width):
             wbq[a, c0] = held("wbq%d_%d" % (a, c0), [P, width], I32)
@@ -143,7 +133,7 @@ def tile_list_minmod_neighbour_fluxes_kernel(
                     out=bank[:],
                     lhsT=v_codes(a, jt),
                     lhsT_scale=v_scales(a, jt),
-                    rhs=wf[:, 2048 * a + 1024 * s : 2048 * a + 1024 * (s + 1)].bitcast(E2M1),
+                    rhs=wf[s][:, a, :].bitcast(E2M1),
                     rhs_scale=wfs[:, a, 512 * s : 512 * (s + 1)],
                     start=(a == 0),
                     stop=(a == 1),
@@ -204,47 +194,61 @@ def tile_list_minmod_neighbour_fluxes_kernel(
         hq = [held("hq%d" % s, [P, S], I32) for s in range(2)]
         hs = [held("hs%d" % s, [P, S], U8) for s in range(2)]
 
-        def turn(s, b):
-            bank = ps_t.tile([P, 4, P], F32, name="tbank")
-            for x in range(4):
-                nc.tensor.transpose(bank[:, x, :], h_sb[s, b][:, x, :].bitcast(F32), ident[:])
-            h_t[s, b] = held("ht%d_%d" % (s, b), [P, 1024], BF16)
+        def cells(jts):
+            return slice(128 * jts[0], 128 * (jts[-1] + 1))
+
+        def turn(s, jts):
+            bank = ps_t.tile([P, 2 * len(jts), P], F32, name="tbank")
+            for y, jt in reversed(list(enumerate(jts))):
+                for u in range(2):
+                    words = h_sb[s, jt // 2][:, 2 * (jt % 2) + u, :].bitcast(F32)
+                    nc.tensor.transpose(bank[:, 2 * y + u, :], words, ident[:])
+            h_t[s, jts] = held("ht%d_%d" % (s, jts[0]), [P, 512 * len(jts)], BF16)
             nc.scalar.copy(
-                h_t[s, b][:].bitcast(F32).rearrange("p (y j u) -> p y j u", y=2, u=2),
+                h_t[s, jts][:].bitcast(F32).rearrange("p (y j u) -> p y j u", y=len(jts), u=2),
                 bank[:].rearrange("p (y u) j -> p y j u", u=2),
             )
 
-        def quant_h(s, b):
-            cols = slice(256 * b, 256 * (b + 1))
-            nc.vector.quantize_mx(out=hq[s][:, cols].bitcast(E4M3), scales=hs[s][:, cols], in_=h_t[s, b][:])
+        def quant_h(s, jts):
+            cols = cells(jts)
+            nc.vector.quantize_mx(out=hq[s][:, cols].bitcast(E4M3), scales=hs[s][:, cols], in_=h_t[s, jts][:])
 
         faces = {}
-        wx = []
+        late = {}
 
-        def face(b):
-            cols = slice(256 * b, 256 * (b + 1))
-            for g in range(2):
-                bank = ps_o.tile([P, 2, 256], F32, name="obank")
-                for y in range(2):
-                    rows = slice(128 * (2 * g + y), 128 * (2 * g + y + 1))
+        def face(jts):
+            cols = cells(jts)
+            per_bank = 4 // len(jts)
+            for g in range(len(jts)):
+                bank = ps_o.tile([P, per_bank, 128 * len(jts)], F32, name="obank")
+                for y in range(per_bank):
+                    rows = slice(128 * (per_bank * g + y), 128 * (per_bank * g + y + 1))
                     for s in range(2):
                         nc.tensor.matmul_mx(
                             out=bank[:, y, :],
-                            lhsT=wx[0][:, s, rows].bitcast(E4M3),
-                            lhsT_scale=wxs[:, s, rows],
+                            lhsT=late["wx"][:, s, rows].bitcast(E4M3),
+                            lhsT_scale=late["wxs"][:, s, rows],
                             rhs=hq[s][:, cols].bitcast(E4M3),
                             rhs_scale=hs[s][:, cols],
                             start=(s == 0),
                             stop=(s == 1),
                         )
-                faces[b, g] = bank
+                faces[jts, g] = bank
 
-        def flux(b, g):
-            res = held("res%d_%d" % (b, g), [P, 2, 256], F32)
-            nc.vector.tensor_tensor(res[:], faces[b, g][:], winds[b // 2][:, 2 * g : 2 * g + 2, 256 * (b % 2) : 256 * (b % 2 + 1)], ALU.mult)
-            nc.sync.dma_start(
-                out[256 * g : 256 * (g + 1), 256 * b : 256 * (b + 1)].rearrange("(y p) j -> p y j", p=P), res[:]
-            )
+        def flux(jts):
+            per_bank, width = 4 // len(jts), 128 * len(jts)
+            inside = 128 * (jts[0] % 4)
+            for g in range(len(jts)):
+                res = held("res%d_%d" % (jts[0], g), [P, per_bank, width], F32)
+                factor = winds[jts[0] // 4][:, per_bank * g : per_bank * (g + 1), inside : inside + width]
+                if (jts[0], g) in []:
+                    sums = ring.tile([P, per_bank, width], F32, name="sums")
+                    nc.scalar.copy(sums[:], faces[jts, g][:])
+                    nc.gpsimd.tensor_tensor(res[:], sums[:], factor, ALU.mult)
+                else:
+                    nc.vector.tensor_tensor(res[:], faces[jts, g][:], factor, ALU.mult)
+                rows = slice(128 * per_bank * g, 128 * per_bank * (g + 1))
+                nc.sync.dma_start(out[rows, cells(jts)].rearrange("(y p) j -> p y j", p=P), res[:])
 
         gather_words(0, 0)
         gather_words(1, 0)
@@ -256,52 +260,65 @@ def tile_list_minmod_neighbour_fluxes_kernel(
         gather_words(0, 1)
         gather_words(1, 1)
         for a in range(2):
-            wide = held("raw%d_512" % a, [P, 4, 512], F32, "big%d" % a)
-            load_wb(a, 512, 512, wide[:])
+            load_wb(a, 256, 256, placed("raw%d_256" % a, [P, 4, 256], F32, 4 * a))
+        for a in range(2):
+            load_wb(a, 512, 512, placed("raw%d_512" % a, [P, 4, 512], F32, 8 + 8 * a))
+        load_wf(1, placed("wf1", [P, 2, H], U8, 28))
 
         winds = {}
 
         def load_wind(x):
-            winds[x] = held("wind%d" % x, [P, 4, 512], F32, "big%d" % x)
+            winds[x] = placed("wind%d" % x, [P, 4, 512], F32, 8 + 8 * x)
             nc.sync.dma_start(winds[x][:], wind[:, 512 * x : 512 * (x + 1)].rearrange("(m p) j -> p m j", p=P))
 
         def load_wx():
-            wx.append(held("wx", [P, 2, N], I32, "grp0_256"))
-            nc.sync.dma_start(wx[0][:], wx_words.rearrange("a p c i -> p a (c i)").bitcast(I32))
+            late["wx"] = placed("wx", [P, 2, N], I32, 0)
+            nc.sync.dma_start(late["wx"][:], wx_words.rearrange("a p c i -> p a (c i)").bitcast(I32))
+            late["wxs"] = placed("wxs", [P, 2, N], U8, 4)
+            nc.gpsimd.memset(late["wxs"][:].bitcast(I32), 0)
+            for d in range(4):
+                nc.sync.dma_start(
+                    late["wxs"][:].bitcast(I32)[32 * d : 32 * d + 4],
+                    wx_scales.bitcast(I32)[:, 4 * d : 4 * d + 4, :].rearrange("a r c -> r a c"),
+                )
 
-        units = []
-        for half in range(2):
-            for c0 in (0, 256):
-                for b in (2 * half, 2 * half + 1):
-                    units.append((c0, 256, (2 * b, 2 * b + 1)))
-        for jt in range(8):
-            units.append((512, 512, (jt,)))
-
-        before = {i: [] for i in range(len(units) + 4)}
-        before[1] += [lambda: forward(0, 2), lambda: forward(0, 3)]
-        before[1] += [lambda: cast_wb(0, 256, 256), lambda: cast_wb(1, 256, 256)]
-        before[2] += [lambda: quant_wb(0, 256, 256), lambda: quant_wb(1, 256, 256), load_wx]
-        before[3] += [lambda: forward(0, 4), lambda: forward(0, 5)]
-        before[4] += [lambda: forward(0, 6), lambda: forward(0, 7), lambda: turn(0, 0)]
-        before[5] += [lambda: cast_wb(0, 512, 512), lambda: turn(0, 1)]
-        before[6] += [lambda: cast_wb(1, 512, 512), lambda: quant_wb(0, 512, 512), lambda: quant_h(0, 0)]
-        before[7] += [lambda: forward(1, 0), lambda: quant_wb(1, 512, 512), lambda: quant_h(0, 1)]
-        before[8] += [lambda: turn(0, 2), lambda: load_wind(0), lambda: load_wind(1)]
-        before[9] += [lambda: turn(0, 3)]
-        before[10] += [lambda: quant_h(0, 2)]
-        before[11] += [lambda: quant_h(0, 3)]
-        for jt in range(1, 8):
-            before[7 + jt].append(lambda jt=jt: forward(1, jt))
-        for b in range(4):
-            before[11 + 2 * b].append(lambda b=b: turn(1, b))
-            before[12 + 2 * b] += [lambda b=b: quant_h(1, b), lambda b=b: face(b)]
-            before[13 + 2 * b] += [lambda b=b: flux(b, 0), lambda b=b: flux(b, 1)]
+        pairs = [(0, 1), (2, 3), (4, 5), (6, 7)]
+        units = [(0, 256, (0, 1)), (0, 256, (2, 3)), (256, 256, (0, 1)), (256, 256, (2, 3)), (0, 256, (4, 5)), (0, 256, (6, 7)), (256, 256, (4, 5)), (256, 256, (6, 7)), (512, 512, (0,)), (512, 512, (1,)), (512, 512, (2,)), (512, 512, (3,)), (512, 512, (4,)), (512, 512, (5,)), (512, 512, (6,)), (512, 512, (7,))]
+        before = {i: [] for i in range(-4, len(units) + 5)}
+        seen = {(0, 0), (0, 1), 0}
+        last = {}
+        for i, (c0, width, jts) in enumerate(units):
+            for jt in jts:
+                last[c0 // 512, jt] = i
+                if (c0 // 512, jt) not in seen:
+                    seen.add((c0 // 512, jt))
+                    before[max(i - 2, 0)].append(lambda s=c0 // 512, jt=jt: forward(s, jt))
+            if c0 not in seen:
+                seen.add(c0)
+                for a in range(2):
+                    before[i - 2 + a].append(lambda a=a, c0=c0, width=width: cast_wb(a, c0, width))
+                    before[min(i - 2 + a + 1, i)].append(lambda a=a, c0=c0, width=width: quant_wb(a, c0, width))
+                before[i].append(load_wx if c0 == 256 else lambda: [load_wind(x) for x in range(2)])
+        turned = {}
+        for jts in pairs:
+            at = max(last[0, jts[-1]] + 2, last[1, jts[0]] - 2)
+            before[at].append(lambda jts=jts: turn(0, jts))
+            before[at + 1].append(lambda jts=jts: quant_h(0, jts))
+            for jt in jts:
+                turned[jt] = at + 1
+        for jts in [(0, 1), (2, 3), (4, 5), (6,), (7,)]:
+            done = last[1, jts[-1]] + 2
+            before[done].append(lambda jts=jts: turn(1, jts))
+            before[done + 1].append(lambda jts=jts: quant_h(1, jts))
+            at = max(done + 1, turned[jts[-1]])
+            before[at].append(lambda jts=jts: face(jts))
+            before[at + 1].append(lambda jts=jts: flux(jts))
 
         pending = None
-        for i in range(len(units) + 4):
+        for i in range(-4, len(units) + 5):
             for step in before[i]:
                 step()
-            made = lower(units[i]) if i < len(units) else None
+            made = lower(units[i]) if 0 <= i < len(units) else None
             if pending is not None:
                 upper(units[i - 1], *pending)
             pending = made

@@ -28,8 +28,7 @@ def tile_list_minmod_neighbour_fluxes_kernel(
         keep = ctx.enter_context(tc.tile_pool(name="keep", bufs=1))
         shared = ctx.enter_context(tc.tile_pool(name="shared", bufs=1))
         ring = ctx.enter_context(tc.tile_pool(name="ring", bufs=3))
-        ps_b = ctx.enter_context(tc.psum_pool(name="ps_b", bufs=3))
-        ps_f = ctx.enter_context(tc.psum_pool(name="ps_f", bufs=2))
+        ps_b = ctx.enter_context(tc.psum_pool(name="ps_b", bufs=5))
         ps_t = ctx.enter_context(tc.psum_pool(name="ps_t", bufs=1))
         ps_o = ctx.enter_context(tc.psum_pool(name="ps_o", bufs=2))
 
@@ -115,7 +114,15 @@ def tile_list_minmod_neighbour_fluxes_kernel(
             dst = grouped[a, c0][:].rearrange("p (u m e i) -> p m i u e", u=2, e=2, i=4)
             src = raw[a, c0][:].rearrange("p i (m u e) -> p m i u e", u=2, e=2)
             for m0 in range(0, width // 4, 64):
-                copy = nc.vector.tensor_copy if (a, c0) in [(1, 0), (1, 256)] else nc.scalar.copy
+                if (a, c0 + 4 * m0) in []:
+                    for u in range(2):
+                        nc.gpsimd.tensor_scalar(
+                            dst[:, m0 : m0 + 64, :, u, :].rearrange("p m i e -> p m e i"),
+                            src[:, m0 : m0 + 64, :, u, :].rearrange("p m i e -> p m e i"),
+                            1.0, 0.0, ALU.mult, ALU.add,
+                        )
+                    continue
+                copy = nc.vector.tensor_copy if (a, c0) in [(1, 0), (0, 256)] else nc.scalar.copy
                 copy(dst[:, m0 : m0 + 64], src[:, m0 : m0 + 64])
 
         def quant_wb(a, c0, width):
@@ -127,7 +134,7 @@ def tile_list_minmod_neighbour_fluxes_kernel(
         h_sb = {(s, b): held("h%d_%d" % (s, b), [P, 4, 256], BF16) for s in range(2) for b in range(4)}
 
         def forward(s, jt):
-            bank = ps_f.tile([P, 512], F32, name="fbank")
+            bank = ps_b.tile([P, 512], F32, name="fbank", tag="slope")
             for a in range(2):
                 nc.tensor.matmul_mx(
                     out=bank[:],
@@ -145,7 +152,7 @@ def tile_list_minmod_neighbour_fluxes_kernel(
             )
 
         def backward(c0, width, jts):
-            bank = ps_b.tile([P, 512], F32, name="bbank")
+            bank = ps_b.tile([P, 512], F32, name="bbank", tag="slope")
             for x, jt in enumerate(jts):
                 for a in range(2):
                     nc.tensor.matmul_mx(
@@ -241,7 +248,7 @@ def tile_list_minmod_neighbour_fluxes_kernel(
             for g in range(len(jts)):
                 res = held("res%d_%d" % (jts[0], g), [P, per_bank, width], F32)
                 factor = winds[jts[0] // 4][:, per_bank * g : per_bank * (g + 1), inside : inside + width]
-                if (jts[0], g) in []:
+                if (jts[0], g) in [(0, 0), (2, 0)]:
                     sums = ring.tile([P, per_bank, width], F32, name="sums")
                     nc.scalar.copy(sums[:], faces[jts, g][:])
                     nc.gpsimd.tensor_tensor(res[:], sums[:], factor, ALU.mult)

@@ -18,6 +18,14 @@ ALU = mybir.AluOpType
 
 P = 128
 PASS = 512
+ON_POOL = [(1, 256)]
+ON_VECTOR = [(1, 0)]
+POOL_WIND = 2
+LAG = 2
+AHEAD = 2
+FWD1_AT = 3
+FWD_WIDE = 12
+GROUPS = [(0, 1), (2, 3), (4,), (5,), (6,), (7,)]
 
 
 def tile_list_minmod_neighbour_fluxes_kernel(
@@ -28,9 +36,22 @@ def tile_list_minmod_neighbour_fluxes_kernel(
         keep = ctx.enter_context(tc.tile_pool(name="keep", bufs=1))
         shared = ctx.enter_context(tc.tile_pool(name="shared", bufs=1))
         ring = ctx.enter_context(tc.tile_pool(name="ring", bufs=3))
-        ps_b = ctx.enter_context(tc.psum_pool(name="ps_b", bufs=5))
-        ps_t = ctx.enter_context(tc.psum_pool(name="ps_t", bufs=1))
-        ps_o = ctx.enter_context(tc.psum_pool(name="ps_o", bufs=2))
+        psum = ctx.enter_context(tc.psum_pool(name="psum", bufs=1))
+        turns = {"fwd": 0, "back": 0, "turn": 0, "face": 0}
+
+        def bank_for(role, shape):
+            n = turns[role]
+            turns[role] = n + 1
+            if role == "back":
+                number = n % 4
+            elif role == "fwd":
+                number = 4 + n % 4 if n < FWD_WIDE else 4 + n % 2
+            elif role == "turn":
+                number = 7 - n % 2
+            else:
+                number = 4 + (n + 2) % 4
+            return psum.tile(shape, F32, name=role, tag="bank%d" % number)
+
 
         def held(name, shape, dtype, slot=None):
             return keep.tile(shape, dtype, name=name, tag=slot or name, align_bytes=64)
@@ -41,16 +62,15 @@ def tile_list_minmod_neighbour_fluxes_kernel(
         def placed(name, shape, dtype, kib):
             return shared.tile(shape, dtype, name=name, align_bytes=64, offset=1024 * kib)
 
-        win = placed("win", [P, T], U8, 27)
+        win = placed("win", [P, T], U8, 34)
         for a in range(2):
             for e in range(2):
                 nc.sync.dma_start(
                     win[:].bitcast(I32)[2 * a + e : P : 4, :],
                     tab_scales[a].bitcast(I32)[e::2].unsqueeze(1).to_broadcast([8, 4, T // 4]),
                 )
-        tab = [placed("tab0", [P, T], I32, 0), placed("tab1", [P, T], I32, 12)]
+        tab = [placed("tab0", [P, T], I32, 12), placed("tab1", [P, T], I32, 44)]
         nc.sync.dma_start(tab[0][:], tab_words[0].rearrange("p t i -> p (t i)").bitcast(I32))
-        nc.sync.dma_start(tab[1][:], tab_words[1].rearrange("p t i -> p (t i)").bitcast(I32))
 
         raw = {}
 
@@ -70,7 +90,7 @@ def tile_list_minmod_neighbour_fluxes_kernel(
             )
 
         load_wf(0, held("wf0", [P, 2, H], U8))
-        load_wb(0, 0, 256, held("raw00", [P, 4, 256], F32))
+        nc.sync.dma_start(tab[1][:], tab_words[1].rearrange("p t i -> p (t i)").bitcast(I32))
 
         wfs = held("wfs", [P, 2, H], U8)
         nc.vector.memset(wfs[:].bitcast(I32), 0)
@@ -87,72 +107,88 @@ def tile_list_minmod_neighbour_fluxes_kernel(
         nc.vector.tensor_copy(vs[0][:].bitcast(I32), gs[:].bitcast(I32))
         for a, r in [(1, 0), (1, 1), (1, 2), (1, 3), (0, 2), (0, 3)]:
             first = 16 * (r // 2) + 2 * a + r % 2
-            queue = nc.gpsimd if (a, r) == (0, 3) else nc.sync
+            queue = nc.sync if a == 1 else nc.scalar
             queue.dma_start(vs[a][:].bitcast(I32)[r:P:32, :], gs[:].bitcast(I32)[first:P:32, :])
-        load_wb(1, 0, 256, placed("raw10", [P, 4, 256], F32, 28))
+        load_wb(0, 0, 256, placed("raw00", [P, 4, 256], F32, 31))
         ident = held("ident", [P, P], F32)
         make_identity(nc, ident[:])
 
         v = {}
 
-        def gather_words(a, half):
-            v[a, half] = held("v%d_%d" % (a, half), [P, 512], I32)
+        def gather_words(a, first, count, kib=None):
+            name = "v%d_%d" % (a, first)
+            picked = held(name, [P, 128 * count], I32) if kib is None else placed(name, [P, 128 * count], I32, kib)
             nc.vector.tensor_copy(
-                v[a, half][:].bitcast(U32), tab[a][:].bitcast(U32).indirect(offsets[:, 32 * half : 32 * (half + 1)])
+                picked[:].bitcast(U32), tab[a][:].bitcast(U32).indirect(offsets[:, 8 * first : 8 * (first + count)])
             )
+            for x in range(count):
+                v[a, first + x] = picked[:, 128 * x : 128 * (x + 1)]
 
         def v_codes(a, jt):
-            return v[a, jt // 4][:, 128 * (jt % 4) : 128 * (jt % 4 + 1)].bitcast(E4M3)
+            return v[a, jt].bitcast(E4M3)
 
         def v_scales(a, jt):
             return vs[a][:, 128 * jt : 128 * (jt + 1)]
 
         grouped, wbq, wbs = {}, {}, {}
 
+        def pool_cast(dst, src):
+            nc.gpsimd.tensor_scalar(dst, src, 1.0, 0.0, ALU.mult, ALU.add)
+
         def cast_wb(a, c0, width):
-            grouped[a, c0] = held("grp%d_%d" % (a, c0), [P, 4 * width], BF16)
+            if (a, c0) == (1, 0):
+                grouped[a, c0] = placed("grp1_0", [P, 4 * width], BF16, 60)
+            else:
+                grouped[a, c0] = held("grp%d_%d" % (a, c0), [P, 4 * width], BF16)
+            if c0 == 512:
+                dst = grouped[a, c0][:].rearrange("p (t m i) -> p m i t", t=4, i=4)
+                src = raw[a, c0][:].rearrange("p i (m t) -> p m i t", t=4)
+                copy, run = (pool_cast, 32) if (a, c0) in ON_POOL else (nc.scalar.copy, 64)
+                for m0 in range(0, 128, run):
+                    copy(dst[:, m0 : m0 + run], src[:, m0 : m0 + run])
+                return
             dst = grouped[a, c0][:].rearrange("p (u m e i) -> p m i u e", u=2, e=2, i=4)
             src = raw[a, c0][:].rearrange("p i (m u e) -> p m i u e", u=2, e=2)
-            for m0 in range(0, width // 4, 64):
-                if (a, c0 + 4 * m0) in []:
-                    for u in range(2):
-                        nc.gpsimd.tensor_scalar(
-                            dst[:, m0 : m0 + 64, :, u, :].rearrange("p m i e -> p m e i"),
-                            src[:, m0 : m0 + 64, :, u, :].rearrange("p m i e -> p m e i"),
-                            1.0, 0.0, ALU.mult, ALU.add,
-                        )
-                    continue
-                copy = nc.vector.tensor_copy if (a, c0) in [(1, 0), (0, 256)] else nc.scalar.copy
-                copy(dst[:, m0 : m0 + 64], src[:, m0 : m0 + 64])
+            if (a, c0) in ON_POOL:
+                for u in range(2):
+                    pool_cast(
+                        dst[:, :, :, u, :].rearrange("p m i e -> p m e i"),
+                        src[:, :, :, u, :].rearrange("p m i e -> p m e i"),
+                    )
+            else:
+                copy = nc.vector.tensor_copy if (a, c0) in ON_VECTOR else nc.scalar.copy
+                copy(dst, src)
 
         def quant_wb(a, c0, width):
             wbq[a, c0] = held("wbq%d_%d" % (a, c0), [P, width], I32)
             wbs[a, c0] = held("wbs%d_%d" % (a, c0), [P, width], U8)
             nc.vector.quantize_mx(out=wbq[a, c0][:].bitcast(E4M3), scales=wbs[a, c0][:], in_=grouped[a, c0][:])
 
-        f_sb = {(s, b): held("f%d_%d" % (s, b), [P, 4, 256], F32) for s in range(2) for b in range(4)}
-        h_sb = {(s, b): held("h%d_%d" % (s, b), [P, 4, 256], BF16) for s in range(2) for b in range(4)}
+        f_sb = {(s, b): held("f%d_%d" % (s, b), [P, 4, 256], F32) for s in range(1) for b in range(4)}
+        h_sb = {(s, b): held("h%d_%d" % (s, b), [P, 4, 256], BF16) for s in range(1) for b in range(4)}
 
-        def forward(s, jt):
-            bank = ps_b.tile([P, 512], F32, name="fbank", tag="slope")
+        def forward(s, jts):
+            banks = {jt: bank_for("fwd", [P, 512]) for jt in jts}
             for a in range(2):
-                nc.tensor.matmul_mx(
-                    out=bank[:],
-                    lhsT=v_codes(a, jt),
-                    lhsT_scale=v_scales(a, jt),
-                    rhs=wf[s][:, a, :].bitcast(E2M1),
-                    rhs_scale=wfs[:, a, 512 * s : 512 * (s + 1)],
-                    start=(a == 0),
-                    stop=(a == 1),
+                for jt in jts:
+                    nc.tensor.matmul_mx(
+                        out=banks[jt][:],
+                        lhsT=v_codes(a, jt),
+                        lhsT_scale=v_scales(a, jt),
+                        rhs=wf[s][:, a, :].bitcast(E2M1),
+                        rhs_scale=wfs[:, a, 512 * s : 512 * (s + 1)],
+                        start=(a == 0),
+                        stop=(a == 1),
+                    )
+            for jt in jts:
+                jj = jt % 2
+                nc.scalar.copy(
+                    f_sb[s, jt // 2][:, 2 * jj : 2 * jj + 2, :].rearrange("p u (m e) -> p u m e", e=2),
+                    banks[jt][:].rearrange("p (m u e) -> p u m e", u=2, e=2),
                 )
-            jj = jt % 2
-            nc.scalar.copy(
-                f_sb[s, jt // 2][:, 2 * jj : 2 * jj + 2, :].rearrange("p u (m e) -> p u m e", e=2),
-                bank[:].rearrange("p (m u e) -> p u m e", u=2, e=2),
-            )
 
         def backward(c0, width, jts):
-            bank = ps_b.tile([P, 512], F32, name="bbank", tag="slope")
+            bank = bank_for("back", [P, 512])
             for x, jt in enumerate(jts):
                 for a in range(2):
                     nc.tensor.matmul_mx(
@@ -172,8 +208,7 @@ def tile_list_minmod_neighbour_fluxes_kernel(
             col = (c0 % 512) // 2
             return tiles[s, b][:, first : first + 2 * len(jts), col : col + run]
 
-        def lower(unit):
-            bank = backward(*unit)
+        def lower(unit, bank):
             run = unit[1] // 2
             t1 = ring.tile([P, 512], F32, name="t1")
             nc.vector.scalar_tensor_tensor(
@@ -197,6 +232,57 @@ def tile_list_minmod_neighbour_fluxes_kernel(
                 op1=ALU.min,
             )
 
+        dealt, f_late = {}, {}
+        h_late = [held("hl%d" % b, [P, 2, 512], BF16) for b in range(4)]
+
+        def deal_wf():
+            dealt["codes"] = placed("wfd", [P, 2, 4, 128], U16, 46)
+            nc.vector.tensor_copy(dealt["codes"][:], wf[1][:].bitcast(U16).rearrange("p a (m t) -> p a t m", t=4))
+            dealt["scales"] = placed("wfp", [P, 2, 4, 128], U8, 48)
+            nc.vector.tensor_copy(dealt["scales"][:], wfs[:, :, PASS:].rearrange("p a (m t) -> p a t m", t=4))
+
+        def slope(role, jt):
+            bank = bank_for(role, [P, 4, 128])
+            for t in range(4):
+                for a in range(2):
+                    cols = slice(128 * t, 128 * (t + 1))
+                    if role == "back":
+                        codes, scales = wbq[a, 512][:, cols].bitcast(E4M3), wbs[a, 512][:, cols]
+                    else:
+                        codes, scales = dealt["codes"][:, a, t, :].bitcast(E2M1), dealt["scales"][:, a, t, :]
+                    nc.tensor.matmul_mx(
+                        out=bank[:, t, :],
+                        lhsT=codes,
+                        lhsT_scale=scales,
+                        rhs=v_codes(a, jt),
+                        rhs_scale=v_scales(a, jt),
+                        start=(a == 0),
+                        stop=(a == 1),
+                    )
+            return bank[:].rearrange("p t c -> p c t")
+
+        def forward_late(jt):
+            f_late[jt] = held("fl%d" % jt, [P, 128, 4], F32)
+            nc.scalar.copy(f_late[jt][:], slope("fwd", jt))
+
+        def lower_late(jt, back):
+            t1 = ring.tile([P, 512], F32, name="t1")
+            nc.vector.scalar_tensor_tensor(
+                out=t1[:].rearrange("p (c t) -> p c t", t=4),
+                in0=back, scalar=0.0, in1=f_late[jt][:], op0=ALU.min, op1=ALU.max
+            )
+            return back, t1
+
+        def upper_late(jt, back, t1):
+            nc.vector.scalar_tensor_tensor(
+                out=h_late[jt // 2][:, jt % 2, :].rearrange("p (c t) -> p c t", t=4),
+                in0=back,
+                scalar=0.0,
+                in1=t1[:].rearrange("p (c t) -> p c t", t=4),
+                op0=ALU.max,
+                op1=ALU.min,
+            )
+
         h_t = {}
         hq = [held("hq%d" % s, [P, S], I32) for s in range(2)]
         hs = [held("hs%d" % s, [P, S], U8) for s in range(2)]
@@ -205,7 +291,7 @@ def tile_list_minmod_neighbour_fluxes_kernel(
             return slice(128 * jts[0], 128 * (jts[-1] + 1))
 
         def turn(s, jts):
-            bank = ps_t.tile([P, 2 * len(jts), P], F32, name="tbank")
+            bank = bank_for("turn", [P, 2 * len(jts), P])
             for y, jt in reversed(list(enumerate(jts))):
                 for u in range(2):
                     words = h_sb[s, jt // 2][:, 2 * (jt % 2) + u, :].bitcast(F32)
@@ -218,114 +304,127 @@ def tile_list_minmod_neighbour_fluxes_kernel(
 
         def quant_h(s, jts):
             cols = cells(jts)
-            nc.vector.quantize_mx(out=hq[s][:, cols].bitcast(E4M3), scales=hs[s][:, cols], in_=h_t[s, jts][:])
+            if s == 0:
+                values = h_t[s, jts][:]
+            else:
+                first = jts[0] % 2
+                values = h_late[jts[0] // 2][:, first : first + len(jts), :].rearrange("p x c -> p (x c)")
+            nc.vector.quantize_mx(out=hq[s][:, cols].bitcast(E4M3), scales=hs[s][:, cols], in_=values)
 
         faces = {}
         late = {}
 
-        def face(jts):
+        def face(jts, groups):
             cols = cells(jts)
-            per_bank = 4 // len(jts)
-            for g in range(len(jts)):
-                bank = ps_o.tile([P, per_bank, 128 * len(jts)], F32, name="obank")
+            per_bank = 4 // groups
+            for g in range(groups):
+                bank = bank_for("face", [P, per_bank, 128 * len(jts)])
                 for y in range(per_bank):
                     rows = slice(128 * (per_bank * g + y), 128 * (per_bank * g + y + 1))
-                    for s in range(2):
+                    for s in (1, 0):
                         nc.tensor.matmul_mx(
                             out=bank[:, y, :],
                             lhsT=late["wx"][:, s, rows].bitcast(E4M3),
-                            lhsT_scale=late["wxs"][:, s, rows],
+                            lhsT_scale=wxs[:, s, rows],
                             rhs=hq[s][:, cols].bitcast(E4M3),
                             rhs_scale=hs[s][:, cols],
-                            start=(s == 0),
-                            stop=(s == 1),
+                            start=(s == 1),
+                            stop=(s == 0),
                         )
                 faces[jts, g] = bank
 
-        def flux(jts):
-            per_bank, width = 4 // len(jts), 128 * len(jts)
+        def flux(jts, groups):
+            per_bank, width = 4 // groups, 128 * len(jts)
             inside = 128 * (jts[0] % 4)
-            for g in range(len(jts)):
+            for g in range(groups):
                 res = held("res%d_%d" % (jts[0], g), [P, per_bank, width], F32)
                 factor = winds[jts[0] // 4][:, per_bank * g : per_bank * (g + 1), inside : inside + width]
-                if (jts[0], g) in [(0, 0), (2, 0)]:
+                if jts[0] + g < POOL_WIND:
                     sums = ring.tile([P, per_bank, width], F32, name="sums")
                     nc.scalar.copy(sums[:], faces[jts, g][:])
-                    nc.gpsimd.tensor_tensor(res[:], sums[:], factor, ALU.mult)
+                    for y in range(per_bank):
+                        nc.gpsimd.tensor_tensor(res[:, y, :], sums[:, y, :], factor[:, y, :], ALU.mult)
                 else:
                     nc.vector.tensor_tensor(res[:], faces[jts, g][:], factor, ALU.mult)
                 rows = slice(128 * per_bank * g, 128 * per_bank * (g + 1))
                 nc.sync.dma_start(out[rows, cells(jts)].rearrange("(y p) j -> p y j", p=P), res[:])
 
-        gather_words(0, 0)
-        gather_words(1, 0)
-        for a in range(2):
-            cast_wb(a, 0, 256)
-            quant_wb(a, 0, 256)
-        forward(0, 0)
-        forward(0, 1)
-        gather_words(0, 1)
-        gather_words(1, 1)
-        for a in range(2):
-            load_wb(a, 256, 256, placed("raw%d_256" % a, [P, 4, 256], F32, 4 * a))
-        for a in range(2):
-            load_wb(a, 512, 512, placed("raw%d_512" % a, [P, 4, 512], F32, 8 + 8 * a))
-        load_wf(1, placed("wf1", [P, 2, H], U8, 28))
+        gather_words(0, 0, 4)
+        gather_words(0, 4, 4)
+        load_wb(1, 0, 256, placed("raw10", [P, 4, 256], F32, 9))
+        load_wf(1, placed("wf1", [P, 2, H], U8, 17))
+        load_wb(0, 256, 256, placed("raw0_256", [P, 4, 256], F32, 13))
+        load_wb(1, 256, 256, placed("raw1_256", [P, 4, 256], F32, 19))
+        gather_words(1, 0, 2)
+        gather_words(1, 2, 2)
+        gather_words(1, 4, 4)
+        load_wb(0, 512, 512, placed("raw0_512", [P, 4, 512], F32, 37))
+        load_wb(1, 512, 512, placed("raw1_512", [P, 4, 512], F32, 51))
+        cast_wb(0, 0, 256)
+        quant_wb(0, 0, 256)
+        cast_wb(1, 0, 256)
+        quant_wb(1, 0, 256)
+        deal_wf()
+        wxs = placed("wxs", [P, 2, N], U8, 60)
+        nc.gpsimd.memset(wxs[:].bitcast(I32), 0)
+        for d in range(4):
+            nc.sync.dma_start(
+                wxs[:].bitcast(I32)[32 * d : 32 * d + 4],
+                wx_scales.bitcast(I32)[:, 4 * d : 4 * d + 4, :].rearrange("a r c -> r a c"),
+            )
+        forward(0, (0, 1, 2, 3))
 
         winds = {}
 
         def load_wind(x):
-            winds[x] = placed("wind%d" % x, [P, 4, 512], F32, 8 + 8 * x)
+            winds[x] = placed("wind%d" % x, [P, 4, 512], F32, 6 + 16 * x)
             nc.sync.dma_start(winds[x][:], wind[:, 512 * x : 512 * (x + 1)].rearrange("(m p) j -> p m j", p=P))
 
         def load_wx():
-            late["wx"] = placed("wx", [P, 2, N], I32, 0)
+            late["wx"] = placed("wx", [P, 2, N], I32, 30)
             nc.sync.dma_start(late["wx"][:], wx_words.rearrange("a p c i -> p a (c i)").bitcast(I32))
-            late["wxs"] = placed("wxs", [P, 2, N], U8, 4)
-            nc.gpsimd.memset(late["wxs"][:].bitcast(I32), 0)
-            for d in range(4):
-                nc.sync.dma_start(
-                    late["wxs"][:].bitcast(I32)[32 * d : 32 * d + 4],
-                    wx_scales.bitcast(I32)[:, 4 * d : 4 * d + 4, :].rearrange("a r c -> r a c"),
-                )
 
         pairs = [(0, 1), (2, 3), (4, 5), (6, 7)]
-        units = [(0, 256, (0, 1)), (0, 256, (2, 3)), (256, 256, (0, 1)), (256, 256, (2, 3)), (0, 256, (4, 5)), (0, 256, (6, 7)), (256, 256, (4, 5)), (256, 256, (6, 7)), (512, 512, (0,)), (512, 512, (1,)), (512, 512, (2,)), (512, 512, (3,)), (512, 512, (4,)), (512, 512, (5,)), (512, 512, (6,)), (512, 512, (7,))]
-        before = {i: [] for i in range(-4, len(units) + 5)}
-        seen = {(0, 0), (0, 1), 0}
-        last = {}
-        for i, (c0, width, jts) in enumerate(units):
-            for jt in jts:
-                last[c0 // 512, jt] = i
-                if (c0 // 512, jt) not in seen:
-                    seen.add((c0 // 512, jt))
-                    before[max(i - 2, 0)].append(lambda s=c0 // 512, jt=jt: forward(s, jt))
-            if c0 not in seen:
-                seen.add(c0)
-                for a in range(2):
-                    before[i - 2 + a].append(lambda a=a, c0=c0, width=width: cast_wb(a, c0, width))
-                    before[min(i - 2 + a + 1, i)].append(lambda a=a, c0=c0, width=width: quant_wb(a, c0, width))
-                before[i].append(load_wx if c0 == 256 else lambda: [load_wind(x) for x in range(2)])
-        turned = {}
-        for jts in pairs:
-            at = max(last[0, jts[-1]] + 2, last[1, jts[0]] - 2)
-            before[at].append(lambda jts=jts: turn(0, jts))
-            before[at + 1].append(lambda jts=jts: quant_h(0, jts))
-            for jt in jts:
-                turned[jt] = at + 1
-        for jts in [(0, 1), (2, 3), (4, 5), (6,), (7,)]:
-            done = last[1, jts[-1]] + 2
-            before[done].append(lambda jts=jts: turn(1, jts))
-            before[done + 1].append(lambda jts=jts: quant_h(1, jts))
-            at = max(done + 1, turned[jts[-1]])
-            before[at].append(lambda jts=jts: face(jts))
-            before[at + 1].append(lambda jts=jts: flux(jts))
+        units = [(c0, 256, jts) for c0 in (0, 256) for jts in pairs]
+        before = {i: [] for i in range(-4, 25)}
+        after = {i: [] for i in before}
+        load_wx()
+        for jt in range(4, 8):
+            before[jt // 2 - 3].append(lambda jt=jt: forward(0, (jt,)))
+        for a in range(2):
+            before[a - 1].append(lambda a=a: cast_wb(a, 256, 256))
+            before[3 - AHEAD + a].append(lambda a=a: quant_wb(a, 256, 256))
+            before[1 + a].append(lambda a=a: cast_wb(a, 512, 512))
+            before[1].append(lambda a=a: load_wind(a))
+            before[7 - AHEAD + a].append(lambda a=a: quant_wb(a, 512, 512))
+        for jt in range(8):
+            after[FWD1_AT + jt].append(lambda jt=jt: forward_late(jt))
+        for x, jts in enumerate(pairs):
+            before[6 + x].append(lambda jts=jts: turn(0, jts))
+            before[7 + x].append(lambda jts=jts: quant_h(0, jts))
+        for jts in GROUPS:
+            done = 8 + jts[-1] + 2
+            groups = 2 if jts == (7,) else len(jts)
+            before[done].append(lambda jts=jts: quant_h(1, jts))
+            after[done].append(lambda jts=jts, groups=groups: face(jts, groups))
+            after[done + LAG].append(lambda jts=jts, groups=groups: flux(jts, groups))
 
         pending = None
-        for i in range(-4, len(units) + 5):
+        sums_of = {}
+        for i in range(-4, 25):
             for step in before[i]:
                 step()
-            made = lower(units[i]) if 0 <= i < len(units) else None
+            nxt = i + AHEAD
+            if 0 <= nxt < 16:
+                sums_of[nxt] = backward(*units[nxt]) if nxt < 8 else slope("back", nxt - 8)
+            for step in after[i]:
+                step()
+            made = None
+            if 0 <= i < 16:
+                made = lower(units[i], sums_of[i]) if i < 8 else lower_late(i - 8, sums_of[i])
             if pending is not None:
-                upper(units[i - 1], *pending)
+                if i <= 8:
+                    upper(units[i - 1], *pending)
+                else:
+                    upper_late(i - 9, *pending)
             pending = made

@@ -69,7 +69,7 @@ def tile_list_minmod_neighbour_fluxes_kernel(
                     win[:].bitcast(I32)[2 * a + e : P : 4, :],
                     tab_scales[a].bitcast(I32)[e::2].unsqueeze(1).to_broadcast([8, 4, T // 4]),
                 )
-        tab = [placed("tab0", [P, T], I32, 12), placed("tab1", [P, T], I32, 44)]
+        tab = [placed("tab0", [P, T], I32, 12)]
         nc.sync.dma_start(tab[0][:], tab_words[0].rearrange("p t i -> p (t i)").bitcast(I32))
 
         raw = {}
@@ -89,16 +89,19 @@ def tile_list_minmod_neighbour_fluxes_kernel(
                 wf_words.bitcast(I32)[:, :, 256 * s : 256 * (s + 1)].rearrange("a p c -> p a c"),
             )
 
-        load_wf(0, held("wf0", [P, 2, H], U8))
-        nc.sync.dma_start(tab[1][:], tab_words[1].rearrange("p t i -> p (t i)").bitcast(I32))
-
+        zero = placed("zero", [P, H // 2], I32, 44)
+        nc.vector.memset(zero[:], 0)
         wfs = held("wfs", [P, 2, H], U8)
-        nc.vector.memset(wfs[:].bitcast(I32), 0)
+        nc.vector.tensor_copy(wfs[:].bitcast(I32).rearrange("p a c -> p (a c)"), zero[:])
         for d in range(4):
-            nc.gpsimd.dma_start(
+            nc.sync.dma_start(
                 wfs[:].bitcast(I32)[32 * d : 32 * d + 4],
                 wf_scales.bitcast(I32)[:, 4 * d : 4 * d + 4, :].rearrange("a r c -> r a c"),
             )
+        load_wf(0, placed("wf0", [P, 2, H], U8, 43))
+        tab.append(placed("tab1", [P, T], I32, 45))
+        nc.sync.dma_start(tab[1][:], tab_words[1].rearrange("p t i -> p (t i)").bitcast(I32))
+
         vs = [held("vs%d" % a, [P, S], U8) for a in range(2)]
         nc.vector.memset(vs[1][:].bitcast(I32), 0)
 
@@ -107,8 +110,7 @@ def tile_list_minmod_neighbour_fluxes_kernel(
         nc.vector.tensor_copy(vs[0][:].bitcast(I32), gs[:].bitcast(I32))
         for a, r in [(1, 0), (1, 1), (1, 2), (1, 3), (0, 2), (0, 3)]:
             first = 16 * (r // 2) + 2 * a + r % 2
-            queue = nc.sync if a == 1 else nc.scalar
-            queue.dma_start(vs[a][:].bitcast(I32)[r:P:32, :], gs[:].bitcast(I32)[first:P:32, :])
+            nc.sync.dma_start(vs[a][:].bitcast(I32)[r:P:32, :], gs[:].bitcast(I32)[first:P:32, :])
         load_wb(0, 0, 256, placed("raw00", [P, 4, 256], F32, 31))
         ident = held("ident", [P, P], F32)
         make_identity(nc, ident[:])
@@ -164,7 +166,7 @@ def tile_list_minmod_neighbour_fluxes_kernel(
             wbs[a, c0] = held("wbs%d_%d" % (a, c0), [P, width], U8)
             nc.vector.quantize_mx(out=wbq[a, c0][:].bitcast(E4M3), scales=wbs[a, c0][:], in_=grouped[a, c0][:])
 
-        f_sb = {(s, b): held("f%d_%d" % (s, b), [P, 4, 256], F32) for s in range(1) for b in range(4)}
+        f_sb = {(0, b): held("f0_%d" % b, [P, 4, 256], F32) for b in range(2, 4)}
         h_sb = {(s, b): held("h%d_%d" % (s, b), [P, 4, 256], BF16) for s in range(1) for b in range(4)}
 
         def forward(s, jts):
@@ -210,24 +212,23 @@ def tile_list_minmod_neighbour_fluxes_kernel(
 
         def lower(unit, bank):
             run = unit[1] // 2
-            t1 = ring.tile([P, 512], F32, name="t1")
             nc.vector.scalar_tensor_tensor(
-                out=t1[:].rearrange("p (x c) -> p x c", c=run),
+                out=place(f_sb, *unit),
                 in0=bank[:].rearrange("p (x c) -> p x c", c=run),
                 scalar=0.0,
                 in1=place(f_sb, *unit),
                 op0=ALU.min,
                 op1=ALU.max,
             )
-            return bank, t1
+            return (bank,)
 
-        def upper(unit, bank, t1):
+        def upper(unit, bank):
             run = unit[1] // 2
             nc.vector.scalar_tensor_tensor(
                 out=place(h_sb, *unit),
                 in0=bank[:].rearrange("p (x c) -> p x c", c=run),
                 scalar=0.0,
-                in1=t1[:].rearrange("p (x c) -> p x c", c=run),
+                in1=place(f_sb, *unit),
                 op0=ALU.max,
                 op1=ALU.min,
             )
@@ -236,9 +237,9 @@ def tile_list_minmod_neighbour_fluxes_kernel(
         h_late = [held("hl%d" % b, [P, 2, 512], BF16) for b in range(4)]
 
         def deal_wf():
-            dealt["codes"] = placed("wfd", [P, 2, 4, 128], U16, 46)
+            dealt["codes"] = placed("wfd", [P, 2, 4, 128], U16, 47)
             nc.vector.tensor_copy(dealt["codes"][:], wf[1][:].bitcast(U16).rearrange("p a (m t) -> p a t m", t=4))
-            dealt["scales"] = placed("wfp", [P, 2, 4, 128], U8, 48)
+            dealt["scales"] = placed("wfp", [P, 2, 4, 128], U8, 49)
             nc.vector.tensor_copy(dealt["scales"][:], wfs[:, :, PASS:].rearrange("p a (m t) -> p a t m", t=4))
 
         def slope(role, jt):
@@ -266,19 +267,17 @@ def tile_list_minmod_neighbour_fluxes_kernel(
             nc.scalar.copy(f_late[jt][:], slope("fwd", jt))
 
         def lower_late(jt, back):
-            t1 = ring.tile([P, 512], F32, name="t1")
             nc.vector.scalar_tensor_tensor(
-                out=t1[:].rearrange("p (c t) -> p c t", t=4),
-                in0=back, scalar=0.0, in1=f_late[jt][:], op0=ALU.min, op1=ALU.max
+                out=f_late[jt][:], in0=back, scalar=0.0, in1=f_late[jt][:], op0=ALU.min, op1=ALU.max
             )
-            return back, t1
+            return (back,)
 
-        def upper_late(jt, back, t1):
+        def upper_late(jt, back):
             nc.vector.scalar_tensor_tensor(
                 out=h_late[jt // 2][:, jt % 2, :].rearrange("p (c t) -> p c t", t=4),
                 in0=back,
                 scalar=0.0,
-                in1=t1[:].rearrange("p (c t) -> p c t", t=4),
+                in1=f_late[jt][:],
                 op0=ALU.max,
                 op1=ALU.min,
             )
@@ -358,11 +357,11 @@ def tile_list_minmod_neighbour_fluxes_kernel(
         gather_words(1, 0, 2)
         gather_words(1, 2, 2)
         gather_words(1, 4, 4)
-        load_wb(0, 512, 512, placed("raw0_512", [P, 4, 512], F32, 37))
-        load_wb(1, 512, 512, placed("raw1_512", [P, 4, 512], F32, 51))
+        load_wb(0, 512, 512, placed("raw0_512", [P, 4, 512], F32, 52))
         cast_wb(0, 0, 256)
         quant_wb(0, 0, 256)
         cast_wb(1, 0, 256)
+        load_wb(1, 512, 512, placed("raw1_512", [P, 4, 512], F32, 2))
         quant_wb(1, 0, 256)
         deal_wf()
         wxs = placed("wxs", [P, 2, N], U8, 60)
@@ -372,16 +371,18 @@ def tile_list_minmod_neighbour_fluxes_kernel(
                 wxs[:].bitcast(I32)[32 * d : 32 * d + 4],
                 wx_scales.bitcast(I32)[:, 4 * d : 4 * d + 4, :].rearrange("a r c -> r a c"),
             )
+        for b in range(2):
+            f_sb[0, b] = placed("f0_%d" % b, [P, 4, 256], F32, 28 + 6 * b)
         forward(0, (0, 1, 2, 3))
 
         winds = {}
 
         def load_wind(x):
-            winds[x] = placed("wind%d" % x, [P, 4, 512], F32, 6 + 16 * x)
+            winds[x] = placed("wind%d" % x, [P, 4, 512], F32, 19 - 13 * x)
             nc.sync.dma_start(winds[x][:], wind[:, 512 * x : 512 * (x + 1)].rearrange("(m p) j -> p m j", p=P))
 
         def load_wx():
-            late["wx"] = placed("wx", [P, 2, N], I32, 30)
+            late["wx"] = placed("wx", [P, 2, N], I32, 61)
             nc.sync.dma_start(late["wx"][:], wx_words.rearrange("a p c i -> p a (c i)").bitcast(I32))
 
         pairs = [(0, 1), (2, 3), (4, 5), (6, 7)]
@@ -395,7 +396,7 @@ def tile_list_minmod_neighbour_fluxes_kernel(
             before[a - 1].append(lambda a=a: cast_wb(a, 256, 256))
             before[3 - AHEAD + a].append(lambda a=a: quant_wb(a, 256, 256))
             before[1 + a].append(lambda a=a: cast_wb(a, 512, 512))
-            before[1].append(lambda a=a: load_wind(a))
+            before[2].append(lambda a=a: load_wind(a))
             before[7 - AHEAD + a].append(lambda a=a: quant_wb(a, 512, 512))
         for jt in range(8):
             after[FWD1_AT + jt].append(lambda jt=jt: forward_late(jt))

@@ -20,12 +20,21 @@ P = 128
 PASS = 512
 ON_POOL = [(1, 256)]
 ON_VECTOR = [(1, 0)]
-POOL_WIND = 2
-LAG = 2
+POOL_WIND = 4
+LAG = 1
+POOL_COLS = (0, 0)
+HOLD = 1
+JOINT = (256, 512)
+FIRST_GROUPS = [(0, 1), (2, 3), (4, 5), (6, 7)]
+HELD = ()
+PIECE = 256
+EARLY = 4
+FWD_LEAD = 4
+BANKS = 1
 AHEAD = 2
 FWD1_AT = 3
 FWD_WIDE = 12
-GROUPS = [(0, 1), (2, 3), (4,), (5,), (6,), (7,)]
+GROUPS = [(0, 1), (2, 3), (4, 5), (6,), (7,)]
 
 
 def tile_list_minmod_neighbour_fluxes_kernel(
@@ -44,12 +53,15 @@ def tile_list_minmod_neighbour_fluxes_kernel(
             turns[role] = n + 1
             if role == "back":
                 number = n % 4
+            elif BANKS == 1:
+                turns["other"] = turns.get("other", -1) + 1
+                number = 4 + turns["other"] % 4
             elif role == "fwd":
-                number = 4 + n % 4 if n < FWD_WIDE else 4 + n % 2
+                number = 4 + n % 4 if n < FWD_WIDE else 4
             elif role == "turn":
-                number = 7 - n % 2
+                number = 5
             else:
-                number = 4 + (n + 2) % 4
+                number = 6 + n % 2
             return psum.tile(shape, F32, name=role, tag="bank%d" % number)
 
 
@@ -139,17 +151,24 @@ def tile_list_minmod_neighbour_fluxes_kernel(
 
         def cast_wb(a, c0, width):
             if (a, c0) == (1, 0):
-                grouped[a, c0] = placed("grp1_0", [P, 4 * width], BF16, 60)
+                grouped[a, c0] = placed("grp1_0", [P, 4 * width], BF16, 60)[:]
+            elif c0 not in JOINT:
+                grouped[a, c0] = held("grp%d_%d" % (a, c0), [P, 4 * width], BF16)[:]
             else:
-                grouped[a, c0] = held("grp%d_%d" % (a, c0), [P, 4 * width], BF16)
+                if a == 0:
+                    grouped[c0] = placed("grp_%d" % c0, [P, 8 * width], BF16, 90)
+                grouped[a, c0] = grouped[c0][:, 4 * width * a : 4 * width * (a + 1)]
             if c0 == 512:
-                dst = grouped[a, c0][:].rearrange("p (t m i) -> p m i t", t=4, i=4)
+                dst = grouped[a, c0].rearrange("p (t m i) -> p m i t", t=4, i=4)
                 src = raw[a, c0][:].rearrange("p i (m t) -> p m i t", t=4)
-                copy, run = (pool_cast, 32) if (a, c0) in ON_POOL else (nc.scalar.copy, 64)
-                for m0 in range(0, 128, run):
-                    copy(dst[:, m0 : m0 + run], src[:, m0 : m0 + run])
+                split = 128 - POOL_COLS[a]
+                for m0 in range(0, split, 64):
+                    m1 = min(m0 + 64, split)
+                    nc.scalar.copy(dst[:, m0:m1], src[:, m0:m1])
+                for t in range(4 if split < 128 else 0):
+                    pool_cast(dst[:, split:, :, t], src[:, split:, :, t])
                 return
-            dst = grouped[a, c0][:].rearrange("p (u m e i) -> p m i u e", u=2, e=2, i=4)
+            dst = grouped[a, c0].rearrange("p (u m e i) -> p m i u e", u=2, e=2, i=4)
             src = raw[a, c0][:].rearrange("p i (m u e) -> p m i u e", u=2, e=2)
             if (a, c0) in ON_POOL:
                 for u in range(2):
@@ -162,9 +181,19 @@ def tile_list_minmod_neighbour_fluxes_kernel(
                 copy(dst, src)
 
         def quant_wb(a, c0, width):
-            wbq[a, c0] = held("wbq%d_%d" % (a, c0), [P, width], I32)
-            wbs[a, c0] = held("wbs%d_%d" % (a, c0), [P, width], U8)
-            nc.vector.quantize_mx(out=wbq[a, c0][:].bitcast(E4M3), scales=wbs[a, c0][:], in_=grouped[a, c0][:])
+            if c0 in JOINT:
+                if a == 0:
+                    return
+                codes = held("wbq_%d" % c0, [P, 2 * width], I32)
+                scales = held("wbs_%d" % c0, [P, 2 * width], U8)
+                nc.vector.quantize_mx(out=codes[:].bitcast(E4M3), scales=scales[:], in_=grouped[c0][:])
+                for x in range(2):
+                    wbq[x, c0] = codes[:, width * x : width * (x + 1)]
+                    wbs[x, c0] = scales[:, width * x : width * (x + 1)]
+                return
+            wbq[a, c0] = held("wbq%d_%d" % (a, c0), [P, width], I32)[:]
+            wbs[a, c0] = held("wbs%d_%d" % (a, c0), [P, width], U8)[:]
+            nc.vector.quantize_mx(out=wbq[a, c0].bitcast(E4M3), scales=wbs[a, c0], in_=grouped[a, c0])
 
         f_sb = {(0, b): held("f0_%d" % b, [P, 4, 256], F32) for b in range(2, 4)}
         h_sb = {(s, b): held("h%d_%d" % (s, b), [P, 4, 256], BF16) for s in range(1) for b in range(4)}
@@ -191,16 +220,16 @@ def tile_list_minmod_neighbour_fluxes_kernel(
 
         def backward(c0, width, jts):
             bank = bank_for("back", [P, 512])
-            for x, jt in enumerate(jts):
-                for a in range(2):
+            for a in range(2):
+                for x, jt in enumerate(jts):
                     nc.tensor.matmul_mx(
                         out=bank[:, width * x : width * (x + 1)],
                         lhsT=v_codes(a, jt),
                         lhsT_scale=v_scales(a, jt),
-                        rhs=wbq[a, c0][:].bitcast(E4M3),
-                        rhs_scale=wbs[a, c0][:],
-                        start=(a == 0),
-                        stop=(a == 1),
+                        rhs=wbq[a, c0].bitcast(E4M3),
+                        rhs_scale=wbs[a, c0],
+                        start=(a == 0 and x == 0),
+                        stop=(a == 1 and x == len(jts) - 1),
                     )
             return bank
 
@@ -234,12 +263,12 @@ def tile_list_minmod_neighbour_fluxes_kernel(
             )
 
         dealt, f_late = {}, {}
-        h_late = [held("hl%d" % b, [P, 2, 512], BF16) for b in range(4)]
+        h_late = [placed("hl%d" % b, [P, 2, 512], BF16, 71 + 4 * b) for b in range(4)]
 
         def deal_wf():
-            dealt["codes"] = placed("wfd", [P, 2, 4, 128], U16, 47)
+            dealt["codes"] = placed("wfd", [P, 2, 4, 128], U16, 61)
             nc.vector.tensor_copy(dealt["codes"][:], wf[1][:].bitcast(U16).rearrange("p a (m t) -> p a t m", t=4))
-            dealt["scales"] = placed("wfp", [P, 2, 4, 128], U8, 49)
+            dealt["scales"] = placed("wfp", [P, 2, 4, 128], U8, 50)
             nc.vector.tensor_copy(dealt["scales"][:], wfs[:, :, PASS:].rearrange("p a (m t) -> p a t m", t=4))
 
         def slope(role, jt):
@@ -282,7 +311,7 @@ def tile_list_minmod_neighbour_fluxes_kernel(
                 op1=ALU.min,
             )
 
-        h_t = {}
+        h_t = held("h_t", [P, 4 * S], BF16)
         hq = [held("hq%d" % s, [P, S], I32) for s in range(2)]
         hs = [held("hs%d" % s, [P, S], U8) for s in range(2)]
 
@@ -295,16 +324,15 @@ def tile_list_minmod_neighbour_fluxes_kernel(
                 for u in range(2):
                     words = h_sb[s, jt // 2][:, 2 * (jt % 2) + u, :].bitcast(F32)
                     nc.tensor.transpose(bank[:, 2 * y + u, :], words, ident[:])
-            h_t[s, jts] = held("ht%d_%d" % (s, jts[0]), [P, 512 * len(jts)], BF16)
             nc.scalar.copy(
-                h_t[s, jts][:].bitcast(F32).rearrange("p (y j u) -> p y j u", y=len(jts), u=2),
+                h_t[:, 512 * jts[0] : 512 * (jts[-1] + 1)].bitcast(F32).rearrange("p (y j u) -> p y j u", y=len(jts), u=2),
                 bank[:].rearrange("p (y u) j -> p y j u", u=2),
             )
 
         def quant_h(s, jts):
             cols = cells(jts)
             if s == 0:
-                values = h_t[s, jts][:]
+                values = h_t[:, 512 * jts[0] : 512 * (jts[-1] + 1)]
             else:
                 first = jts[0] % 2
                 values = h_late[jts[0] // 2][:, first : first + len(jts), :].rearrange("p x c -> p (x c)")
@@ -318,17 +346,17 @@ def tile_list_minmod_neighbour_fluxes_kernel(
             per_bank = 4 // groups
             for g in range(groups):
                 bank = bank_for("face", [P, per_bank, 128 * len(jts)])
-                for y in range(per_bank):
-                    rows = slice(128 * (per_bank * g + y), 128 * (per_bank * g + y + 1))
-                    for s in (1, 0):
+                for s in range(2):
+                    for y in range(per_bank):
+                        rows = slice(128 * (per_bank * g + y), 128 * (per_bank * g + y + 1))
                         nc.tensor.matmul_mx(
                             out=bank[:, y, :],
                             lhsT=late["wx"][:, s, rows].bitcast(E4M3),
                             lhsT_scale=wxs[:, s, rows],
                             rhs=hq[s][:, cols].bitcast(E4M3),
                             rhs_scale=hs[s][:, cols],
-                            start=(s == 1),
-                            stop=(s == 0),
+                            start=(s == 0 and y == 0),
+                            stop=(s == 1 and y == per_bank - 1),
                         )
                 faces[jts, g] = bank
 
@@ -336,27 +364,34 @@ def tile_list_minmod_neighbour_fluxes_kernel(
             per_bank, width = 4 // groups, 128 * len(jts)
             inside = 128 * (jts[0] % 4)
             for g in range(groups):
-                res = held("res%d_%d" % (jts[0], g), [P, per_bank, width], F32)
+                name = "res%d_%d" % (jts[0], g)
+                if jts[0] + g in HELD:
+                    res = placed(name, [P, per_bank, width], F32, 74 + 2 * (jts[0] + g))
+                else:
+                    res = held(name, [P, per_bank, width], F32)
                 factor = winds[jts[0] // 4][:, per_bank * g : per_bank * (g + 1), inside : inside + width]
                 if jts[0] + g < POOL_WIND:
                     sums = ring.tile([P, per_bank, width], F32, name="sums")
                     nc.scalar.copy(sums[:], faces[jts, g][:])
-                    for y in range(per_bank):
-                        nc.gpsimd.tensor_tensor(res[:, y, :], sums[:, y, :], factor[:, y, :], ALU.mult)
+                    for c0 in range(0, 512, PIECE):
+                        y0, y1, x0 = c0 // width, (c0 + PIECE - 1) // width + 1, c0 % width
+                        x1 = x0 + min(PIECE, width)
+                        nc.gpsimd.tensor_tensor(
+                            res[:, y0:y1, x0:x1], sums[:, y0:y1, x0:x1], factor[:, y0:y1, x0:x1], ALU.mult
+                        )
                 else:
                     nc.vector.tensor_tensor(res[:], faces[jts, g][:], factor, ALU.mult)
                 rows = slice(128 * per_bank * g, 128 * per_bank * (g + 1))
-                nc.sync.dma_start(out[rows, cells(jts)].rearrange("(y p) j -> p y j", p=P), res[:])
+                queue = nc.sync if jts[0] + g < POOL_WIND else nc.scalar
+                queue.dma_start(out[rows, cells(jts)].rearrange("(y p) j -> p y j", p=P), res[:])
 
-        gather_words(0, 0, 4)
-        gather_words(0, 4, 4)
+        gather_words(0, 0, 8)
         load_wb(1, 0, 256, placed("raw10", [P, 4, 256], F32, 9))
         load_wf(1, placed("wf1", [P, 2, H], U8, 17))
         load_wb(0, 256, 256, placed("raw0_256", [P, 4, 256], F32, 13))
         load_wb(1, 256, 256, placed("raw1_256", [P, 4, 256], F32, 19))
         gather_words(1, 0, 2)
-        gather_words(1, 2, 2)
-        gather_words(1, 4, 4)
+        gather_words(1, 2, 6)
         load_wb(0, 512, 512, placed("raw0_512", [P, 4, 512], F32, 52))
         cast_wb(0, 0, 256)
         quant_wb(0, 0, 256)
@@ -373,42 +408,56 @@ def tile_list_minmod_neighbour_fluxes_kernel(
             )
         for b in range(2):
             f_sb[0, b] = placed("f0_%d" % b, [P, 4, 256], F32, 28 + 6 * b)
-        forward(0, (0, 1, 2, 3))
+        forward(0, (0, 1))
+        forward(0, (2, 3))
 
         winds = {}
 
         def load_wind(x):
-            winds[x] = placed("wind%d" % x, [P, 4, 512], F32, 19 - 13 * x)
+            winds[x] = placed("wind%d" % x, [P, 4, 512], F32, 19 - 17 * x)
             nc.sync.dma_start(winds[x][:], wind[:, 512 * x : 512 * (x + 1)].rearrange("(m p) j -> p m j", p=P))
 
         def load_wx():
-            late["wx"] = placed("wx", [P, 2, N], I32, 61)
+            late["wx"] = placed("wx", [P, 2, N], I32, 13)
             nc.sync.dma_start(late["wx"][:], wx_words.rearrange("a p c i -> p a (c i)").bitcast(I32))
 
         pairs = [(0, 1), (2, 3), (4, 5), (6, 7)]
-        units = [(c0, 256, jts) for c0 in (0, 256) for jts in pairs]
+        units = [(0, 256, jts) for jts in pairs] + [(256, 256, jts) for jts in pairs[:EARLY]]
+        for x, jts in enumerate(pairs):
+            units.extend(jts)
+            if x + EARLY < 4:
+                units.append((256, 256, pairs[x + EARLY]))
         before = {i: [] for i in range(-4, 25)}
         after = {i: [] for i in before}
-        load_wx()
         for jt in range(4, 8):
             before[jt // 2 - 3].append(lambda jt=jt: forward(0, (jt,)))
         for a in range(2):
             before[a - 1].append(lambda a=a: cast_wb(a, 256, 256))
             before[3 - AHEAD + a].append(lambda a=a: quant_wb(a, 256, 256))
             before[1 + a].append(lambda a=a: cast_wb(a, 512, 512))
-            before[2].append(lambda a=a: load_wind(a))
-            before[7 - AHEAD + a].append(lambda a=a: quant_wb(a, 512, 512))
+            before[3 + EARLY - AHEAD + a].append(lambda a=a: quant_wb(a, 512, 512))
         for jt in range(8):
-            after[FWD1_AT + jt].append(lambda jt=jt: forward_late(jt))
-        for x, jts in enumerate(pairs):
-            before[6 + x].append(lambda jts=jts: turn(0, jts))
-            before[7 + x].append(lambda jts=jts: quant_h(0, jts))
+            after[min(FWD1_AT + jt, units.index(jt) - 2) if jt < 4 else units.index(jt) - FWD_LEAD].append(lambda jt=jt: forward_late(jt))
+        before[1].append(load_wx)
+        before[1].append(lambda: load_wind(0))
+        before[3].append(lambda: load_wind(1))
+        turned = {}
+        for jts in pairs:
+            at = units.index((256, 256, jts)) + 2
+            before[at].append(lambda jts=jts: turn(0, jts))
+        for jts in FIRST_GROUPS:
+            at = units.index((256, 256, jts[-2:])) + 3
+            before[at].append(lambda jts=jts: quant_h(0, jts))
+            for jt in jts:
+                turned[jt] = at
         for jts in GROUPS:
-            done = 8 + jts[-1] + 2
+            done = max(units.index(jts[-1]) + 2, turned[jts[-1]])
             groups = 2 if jts == (7,) else len(jts)
+            later = units.index(min(2 * (jts[0] // 2) + 3, 7)) + 2
+            lag = max(later - done, 0) if jts[0] + 1 in HELD and jts[0] < 6 else LAG
             before[done].append(lambda jts=jts: quant_h(1, jts))
             after[done].append(lambda jts=jts, groups=groups: face(jts, groups))
-            after[done + LAG].append(lambda jts=jts, groups=groups: flux(jts, groups))
+            after[done + lag].append(lambda jts=jts, groups=groups: flux(jts, groups))
 
         pending = None
         sums_of = {}
@@ -417,15 +466,12 @@ def tile_list_minmod_neighbour_fluxes_kernel(
                 step()
             nxt = i + AHEAD
             if 0 <= nxt < 16:
-                sums_of[nxt] = backward(*units[nxt]) if nxt < 8 else slope("back", nxt - 8)
+                sums_of[nxt] = slope("back", units[nxt]) if isinstance(units[nxt], int) else backward(*units[nxt])
             for step in after[i]:
                 step()
             made = None
             if 0 <= i < 16:
-                made = lower(units[i], sums_of[i]) if i < 8 else lower_late(i - 8, sums_of[i])
+                made = (lower_late if isinstance(units[i], int) else lower)(units[i], sums_of[i])
             if pending is not None:
-                if i <= 8:
-                    upper(units[i - 1], *pending)
-                else:
-                    upper_late(i - 9, *pending)
+                (upper_late if isinstance(units[i - 1], int) else upper)(units[i - 1], *pending)
             pending = made

@@ -21,13 +21,13 @@ PASS = 512
 ON_POOL = [(1, 256)]
 ON_VECTOR = [(1, 0)]
 POOL_WIND = 4
-LAG = 1
+LAG = 2
 POOL_COLS = (0, 0)
 HOLD = 1
 JOINT = (256, 512)
-FIRST_GROUPS = [(0, 1), (2, 3), (4, 5), (6, 7)]
-HELD = ()
-PIECE = 256
+FIRST_GROUPS = [(0, 1, 2, 3), (4, 5, 6, 7)]
+HELD = (0, 2)
+PIECE = 512
 EARLY = 4
 FWD_LEAD = 4
 BANKS = 1
@@ -74,7 +74,7 @@ def tile_list_minmod_neighbour_fluxes_kernel(
         def placed(name, shape, dtype, kib):
             return shared.tile(shape, dtype, name=name, align_bytes=64, offset=1024 * kib)
 
-        win = placed("win", [P, T], U8, 34)
+        win = placed("win", [P, T], U8, 37)
         for a in range(2):
             for e in range(2):
                 nc.sync.dma_start(
@@ -101,7 +101,7 @@ def tile_list_minmod_neighbour_fluxes_kernel(
                 wf_words.bitcast(I32)[:, :, 256 * s : 256 * (s + 1)].rearrange("a p c -> p a c"),
             )
 
-        zero = placed("zero", [P, H // 2], I32, 44)
+        zero = placed("zero", [P, H // 2], I32, 51)
         nc.vector.memset(zero[:], 0)
         wfs = held("wfs", [P, 2, H], U8)
         nc.vector.tensor_copy(wfs[:].bitcast(I32).rearrange("p a c -> p (a c)"), zero[:])
@@ -110,8 +110,8 @@ def tile_list_minmod_neighbour_fluxes_kernel(
                 wfs[:].bitcast(I32)[32 * d : 32 * d + 4],
                 wf_scales.bitcast(I32)[:, 4 * d : 4 * d + 4, :].rearrange("a r c -> r a c"),
             )
-        load_wf(0, placed("wf0", [P, 2, H], U8, 43))
-        tab.append(placed("tab1", [P, T], I32, 45))
+        load_wf(0, placed("wf0", [P, 2, H], U8, 50))
+        tab.append(placed("tab1", [P, T], I32, 52))
         nc.sync.dma_start(tab[1][:], tab_words[1].rearrange("p t i -> p (t i)").bitcast(I32))
 
         vs = [held("vs%d" % a, [P, S], U8) for a in range(2)]
@@ -123,7 +123,8 @@ def tile_list_minmod_neighbour_fluxes_kernel(
         for a, r in [(1, 0), (1, 1), (1, 2), (1, 3), (0, 2), (0, 3)]:
             first = 16 * (r // 2) + 2 * a + r % 2
             nc.sync.dma_start(vs[a][:].bitcast(I32)[r:P:32, :], gs[:].bitcast(I32)[first:P:32, :])
-        load_wb(0, 0, 256, placed("raw00", [P, 4, 256], F32, 31))
+        load_wb(0, 0, 256, placed("raw00", [P, 4, 256], F32, 34))
+        load_wb(1, 0, 256, placed("raw10", [P, 4, 256], F32, 38))
         ident = held("ident", [P, P], F32)
         make_identity(nc, ident[:])
 
@@ -151,7 +152,7 @@ def tile_list_minmod_neighbour_fluxes_kernel(
 
         def cast_wb(a, c0, width):
             if (a, c0) == (1, 0):
-                grouped[a, c0] = placed("grp1_0", [P, 4 * width], BF16, 60)[:]
+                grouped[a, c0] = placed("grp1_0", [P, 4 * width], BF16, 67)[:]
             elif c0 not in JOINT:
                 grouped[a, c0] = held("grp%d_%d" % (a, c0), [P, 4 * width], BF16)[:]
             else:
@@ -266,9 +267,9 @@ def tile_list_minmod_neighbour_fluxes_kernel(
         h_late = [placed("hl%d" % b, [P, 2, 512], BF16, 71 + 4 * b) for b in range(4)]
 
         def deal_wf():
-            dealt["codes"] = placed("wfd", [P, 2, 4, 128], U16, 61)
+            dealt["codes"] = placed("wfd", [P, 2, 4, 128], U16, 68)
             nc.vector.tensor_copy(dealt["codes"][:], wf[1][:].bitcast(U16).rearrange("p a (m t) -> p a t m", t=4))
-            dealt["scales"] = placed("wfp", [P, 2, 4, 128], U8, 50)
+            dealt["scales"] = placed("wfp", [P, 2, 4, 128], U8, 57)
             nc.vector.tensor_copy(dealt["scales"][:], wfs[:, :, PASS:].rearrange("p a (m t) -> p a t m", t=4))
 
         def slope(role, jt):
@@ -346,7 +347,7 @@ def tile_list_minmod_neighbour_fluxes_kernel(
             per_bank = 4 // groups
             for g in range(groups):
                 bank = bank_for("face", [P, per_bank, 128 * len(jts)])
-                for s in range(2):
+                for s in (0, 1) if jts == (7,) else (1, 0):
                     for y in range(per_bank):
                         rows = slice(128 * (per_bank * g + y), 128 * (per_bank * g + y + 1))
                         nc.tensor.matmul_mx(
@@ -355,22 +356,22 @@ def tile_list_minmod_neighbour_fluxes_kernel(
                             lhsT_scale=wxs[:, s, rows],
                             rhs=hq[s][:, cols].bitcast(E4M3),
                             rhs_scale=hs[s][:, cols],
-                            start=(s == 0 and y == 0),
-                            stop=(s == 1 and y == per_bank - 1),
+                            start=(s == int(jts != (7,)) and y == 0),
+                            stop=(s == int(jts == (7,)) and y == per_bank - 1),
                         )
                 faces[jts, g] = bank
 
-        def flux(jts, groups):
+        def flux(jts, groups, which):
             per_bank, width = 4 // groups, 128 * len(jts)
             inside = 128 * (jts[0] % 4)
-            for g in range(groups):
+            for g in which:
                 name = "res%d_%d" % (jts[0], g)
                 if jts[0] + g in HELD:
-                    res = placed(name, [P, per_bank, width], F32, 74 + 2 * (jts[0] + g))
+                    res = placed(name, [P, per_bank, width], F32, 74 + 2 * jts[0])
                 else:
                     res = held(name, [P, per_bank, width], F32)
                 factor = winds[jts[0] // 4][:, per_bank * g : per_bank * (g + 1), inside : inside + width]
-                if jts[0] + g < POOL_WIND:
+                if jts[0] + g in HELD:
                     sums = ring.tile([P, per_bank, width], F32, name="sums")
                     nc.scalar.copy(sums[:], faces[jts, g][:])
                     for c0 in range(0, 512, PIECE):
@@ -382,39 +383,38 @@ def tile_list_minmod_neighbour_fluxes_kernel(
                 else:
                     nc.vector.tensor_tensor(res[:], faces[jts, g][:], factor, ALU.mult)
                 rows = slice(128 * per_bank * g, 128 * per_bank * (g + 1))
-                queue = nc.sync if jts[0] + g < POOL_WIND else nc.scalar
-                queue.dma_start(out[rows, cells(jts)].rearrange("(y p) j -> p y j", p=P), res[:])
+                nc.sync.dma_start(out[rows, cells(jts)].rearrange("(y p) j -> p y j", p=P), res[:])
 
         gather_words(0, 0, 8)
-        load_wb(1, 0, 256, placed("raw10", [P, 4, 256], F32, 9))
         load_wf(1, placed("wf1", [P, 2, H], U8, 17))
         load_wb(0, 256, 256, placed("raw0_256", [P, 4, 256], F32, 13))
         load_wb(1, 256, 256, placed("raw1_256", [P, 4, 256], F32, 19))
         gather_words(1, 0, 2)
         gather_words(1, 2, 6)
-        load_wb(0, 512, 512, placed("raw0_512", [P, 4, 512], F32, 52))
+        load_wb(0, 512, 512, placed("raw0_512", [P, 4, 512], F32, 59))
         cast_wb(0, 0, 256)
         quant_wb(0, 0, 256)
         cast_wb(1, 0, 256)
-        load_wb(1, 512, 512, placed("raw1_512", [P, 4, 512], F32, 2))
+        load_wb(1, 512, 512, placed("raw1_512", [P, 4, 512], F32, 41))
         quant_wb(1, 0, 256)
         deal_wf()
-        wxs = placed("wxs", [P, 2, N], U8, 60)
+        wxs = placed("wxs", [P, 2, N], U8, 67)
         nc.gpsimd.memset(wxs[:].bitcast(I32), 0)
         for d in range(4):
             nc.sync.dma_start(
                 wxs[:].bitcast(I32)[32 * d : 32 * d + 4],
                 wx_scales.bitcast(I32)[:, 4 * d : 4 * d + 4, :].rearrange("a r c -> r a c"),
             )
+        first_four = placed("f0_first", [P, 8, 256], F32, 27)
         for b in range(2):
-            f_sb[0, b] = placed("f0_%d" % b, [P, 4, 256], F32, 28 + 6 * b)
+            f_sb[0, b] = first_four[:, 4 * b : 4 * (b + 1), :]
         forward(0, (0, 1))
         forward(0, (2, 3))
 
         winds = {}
 
         def load_wind(x):
-            winds[x] = placed("wind%d" % x, [P, 4, 512], F32, 19 - 17 * x)
+            winds[x] = placed("wind%d" % x, [P, 4, 512], F32, 19 + 22 * x)
             nc.sync.dma_start(winds[x][:], wind[:, 512 * x : 512 * (x + 1)].rearrange("(m p) j -> p m j", p=P))
 
         def load_wx():
@@ -454,10 +454,11 @@ def tile_list_minmod_neighbour_fluxes_kernel(
             done = max(units.index(jts[-1]) + 2, turned[jts[-1]])
             groups = 2 if jts == (7,) else len(jts)
             later = units.index(min(2 * (jts[0] // 2) + 3, 7)) + 2
-            lag = max(later - done, 0) if jts[0] + 1 in HELD and jts[0] < 6 else LAG
             before[done].append(lambda jts=jts: quant_h(1, jts))
             after[done].append(lambda jts=jts, groups=groups: face(jts, groups))
-            after[done + lag].append(lambda jts=jts, groups=groups: flux(jts, groups))
+            for g in range(groups):
+                at = later if jts[0] + g in HELD else done + LAG
+                after[at].append(lambda jts=jts, groups=groups, g=g: flux(jts, groups, [g]))
 
         pending = None
         sums_of = {}

@@ -22,6 +22,8 @@ ON_POOL = [(1, 256)]
 ON_VECTOR = [(1, 0)]
 POOL_WIND = 4
 LAG = 2
+RUNS = 1
+BOTH = (0,)
 POOL_COLS = (0, 0)
 HOLD = 1
 JOINT = (256, 512)
@@ -51,7 +53,10 @@ def tile_list_minmod_neighbour_fluxes_kernel(
         def bank_for(role, shape):
             n = turns[role]
             turns[role] = n + 1
-            if role == "back":
+            if BANKS == 2:
+                turns["all"] = turns.get("all", -1) + 1
+                number = turns["all"] % 8
+            elif role == "back":
                 number = n % 4
             elif BANKS == 1:
                 turns["other"] = turns.get("other", -1) + 1
@@ -157,7 +162,7 @@ def tile_list_minmod_neighbour_fluxes_kernel(
                 grouped[a, c0] = held("grp%d_%d" % (a, c0), [P, 4 * width], BF16)[:]
             else:
                 if a == 0:
-                    grouped[c0] = placed("grp_%d" % c0, [P, 8 * width], BF16, 90)
+                    grouped[c0] = placed("grp_%d" % c0, [P, 8 * width], BF16, 100 if c0 == 256 else 93)
                 grouped[a, c0] = grouped[c0][:, 4 * width * a : 4 * width * (a + 1)]
             if c0 == 512:
                 dst = grouped[a, c0].rearrange("p (t m i) -> p m i t", t=4, i=4)
@@ -197,7 +202,7 @@ def tile_list_minmod_neighbour_fluxes_kernel(
             nc.vector.quantize_mx(out=wbq[a, c0].bitcast(E4M3), scales=wbs[a, c0], in_=grouped[a, c0])
 
         f_sb = {(0, b): held("f0_%d" % b, [P, 4, 256], F32) for b in range(2, 4)}
-        h_sb = {(s, b): held("h%d_%d" % (s, b), [P, 4, 256], BF16) for s in range(1) for b in range(4)}
+        h_sb = {(0, b): held("h0_%d" % b, [P, 4, 256], BF16) for b in range(4)}
 
         def forward(s, jts):
             banks = {jt: bank_for("fwd", [P, 512]) for jt in jts}
@@ -264,13 +269,19 @@ def tile_list_minmod_neighbour_fluxes_kernel(
             )
 
         dealt, f_late = {}, {}
-        h_late = [placed("hl%d" % b, [P, 2, 512], BF16, 71 + 4 * b) for b in range(4)]
+        h_late = [placed("hl%d" % b, [P, 2, 512], BF16, 111 + 8 * b) for b in range(4)]
 
-        def deal_wf():
-            dealt["codes"] = placed("wfd", [P, 2, 4, 128], U16, 68)
-            nc.vector.tensor_copy(dealt["codes"][:], wf[1][:].bitcast(U16).rearrange("p a (m t) -> p a t m", t=4))
-            dealt["scales"] = placed("wfp", [P, 2, 4, 128], U8, 57)
-            nc.vector.tensor_copy(dealt["scales"][:], wfs[:, :, PASS:].rearrange("p a (m t) -> p a t m", t=4))
+        def deal_scales():
+            dealt["scales"] = placed("wfp", [P, 2, 4, 128], U8, 68)
+            nc.gpsimd.tensor_copy(dealt["scales"][:], wfs[:, :, PASS:].rearrange("p a (m t) -> p a t m", t=4))
+
+        def deal_codes():
+            dealt["codes"] = placed("wfd", [P, 2, 4, 256], U8, 103)
+            for a in range(2):
+                nc.gpsimd.tensor_copy(
+                    dealt["codes"][:, a].rearrange("p t (m z) -> p t m z", z=2),
+                    wf[1][:, a, :].rearrange("p (m t z) -> p t m z", t=4, z=2),
+                )
 
         def slope(role, jt):
             bank = bank_for(role, [P, 4, 128])
@@ -364,26 +375,20 @@ def tile_list_minmod_neighbour_fluxes_kernel(
         def flux(jts, groups, which):
             per_bank, width = 4 // groups, 128 * len(jts)
             inside = 128 * (jts[0] % 4)
-            for g in which:
-                name = "res%d_%d" % (jts[0], g)
-                if jts[0] + g in HELD:
-                    res = placed(name, [P, per_bank, width], F32, 74 + 2 * jts[0])
-                else:
-                    res = held(name, [P, per_bank, width], F32)
-                factor = winds[jts[0] // 4][:, per_bank * g : per_bank * (g + 1), inside : inside + width]
-                if jts[0] + g in HELD:
-                    sums = ring.tile([P, per_bank, width], F32, name="sums")
-                    nc.scalar.copy(sums[:], faces[jts, g][:])
-                    for c0 in range(0, 512, PIECE):
-                        y0, y1, x0 = c0 // width, (c0 + PIECE - 1) // width + 1, c0 % width
-                        x1 = x0 + min(PIECE, width)
-                        nc.gpsimd.tensor_tensor(
-                            res[:, y0:y1, x0:x1], sums[:, y0:y1, x0:x1], factor[:, y0:y1, x0:x1], ALU.mult
-                        )
-                else:
-                    nc.vector.tensor_tensor(res[:], faces[jts, g][:], factor, ALU.mult)
-                rows = slice(128 * per_bank * g, 128 * per_bank * (g + 1))
-                nc.sync.dma_start(out[rows, cells(jts)].rearrange("(y p) j -> p y j", p=P), res[:])
+            first, count = per_bank * which[0], per_bank * len(which)
+            name = "res%d_%d" % (jts[0], which[0])
+            factor = winds[jts[0] // 4][:, first : first + count, inside : inside + width]
+            if jts[0] + which[0] in HELD:
+                res = placed(name, [P, count, width], F32, 116 + 4 * jts[0])
+                sums = ring.tile([P, count, width], F32, name="sums")
+                for x, g in enumerate(which):
+                    nc.scalar.copy(sums[:, per_bank * x : per_bank * (x + 1), :], faces[jts, g][:])
+                nc.gpsimd.tensor_tensor(res[:], sums[:], factor, ALU.mult)
+            else:
+                res = held(name, [P, count, width], F32)
+                nc.vector.tensor_tensor(res[:], faces[jts, which[0]][:], factor, ALU.mult)
+            rows = slice(128 * first, 128 * (first + count))
+            nc.sync.dma_start(out[rows, cells(jts)].rearrange("(y p) j -> p y j", p=P), res[:])
 
         gather_words(0, 0, 8)
         load_wf(1, placed("wf1", [P, 2, H], U8, 17))
@@ -397,7 +402,7 @@ def tile_list_minmod_neighbour_fluxes_kernel(
         cast_wb(1, 0, 256)
         load_wb(1, 512, 512, placed("raw1_512", [P, 4, 512], F32, 41))
         quant_wb(1, 0, 256)
-        deal_wf()
+        deal_scales()
         wxs = placed("wxs", [P, 2, N], U8, 67)
         nc.gpsimd.memset(wxs[:].bitcast(I32), 0)
         for d in range(4):
@@ -438,13 +443,14 @@ def tile_list_minmod_neighbour_fluxes_kernel(
             before[3 + EARLY - AHEAD + a].append(lambda a=a: quant_wb(a, 512, 512))
         for jt in range(8):
             after[min(FWD1_AT + jt, units.index(jt) - 2) if jt < 4 else units.index(jt) - FWD_LEAD].append(lambda jt=jt: forward_late(jt))
+        before[4 - AHEAD].append(deal_codes)
         before[1].append(load_wx)
         before[1].append(lambda: load_wind(0))
         before[3].append(lambda: load_wind(1))
         turned = {}
         for jts in pairs:
-            at = units.index((256, 256, jts)) + 2
-            before[at].append(lambda jts=jts: turn(0, jts))
+            at = units.index((256, 256, pairs[jts[0] // 4 * 2 + 1] if RUNS else jts)) + 2
+            before[at].insert(0, lambda jts=jts: turn(0, jts))
         for jts in FIRST_GROUPS:
             at = units.index((256, 256, jts[-2:])) + 3
             before[at].append(lambda jts=jts: quant_h(0, jts))
@@ -456,9 +462,9 @@ def tile_list_minmod_neighbour_fluxes_kernel(
             later = units.index(min(2 * (jts[0] // 2) + 3, 7)) + 2
             before[done].append(lambda jts=jts: quant_h(1, jts))
             after[done].append(lambda jts=jts, groups=groups: face(jts, groups))
-            for g in range(groups):
-                at = later if jts[0] + g in HELD else done + LAG
-                after[at].append(lambda jts=jts, groups=groups, g=g: flux(jts, groups, [g]))
+            for which in [[0, 1]] if jts[0] in BOTH else [[g] for g in range(groups)]:
+                at = later if jts[0] + which[0] in HELD else done + LAG
+                after[at].append(lambda jts=jts, groups=groups, which=which: flux(jts, groups, which))
 
         pending = None
         sums_of = {}

@@ -18,25 +18,23 @@ ALU = mybir.AluOpType
 
 P = 128
 PASS = 512
-ON_POOL = [(1, 256)]
-ON_VECTOR = [(1, 0)]
-POOL_WIND = 4
-LAG = 2
-RUNS = 1
-BOTH = (0,)
-POOL_COLS = (0, 0)
-HOLD = 1
-JOINT = (256, 512)
-FIRST_GROUPS = [(0, 1, 2, 3), (4, 5, 6, 7)]
-HELD = (0, 2)
-PIECE = 512
 EARLY = 4
-FWD_LEAD = 4
-BANKS = 1
-AHEAD = 2
-FWD1_AT = 3
-FWD_WIDE = 12
+BACK_AT = (-3, -3, -1, -1, 3, 3, 3, 4, 7, 7, 7, 8, 8, 8, 11, 11)
+WIND_AT = {(2, 0): 14.5, (2, 1): 15.5, (4, 0): 18, (4, 1): 18, (5, 0): 18, (6, 0): 18, (7, 0): 18, (7, 1): 18, (6, 1): 18}
+FWD_AT = (0, 0, 0, 4, 4, 4, 8, 8)
+SPLIT0 = 1
 GROUPS = [(0, 1), (2, 3), (4, 5), (6,), (7,)]
+ON_POOL = [(0, 0), (0, 1)]
+WFS_ON_POOL = 1
+MOVES_ON_ACT = 0
+Q256_AT = (1, 2)
+Q512_AT = (6, 6)
+CAST512_AT = (2, 2, 3, 5)
+CAST_HOLD = (0, 1)
+WIDE_ON_POOL = [(1, 0)]
+COPY_AT = (2, 2, 2, 5, 5, 5, 8, 8)
+TURN_AT = (6, 8)
+QE_AT = (9, 12)
 
 
 def tile_list_minmod_neighbour_fluxes_kernel(
@@ -46,48 +44,35 @@ def tile_list_minmod_neighbour_fluxes_kernel(
     with ExitStack() as ctx:
         keep = ctx.enter_context(tc.tile_pool(name="keep", bufs=1))
         shared = ctx.enter_context(tc.tile_pool(name="shared", bufs=1))
-        ring = ctx.enter_context(tc.tile_pool(name="ring", bufs=3))
         psum = ctx.enter_context(tc.psum_pool(name="psum", bufs=1))
-        turns = {"fwd": 0, "back": 0, "turn": 0, "face": 0}
+        taken = []
 
         def bank_for(role, shape):
-            n = turns[role]
-            turns[role] = n + 1
-            if BANKS == 2:
-                turns["all"] = turns.get("all", -1) + 1
-                number = turns["all"] % 8
-            elif role == "back":
-                number = n % 4
-            elif BANKS == 1:
-                turns["other"] = turns.get("other", -1) + 1
-                number = 4 + turns["other"] % 4
-            elif role == "fwd":
-                number = 4 + n % 4 if n < FWD_WIDE else 4
-            elif role == "turn":
-                number = 5
-            else:
-                number = 6 + n % 2
-            return psum.tile(shape, F32, name=role, tag="bank%d" % number)
+            taken.append(role)
+            return psum.tile(shape, F32, name=role, tag="bank%d" % ((len(taken) - 1) % 8))
 
+        def held(name, shape, dtype):
+            return keep.tile(shape, dtype, name=name, tag=name, align_bytes=64)
 
-        def held(name, shape, dtype, slot=None):
-            return keep.tile(shape, dtype, name=name, tag=slot or name, align_bytes=64)
+        def placed(name, shape, dtype, kib):
+            return shared.tile(shape, dtype, name=name, align_bytes=64, offset=int(1024 * kib))
 
         offsets = keep.tile([P, S // 16], U16, name="offsets")
         nc.sync.dma_start(offsets[:], offs)
 
-        def placed(name, shape, dtype, kib):
-            return shared.tile(shape, dtype, name=name, align_bytes=64, offset=1024 * kib)
+        win = placed("win", [P, T], U8, 0)
+        by_row = tab_scales.bitcast(I32).rearrange("a q c -> q a c")
+        for c in (0, 2):
+            nc.sync.dma_start(win[:].bitcast(I32)[c:P:4, :], by_row)
+        next_row = tab_scales.bitcast(I32).rearrange("a q c -> (a q) c")[1:17]
+        nc.sync.dma_start(win[:].bitcast(I32)[1:P:2, :], next_row.unsqueeze(1).to_broadcast([16, 4, T // 4]))
 
-        win = placed("win", [P, T], U8, 37)
-        for a in range(2):
-            for e in range(2):
-                nc.sync.dma_start(
-                    win[:].bitcast(I32)[2 * a + e : P : 4, :],
-                    tab_scales[a].bitcast(I32)[e::2].unsqueeze(1).to_broadcast([8, 4, T // 4]),
-                )
-        tab = [placed("tab0", [P, T], I32, 12)]
-        nc.sync.dma_start(tab[0][:], tab_words[0].rearrange("p t i -> p (t i)").bitcast(I32))
+        tab = [placed("tab0", [P, T], I32, 14), held("tab1", [P, T], I32)]
+
+        def load_tab(a):
+            nc.sync.dma_start(tab[a][:], tab_words[a].rearrange("p t i -> p (t i)").bitcast(I32))
+
+        load_tab(0)
 
         raw = {}
 
@@ -106,38 +91,37 @@ def tile_list_minmod_neighbour_fluxes_kernel(
                 wf_words.bitcast(I32)[:, :, 256 * s : 256 * (s + 1)].rearrange("a p c -> p a c"),
             )
 
-        zero = placed("zero", [P, H // 2], I32, 51)
-        nc.vector.memset(zero[:], 0)
+        def load_plane(queue, plane, scales):
+            for r in range(4):
+                queue.dma_start(
+                    plane[:].bitcast(I32)[r:P:32], scales.bitcast(I32)[:, r::4, :].rearrange("a d c -> d a c")
+                )
+
         wfs = held("wfs", [P, 2, H], U8)
-        nc.vector.tensor_copy(wfs[:].bitcast(I32).rearrange("p a c -> p (a c)"), zero[:])
-        for d in range(4):
-            nc.sync.dma_start(
-                wfs[:].bitcast(I32)[32 * d : 32 * d + 4],
-                wf_scales.bitcast(I32)[:, 4 * d : 4 * d + 4, :].rearrange("a r c -> r a c"),
-            )
-        load_wf(0, placed("wf0", [P, 2, H], U8, 50))
-        tab.append(placed("tab1", [P, T], I32, 52))
-        nc.sync.dma_start(tab[1][:], tab_words[1].rearrange("p t i -> p (t i)").bitcast(I32))
+        nc.gpsimd.memset(wfs[:].bitcast(I32), 0)
+        load_plane(nc.gpsimd, wfs, wf_scales)
+        load_wf(0, held("wf0", [P, 2, H], U8))
+        load_tab(1)
 
-        vs = [held("vs%d" % a, [P, S], U8) for a in range(2)]
-        nc.vector.memset(vs[1][:].bitcast(I32), 0)
+        vs = [held("vs0", [P, S], U8), placed("vs1", [P, S], U8, 1)]
 
-        gs = held("gs", [P, S], U8)
+        zero = placed("zero", [P, S // 4], I32, 29)
+        nc.vector.memset(zero[:], 0)
+        gs = placed("gs", [P, S], U8, 6)
         nc.vector.tensor_copy(gs[:], win[:].indirect(offsets[:]))
+        nc.vector.tensor_copy(vs[1][:].bitcast(I32), zero[:])
         nc.vector.tensor_copy(vs[0][:].bitcast(I32), gs[:].bitcast(I32))
+        mover = nc.scalar if MOVES_ON_ACT else nc.sync
         for a, r in [(1, 0), (1, 1), (1, 2), (1, 3), (0, 2), (0, 3)]:
-            first = 16 * (r // 2) + 2 * a + r % 2
-            nc.sync.dma_start(vs[a][:].bitcast(I32)[r:P:32, :], gs[:].bitcast(I32)[first:P:32, :])
-        load_wb(0, 0, 256, placed("raw00", [P, 4, 256], F32, 34))
-        load_wb(1, 0, 256, placed("raw10", [P, 4, 256], F32, 38))
-        ident = held("ident", [P, P], F32)
-        make_identity(nc, ident[:])
+            first = 8 * r + 6 * a
+            mover.dma_start(vs[a][:].bitcast(I32)[r:P:32, :], gs[:].bitcast(I32)[first:P:32, :])
+        load_wb(0, 0, 256, placed("raw00", [P, 4, 256], F32, 29))
 
         v = {}
 
         def gather_words(a, first, count, kib=None):
-            name = "v%d_%d" % (a, first)
-            picked = held(name, [P, 128 * count], I32) if kib is None else placed(name, [P, 128 * count], I32, kib)
+            name, shape = "v%d_%d" % (a, first), [P, 128 * count]
+            picked = held(name, shape, I32) if kib is None else placed(name, shape, I32, kib)
             nc.vector.tensor_copy(
                 picked[:].bitcast(U32), tab[a][:].bitcast(U32).indirect(offsets[:, 8 * first : 8 * (first + count)])
             )
@@ -152,141 +136,141 @@ def tile_list_minmod_neighbour_fluxes_kernel(
 
         grouped, wbq, wbs = {}, {}, {}
 
-        def pool_cast(dst, src):
-            nc.gpsimd.tensor_scalar(dst, src, 1.0, 0.0, ALU.mult, ALU.add)
+        def slot(step):
+            return 80 + 9 * step
 
-        def cast_wb(a, c0, width):
-            if (a, c0) == (1, 0):
-                grouped[a, c0] = placed("grp1_0", [P, 4 * width], BF16, 67)[:]
-            elif c0 not in JOINT:
-                grouped[a, c0] = held("grp%d_%d" % (a, c0), [P, 4 * width], BF16)[:]
+        def behind(step, side, name, shape, dtype, kib):
+            return placed(name, shape, dtype, slot(step) + 1 if side else slot(step) + 1 - kib)
+
+        def cast_narrow(a, c0):
+            name = "grp%d_%d" % (a, c0)
+            shape = [P, 1024]
+            if (a, c0) == (0, 256):
+                grouped[a, c0] = held(name, shape, BF16)
+            elif c0 == 256:
+                grouped[a, c0] = placed(name, shape, BF16, 15.5)
             else:
                 if a == 0:
-                    grouped[c0] = placed("grp_%d" % c0, [P, 8 * width], BF16, 100 if c0 == 256 else 93)
-                grouped[a, c0] = grouped[c0][:, 4 * width * a : 4 * width * (a + 1)]
-            if c0 == 512:
-                dst = grouped[a, c0].rearrange("p (t m i) -> p m i t", t=4, i=4)
-                src = raw[a, c0][:].rearrange("p i (m t) -> p m i t", t=4)
-                split = 128 - POOL_COLS[a]
-                for m0 in range(0, split, 64):
-                    m1 = min(m0 + 64, split)
-                    nc.scalar.copy(dst[:, m0:m1], src[:, m0:m1])
-                for t in range(4 if split < 128 else 0):
-                    pool_cast(dst[:, split:, :, t], src[:, split:, :, t])
-                return
-            dst = grouped[a, c0].rearrange("p (u m e i) -> p m i u e", u=2, e=2, i=4)
+                    grouped["first"] = placed("grp_first", [P, 2048], BF16, 2.5)
+                grouped[a, c0] = grouped["first"][:, 1024 * a : 1024 * (a + 1)]
+            dst = grouped[a, c0][:].rearrange("p (u m e i) -> p m i u e", u=2, e=2, i=4)
             src = raw[a, c0][:].rearrange("p i (m u e) -> p m i u e", u=2, e=2)
-            if (a, c0) in ON_POOL:
+            if (a, c0) == (1, 256):
+                nc.scalar.copy(dst, src)
+            elif c0 == 256:
                 for u in range(2):
-                    pool_cast(
+                    nc.gpsimd.tensor_scalar(
                         dst[:, :, :, u, :].rearrange("p m i e -> p m e i"),
                         src[:, :, :, u, :].rearrange("p m i e -> p m e i"),
+                        1.0,
+                        0.0,
+                        ALU.mult,
+                        ALU.add,
                     )
             else:
-                copy = nc.vector.tensor_copy if (a, c0) in ON_VECTOR else nc.scalar.copy
-                copy(dst, src)
+                nc.vector.tensor_copy(dst, src)
+
+        def cast_wide(a, half):
+            if half == 0:
+                name = "grp%d_512" % a
+                grouped[a, 512] = behind(CAST_HOLD[a], 1, name, [P, 2048], BF16, 4)
+            dst = grouped[a, 512][:].rearrange("p (t m i) -> p m i t", t=4, i=4)[:, 64 * half : 64 * (half + 1)]
+            if (a, 768) in raw:
+                src = raw[a, 512 + 256 * half][:].rearrange("p i (m t) -> p m i t", t=4)
+            else:
+                src = raw[a, 512][:].rearrange("p i (m t) -> p m i t", t=4)[:, 64 * half : 64 * (half + 1)]
+            if (a, half) in WIDE_ON_POOL:
+                for u in range(2):
+                    nc.gpsimd.tensor_scalar(
+                        dst[:, :, :, 2 * u : 2 * u + 2].rearrange("p m i e -> p m e i"),
+                        src[:, :, :, 2 * u : 2 * u + 2].rearrange("p m i e -> p m e i"),
+                        1.0,
+                        0.0,
+                        ALU.mult,
+                        ALU.add,
+                    )
+            else:
+                nc.scalar.copy(dst, src)
+
+        def quant_first():
+            codes, scales = held("wbq_first", [P, 512], I32), held("wbs_first", [P, 512], U8)
+            nc.vector.quantize_mx(out=codes[:].bitcast(E4M3), scales=scales[:], in_=grouped["first"][:])
+            for a in range(2):
+                wbq[a, 0], wbs[a, 0] = codes[:, 256 * a : 256 * (a + 1)], scales[:, 256 * a : 256 * (a + 1)]
 
         def quant_wb(a, c0, width):
-            if c0 in JOINT:
-                if a == 0:
-                    return
-                codes = held("wbq_%d" % c0, [P, 2 * width], I32)
-                scales = held("wbs_%d" % c0, [P, 2 * width], U8)
-                nc.vector.quantize_mx(out=codes[:].bitcast(E4M3), scales=scales[:], in_=grouped[c0][:])
-                for x in range(2):
-                    wbq[x, c0] = codes[:, width * x : width * (x + 1)]
-                    wbs[x, c0] = scales[:, width * x : width * (x + 1)]
-                return
-            wbq[a, c0] = held("wbq%d_%d" % (a, c0), [P, width], I32)[:]
-            wbs[a, c0] = held("wbs%d_%d" % (a, c0), [P, width], U8)[:]
-            nc.vector.quantize_mx(out=wbq[a, c0].bitcast(E4M3), scales=wbs[a, c0], in_=grouped[a, c0])
+            name = "wbq%d_%d" % (a, c0)
+            step = (Q256_AT if c0 == 256 else Q512_AT)[a] - 1
+            wbq[a, c0] = behind(step, a if c0 == 512 else 0, name, [P, width], I32, width // 256)
+            wbs[a, c0] = held("wbs%d_%d" % (a, c0), [P, width], U8)
+            nc.vector.quantize_mx(out=wbq[a, c0][:].bitcast(E4M3), scales=wbs[a, c0][:], in_=grouped[a, c0][:])
 
-        f_sb = {(0, b): held("f0_%d" % b, [P, 4, 256], F32) for b in range(2, 4)}
-        h_sb = {(0, b): held("h0_%d" % b, [P, 4, 256], BF16) for b in range(4)}
+        units = [(0, b) for b in range(4)] + [(256, b) for b in range(EARLY)]
+        rest = [(256, b) for b in range(EARLY, 4)]
+        units = units + [0, 1, 2, 3][: 2 * EARLY] + rest + list(range(min(4, 2 * EARLY), 8))
+        f_sb = {}
+        for step, unit in enumerate(units):
+            if not isinstance(unit, int):
+                name = "f%d_%d" % unit
+                f_sb[unit] = placed(name, [P, 4, 128], F32, slot(step)) if step < 8 else held(name, [P, 4, 128], F32)
+        h_sb = [held("h%d" % b, [P, 4, 256], BF16) for b in range(4)]
 
-        def forward(s, jts):
-            banks = {jt: bank_for("fwd", [P, 512]) for jt in jts}
-            for a in range(2):
-                for jt in jts:
-                    nc.tensor.matmul_mx(
-                        out=banks[jt][:],
-                        lhsT=v_codes(a, jt),
-                        lhsT_scale=v_scales(a, jt),
-                        rhs=wf[s][:, a, :].bitcast(E2M1),
-                        rhs_scale=wfs[:, a, 512 * s : 512 * (s + 1)],
-                        start=(a == 0),
-                        stop=(a == 1),
-                    )
+        fwd_banks = {}
+
+        def forward(a, jts):
             for jt in jts:
-                jj = jt % 2
-                nc.scalar.copy(
-                    f_sb[s, jt // 2][:, 2 * jj : 2 * jj + 2, :].rearrange("p u (m e) -> p u m e", e=2),
-                    banks[jt][:].rearrange("p (m u e) -> p u m e", u=2, e=2),
+                if a == 0:
+                    fwd_banks[jt] = bank_for("fwd", [P, 512])
+                nc.tensor.matmul_mx(
+                    out=fwd_banks[jt][:],
+                    lhsT=v_codes(a, jt),
+                    lhsT_scale=v_scales(a, jt),
+                    rhs=wf[0][:, a, :].bitcast(E2M1),
+                    rhs_scale=wfs[:, a, 0:PASS],
+                    start=(a == 0),
+                    stop=(a == 1),
                 )
 
-        def backward(c0, width, jts):
+        def empty_forward(jt):
+            for c0 in (0, 256):
+                nc.scalar.copy(
+                    f_sb[c0, jt // 2][:, 2 * (jt % 2) : 2 * (jt % 2) + 2, :].rearrange("p u (m e) -> p u m e", e=2),
+                    fwd_banks[jt][:, c0 : c0 + 256].rearrange("p (m u e) -> p u m e", u=2, e=2),
+                )
+
+        def backward_pass(bank, a, c0, b):
+            for x in range(2):
+                nc.tensor.matmul_mx(
+                    out=bank[:, 256 * x : 256 * (x + 1)],
+                    lhsT=v_codes(a, 2 * b + x),
+                    lhsT_scale=v_scales(a, 2 * b + x),
+                    rhs=wbq[a, c0][:].bitcast(E4M3),
+                    rhs_scale=wbs[a, c0][:],
+                    start=(a == 0 and x == 0),
+                    stop=(a == 1 and x == 1),
+                )
+            return bank[:].rearrange("p (x c) -> p x c", c=128)
+
+        def backward(c0, b):
             bank = bank_for("back", [P, 512])
-            for a in range(2):
-                for x, jt in enumerate(jts):
-                    nc.tensor.matmul_mx(
-                        out=bank[:, width * x : width * (x + 1)],
-                        lhsT=v_codes(a, jt),
-                        lhsT_scale=v_scales(a, jt),
-                        rhs=wbq[a, c0].bitcast(E4M3),
-                        rhs_scale=wbs[a, c0],
-                        start=(a == 0 and x == 0),
-                        stop=(a == 1 and x == len(jts) - 1),
-                    )
-            return bank
-
-        def place(tiles, c0, width, jts):
-            s, b = c0 // 512, jts[0] // 2
-            first, run = 2 * (jts[0] % 2), width // 2
-            col = (c0 % 512) // 2
-            return tiles[s, b][:, first : first + 2 * len(jts), col : col + run]
-
-        def lower(unit, bank):
-            run = unit[1] // 2
-            nc.vector.scalar_tensor_tensor(
-                out=place(f_sb, *unit),
-                in0=bank[:].rearrange("p (x c) -> p x c", c=run),
-                scalar=0.0,
-                in1=place(f_sb, *unit),
-                op0=ALU.min,
-                op1=ALU.max,
-            )
-            return (bank,)
-
-        def upper(unit, bank):
-            run = unit[1] // 2
-            nc.vector.scalar_tensor_tensor(
-                out=place(h_sb, *unit),
-                in0=bank[:].rearrange("p (x c) -> p x c", c=run),
-                scalar=0.0,
-                in1=place(f_sb, *unit),
-                op0=ALU.max,
-                op1=ALU.min,
-            )
+            backward_pass(bank, 0, c0, b)
+            return backward_pass(bank, 1, c0, b)
 
         dealt, f_late = {}, {}
-        h_late = [placed("hl%d" % b, [P, 2, 512], BF16, 111 + 8 * b) for b in range(4)]
+        h_late = [placed("hl%d" % b, [P, 2, 512], BF16, 48 + 8 * b) for b in range(4)]
 
         def deal_scales():
-            dealt["scales"] = placed("wfp", [P, 2, 4, 128], U8, 68)
-            nc.gpsimd.tensor_copy(dealt["scales"][:], wfs[:, :, PASS:].rearrange("p a (m t) -> p a t m", t=4))
+            dealt["scales"] = placed("wfp", [P, 2, 4, 128], U8, 6.5)
+            nc.vector.tensor_copy(dealt["scales"][:], wfs[:, :, PASS:].rearrange("p a (m t) -> p a t m", t=4))
 
         def deal_codes():
-            dealt["codes"] = placed("wfd", [P, 2, 4, 256], U8, 103)
-            for a in range(2):
-                nc.gpsimd.tensor_copy(
-                    dealt["codes"][:, a].rearrange("p t (m z) -> p t m z", z=2),
-                    wf[1][:, a, :].rearrange("p (m t z) -> p t m z", t=4, z=2),
-                )
+            dealt["codes"] = placed("wfd", [P, 2, 4, 128], U16, 4)
+            nc.vector.tensor_copy(dealt["codes"][:], wf[1][:].bitcast(U16).rearrange("p a (m t) -> p a t m", t=4))
 
         def slope(role, jt):
             bank = bank_for(role, [P, 4, 128])
-            for t in range(4):
-                for a in range(2):
+            for a in range(2):
+                for t in range(4):
                     cols = slice(128 * t, 128 * (t + 1))
                     if role == "back":
                         codes, scales = wbq[a, 512][:, cols].bitcast(E4M3), wbs[a, 512][:, cols]
@@ -298,187 +282,211 @@ def tile_list_minmod_neighbour_fluxes_kernel(
                         lhsT_scale=scales,
                         rhs=v_codes(a, jt),
                         rhs_scale=v_scales(a, jt),
-                        start=(a == 0),
-                        stop=(a == 1),
+                        start=(a == 0 and t == 0),
+                        stop=(a == 1 and t == 3),
                     )
             return bank[:].rearrange("p t c -> p c t")
 
         def forward_late(jt):
-            f_late[jt] = held("fl%d" % jt, [P, 128, 4], F32)
-            nc.scalar.copy(f_late[jt][:], slope("fwd", jt))
+            fwd_banks[8 + jt] = slope("fwd", jt)
 
-        def lower_late(jt, back):
-            nc.vector.scalar_tensor_tensor(
-                out=f_late[jt][:], in0=back, scalar=0.0, in1=f_late[jt][:], op0=ALU.min, op1=ALU.max
-            )
-            return (back,)
+        def empty_late(jt):
+            if jt == 0:
+                f_late["first"] = behind(2, 1, "fl_first", [P, 3, 128, 4], F32, 6)
+            f_late[jt] = f_late["first"][:, jt] if jt < 3 else held("fl%d" % jt, [P, 128, 4], F32)
+            nc.scalar.copy(f_late[jt][:], fwd_banks[8 + jt])
 
-        def upper_late(jt, back):
-            nc.vector.scalar_tensor_tensor(
-                out=h_late[jt // 2][:, jt % 2, :].rearrange("p (c t) -> p c t", t=4),
-                in0=back,
-                scalar=0.0,
-                in1=f_late[jt][:],
-                op0=ALU.max,
-                op1=ALU.min,
-            )
+        def places(unit):
+            if isinstance(unit, int):
+                return f_late[unit][:], h_late[unit // 2][:, unit % 2, :].rearrange("p (c t) -> p c t", t=4)
+            c0, b = unit
+            cols = slice(c0 // 2, c0 // 2 + 128)
+            return f_sb[unit][:], h_sb[b][:, :, cols]
 
-        h_t = held("h_t", [P, 4 * S], BF16)
+        def lower(unit, back):
+            f = places(unit)[0]
+            nc.vector.scalar_tensor_tensor(out=f, in0=back, scalar=0.0, in1=f, op0=ALU.min, op1=ALU.max)
+
+        def upper(unit, back):
+            f, h = places(unit)
+            nc.vector.scalar_tensor_tensor(out=h, in0=back, scalar=0.0, in1=f, op0=ALU.max, op1=ALU.min)
+
+        late = {}
+
+        def make_ident():
+            late["ident"] = behind(3, 0, "ident", [P, P], F32, 0.5)
+            make_identity(nc, late["ident"][:])
+
+        h_t = [held("ht%d" % x, [P, 2048], BF16) for x in range(2)]
         hq = [held("hq%d" % s, [P, S], I32) for s in range(2)]
         hs = [held("hs%d" % s, [P, S], U8) for s in range(2)]
 
         def cells(jts):
             return slice(128 * jts[0], 128 * (jts[-1] + 1))
 
-        def turn(s, jts):
-            bank = bank_for("turn", [P, 2 * len(jts), P])
-            for y, jt in reversed(list(enumerate(jts))):
+        def turn(b):
+            bank = bank_for("turn", [P, 4, P])
+            for y in (1, 0):
                 for u in range(2):
-                    words = h_sb[s, jt // 2][:, 2 * (jt % 2) + u, :].bitcast(F32)
-                    nc.tensor.transpose(bank[:, 2 * y + u, :], words, ident[:])
+                    nc.tensor.transpose(bank[:, 2 * y + u, :], h_sb[b][:, 2 * y + u, :].bitcast(F32), late["ident"][:])
             nc.scalar.copy(
-                h_t[:, 512 * jts[0] : 512 * (jts[-1] + 1)].bitcast(F32).rearrange("p (y j u) -> p y j u", y=len(jts), u=2),
+                h_t[b // 2][:, 1024 * (b % 2) : 1024 * (b % 2 + 1)].bitcast(F32).rearrange("p (y j u) -> p y j u", y=2, u=2),
                 bank[:].rearrange("p (y u) j -> p y j u", u=2),
             )
 
-        def quant_h(s, jts):
+        def quant_early(x):
+            cols = slice(512 * x, 512 * (x + 1))
+            nc.vector.quantize_mx(out=hq[0][:, cols].bitcast(E4M3), scales=hs[0][:, cols], in_=h_t[x][:])
+
+        def quant_late(jts):
             cols = cells(jts)
-            if s == 0:
-                values = h_t[:, 512 * jts[0] : 512 * (jts[-1] + 1)]
-            else:
-                first = jts[0] % 2
-                values = h_late[jts[0] // 2][:, first : first + len(jts), :].rearrange("p x c -> p (x c)")
-            nc.vector.quantize_mx(out=hq[s][:, cols].bitcast(E4M3), scales=hs[s][:, cols], in_=values)
+            first = jts[0] % 2
+            values = h_late[jts[0] // 2][:, first : first + len(jts), :].rearrange("p x c -> p (x c)")
+            nc.vector.quantize_mx(out=hq[1][:, cols].bitcast(E4M3), scales=hs[1][:, cols], in_=values)
 
         faces = {}
-        late = {}
 
         def face(jts, groups):
             cols = cells(jts)
             per_bank = 4 // groups
             for g in range(groups):
                 bank = bank_for("face", [P, per_bank, 128 * len(jts)])
-                for s in (0, 1) if jts == (7,) else (1, 0):
+                order = (0, 1) if jts == (7,) else (1, 0)
+                for s in order:
                     for y in range(per_bank):
                         rows = slice(128 * (per_bank * g + y), 128 * (per_bank * g + y + 1))
                         nc.tensor.matmul_mx(
                             out=bank[:, y, :],
                             lhsT=late["wx"][:, s, rows].bitcast(E4M3),
-                            lhsT_scale=wxs[:, s, rows],
+                            lhsT_scale=late["wxs"][:, s, rows],
                             rhs=hq[s][:, cols].bitcast(E4M3),
                             rhs_scale=hs[s][:, cols],
-                            start=(s == int(jts != (7,)) and y == 0),
-                            stop=(s == int(jts == (7,)) and y == per_bank - 1),
+                            start=(s == order[0] and y == 0),
+                            stop=(s == order[1] and y == per_bank - 1),
                         )
                 faces[jts, g] = bank
 
-        def flux(jts, groups, which):
-            per_bank, width = 4 // groups, 128 * len(jts)
-            inside = 128 * (jts[0] % 4)
-            first, count = per_bank * which[0], per_bank * len(which)
-            name = "res%d_%d" % (jts[0], which[0])
-            factor = winds[jts[0] // 4][:, first : first + count, inside : inside + width]
-            if jts[0] + which[0] in HELD:
-                res = placed(name, [P, count, width], F32, 116 + 4 * jts[0])
-                sums = ring.tile([P, count, width], F32, name="sums")
-                for x, g in enumerate(which):
-                    nc.scalar.copy(sums[:, per_bank * x : per_bank * (x + 1), :], faces[jts, g][:])
-                nc.gpsimd.tensor_tensor(res[:], sums[:], factor, ALU.mult)
-            else:
-                res = held(name, [P, count, width], F32)
-                nc.vector.tensor_tensor(res[:], faces[jts, which[0]][:], factor, ALU.mult)
+        winds = {}
+
+        def store(jts, first, count, res):
             rows = slice(128 * first, 128 * (first + count))
             nc.sync.dma_start(out[rows, cells(jts)].rearrange("(y p) j -> p y j", p=P), res[:])
 
-        gather_words(0, 0, 8)
-        load_wf(1, placed("wf1", [P, 2, H], U8, 17))
-        load_wb(0, 256, 256, placed("raw0_256", [P, 4, 256], F32, 13))
-        load_wb(1, 256, 256, placed("raw1_256", [P, 4, 256], F32, 19))
-        gather_words(1, 0, 2)
-        gather_words(1, 2, 6)
-        load_wb(0, 512, 512, placed("raw0_512", [P, 4, 512], F32, 59))
-        cast_wb(0, 0, 256)
-        quant_wb(0, 0, 256)
-        cast_wb(1, 0, 256)
-        load_wb(1, 512, 512, placed("raw1_512", [P, 4, 512], F32, 41))
-        quant_wb(1, 0, 256)
-        deal_scales()
-        wxs = placed("wxs", [P, 2, N], U8, 67)
-        nc.gpsimd.memset(wxs[:].bitcast(I32), 0)
-        for d in range(4):
-            nc.sync.dma_start(
-                wxs[:].bitcast(I32)[32 * d : 32 * d + 4],
-                wx_scales.bitcast(I32)[:, 4 * d : 4 * d + 4, :].rearrange("a r c -> r a c"),
-            )
-        first_four = placed("f0_first", [P, 8, 256], F32, 27)
-        for b in range(2):
-            f_sb[0, b] = first_four[:, 4 * b : 4 * (b + 1), :]
-        forward(0, (0, 1))
-        forward(0, (2, 3))
+        def factor(jts, first, count):
+            inside = 128 * (jts[0] % 4)
+            return winds[jts[0] // 4][:, first : first + count, inside : inside + 128 * len(jts)]
 
-        winds = {}
+        def flux(jts, groups, g):
+            per_bank = 4 // groups
+            res = held("res%d_%d" % (jts[0], g), [P, per_bank, 128 * len(jts)], F32)
+            nc.vector.tensor_tensor(res[:], faces[jts, g][:], factor(jts, per_bank * g, per_bank), ALU.mult)
+            store(jts, per_bank * g, per_bank, res)
+
+        def flux_on_pool(jts, which):
+            count = 2 * len(which)
+            sums = held("sums%d" % jts[0], [P, count, 256], F32)
+            for x, g in enumerate(which):
+                nc.scalar.copy(sums[:, 2 * x : 2 * x + 2, :], faces[jts, g][:])
+            res = placed("res%d_p" % jts[0], [P, count, 256], F32, 48 + 8 * (jts[0] // 2 + 1) + 1)
+            nc.gpsimd.tensor_tensor(res[:], sums[:], factor(jts, 2 * which[0], count), ALU.mult)
+            store(jts, 2 * which[0], count, res)
+
+        gather_words(0, 0, 8)
+        load_wb(1, 0, 256, placed("raw10", [P, 4, 256], F32, 10.5))
+        load_wf(1, placed("wf1", [P, 2, H], U8, 15.5))
+        load_wb(0, 256, 256, placed("raw0_256", [P, 4, 256], F32, 17.5))
+        load_wb(1, 256, 256, placed("raw1_256", [P, 4, 256], F32, 21.5))
+        gather_words(1, 0, 2)
+        gather_words(1, 2, 4)
+        cast_narrow(0, 0)
+        load_wb(0, 512, 256, placed("raw0_512", [P, 4, 256], F32, 26.5))
+        load_wb(0, 768, 256, placed("raw0_768", [P, 4, 256], F32, 30.5))
+        deal_scales()
+        cast_narrow(1, 0)
+        load_wb(1, 512, 256, placed("raw1_512", [P, 4, 256], F32, 7.5))
+        load_wb(1, 768, 256, placed("raw1_768", [P, 4, 256], F32, 11.5))
+        quant_first()
+        gather_words(1, 6, 2, 3)
+        deal_codes()
+        sums_of = {}
+        forward(0, (0, 1, 2, 3))
+        forward(1, (0, 1))
+        forward(0, (4, 5, 6, 7))
+        forward(1, (2, 3, 4, 5))
+        for jt in range(6):
+            empty_forward(jt)
+        for b in range(2):
+            sums_of[b] = backward(0, b)
+        forward(1, (6, 7))
+        for jt in (6, 7):
+            empty_forward(jt)
 
         def load_wind(x):
-            winds[x] = placed("wind%d" % x, [P, 4, 512], F32, 19 + 22 * x)
+            winds[x] = placed("wind%d" % x, [P, 4, 512], F32, (22.5, 30.5)[x])
             nc.sync.dma_start(winds[x][:], wind[:, 512 * x : 512 * (x + 1)].rearrange("(m p) j -> p m j", p=P))
 
+        def load_wxs():
+            late["wxs"] = placed("wxs", [P, 2, N], U8, 8)
+            nc.gpsimd.memset(late["wxs"][:].bitcast(I32), 0)
+            load_plane(nc.sync, late["wxs"], wx_scales)
+
         def load_wx():
-            late["wx"] = placed("wx", [P, 2, N], I32, 13)
+            late["wx"] = placed("wx", [P, 2, N], I32, 17.5)
             nc.sync.dma_start(late["wx"][:], wx_words.rearrange("a p c i -> p a (c i)").bitcast(I32))
 
-        pairs = [(0, 1), (2, 3), (4, 5), (6, 7)]
-        units = [(0, 256, jts) for jts in pairs] + [(256, 256, jts) for jts in pairs[:EARLY]]
-        for x, jts in enumerate(pairs):
-            units.extend(jts)
-            if x + EARLY < 4:
-                units.append((256, 256, pairs[x + EARLY]))
         before = {i: [] for i in range(-4, 25)}
         after = {i: [] for i in before}
-        for jt in range(4, 8):
-            before[jt // 2 - 3].append(lambda jt=jt: forward(0, (jt,)))
+        last = {i: [] for i in before}
+        early = {i: [] for i in before}
         for a in range(2):
-            before[a - 1].append(lambda a=a: cast_wb(a, 256, 256))
-            before[3 - AHEAD + a].append(lambda a=a: quant_wb(a, 256, 256))
-            before[1 + a].append(lambda a=a: cast_wb(a, 512, 512))
-            before[3 + EARLY - AHEAD + a].append(lambda a=a: quant_wb(a, 512, 512))
+            before[a - 1].append(lambda a=a: cast_narrow(a, 256))
+            after[Q256_AT[a] + 1].append(lambda a=a: quant_wb(a, 256, 256))
+            for half in range(2):
+                before[CAST512_AT[2 * a + half]].append(lambda a=a, half=half: cast_wide(a, half))
+            after[Q512_AT[a] + 1].append(lambda a=a: quant_wb(a, 512, 512))
         for jt in range(8):
-            after[min(FWD1_AT + jt, units.index(jt) - 2) if jt < 4 else units.index(jt) - FWD_LEAD].append(lambda jt=jt: forward_late(jt))
-        before[4 - AHEAD].append(deal_codes)
+            last[FWD_AT[jt]].append(lambda jt=jt: forward_late(jt))
+        for jt in range(8):
+            last[COPY_AT[jt]].append(lambda jt=jt: empty_late(jt))
         before[1].append(load_wx)
-        before[1].append(lambda: load_wind(0))
-        before[3].append(lambda: load_wind(1))
+        before[5].append(make_ident)
+        before[5].append(load_wxs)
+        before[4].append(lambda: load_wind(0))
+        before[4].append(lambda: load_wind(1))
         turned = {}
-        for jts in pairs:
-            at = units.index((256, 256, pairs[jts[0] // 4 * 2 + 1] if RUNS else jts)) + 2
-            before[at].insert(0, lambda jts=jts: turn(0, jts))
-        for jts in FIRST_GROUPS:
-            at = units.index((256, 256, jts[-2:])) + 3
-            before[at].append(lambda jts=jts: quant_h(0, jts))
-            for jt in jts:
-                turned[jt] = at
+        for x in range(2):
+            early[TURN_AT[x]].append(lambda x=x: turn(2 * x))
+            early[TURN_AT[x]].append(lambda x=x: turn(2 * x + 1))
+            mid_at = QE_AT[x]
+            after[mid_at].append(lambda x=x: quant_early(x))
+            for jt in range(4 * x, 4 * x + 4):
+                turned[jt] = mid_at
         for jts in GROUPS:
             done = max(units.index(jts[-1]) + 2, turned[jts[-1]])
             groups = 2 if jts == (7,) else len(jts)
-            later = units.index(min(2 * (jts[0] // 2) + 3, 7)) + 2
-            before[done].append(lambda jts=jts: quant_h(1, jts))
+            after[done].append(lambda jts=jts: quant_late(jts))
             after[done].append(lambda jts=jts, groups=groups: face(jts, groups))
-            for which in [[0, 1]] if jts[0] in BOTH else [[g] for g in range(groups)]:
-                at = later if jts[0] + which[0] in HELD else done + LAG
-                after[at].append(lambda jts=jts, groups=groups, which=which: flux(jts, groups, which))
+            pooled = [g for g in range(groups) if (jts[0], g) in ON_POOL]
+            if pooled:
+                after[done + 2].append(lambda jts=jts, pooled=pooled: flux_on_pool(jts, pooled))
+            for g in range(groups):
+                if g not in pooled:
+                    at = WIND_AT[jts[0], g]
+                    (after if at == int(at) else early)[int(at)].append(lambda jts=jts, groups=groups, g=g: flux(jts, groups, g))
 
-        pending = None
-        sums_of = {}
         for i in range(-4, 25):
             for step in before[i]:
                 step()
-            nxt = i + AHEAD
-            if 0 <= nxt < 16:
-                sums_of[nxt] = slope("back", units[nxt]) if isinstance(units[nxt], int) else backward(*units[nxt])
+            if 0 <= i < 16:
+                lower(units[i], sums_of[i])
             for step in after[i]:
                 step()
-            made = None
-            if 0 <= i < 16:
-                made = (lower_late if isinstance(units[i], int) else lower)(units[i], sums_of[i])
-            if pending is not None:
-                (upper_late if isinstance(units[i - 1], int) else upper)(units[i - 1], *pending)
-            pending = made
+            if 1 <= i <= 16:
+                upper(units[i - 1], sums_of[i - 1])
+            for step in early[i]:
+                step()
+            for x in range(2, 16):
+                if BACK_AT[x] == i:
+                    sums_of[x] = slope("back", units[x]) if isinstance(units[x], int) else backward(*units[x])
+            for step in last[i]:
+                step()

@@ -18,23 +18,30 @@ ALU = mybir.AluOpType
 
 P = 128
 PASS = 512
+ORDER = (
+    "F0 F1 F2 F3 F4 F5 B0 B1 B2 F6 F7 B3 L0 L1 B4 B5 B6 B7 L2 L3 L4 L5 B8 B9 B10 B11 T0 T1 T2 T3"
+    " B12 B13 B14 B15 L6 L7 X0_0 X0_1 - - - - X2_0 X2_1 X4_0 X4_1 X6_0 X6_1 X7_0 X7_1"
+)
 EARLY = 4
-BACK_AT = (-3, -3, -1, -1, 3, 3, 3, 4, 7, 7, 7, 8, 8, 8, 11, 11)
-WIND_AT = {(2, 0): 14.5, (2, 1): 15.5, (4, 0): 18, (4, 1): 18, (5, 0): 18, (6, 0): 18, (7, 0): 18, (7, 1): 18, (6, 1): 18}
-FWD_AT = (0, 0, 0, 4, 4, 4, 8, 8)
+FL_HOLD = 2
+HEAD_BANKS = (0, 1, 2, 3, 4, 5, 6, 7, 0, 3, 4)
+RING = (1, 2, 5, 6, 7, 3, 4, 0)
+BACK_AT = (-3, -3, -1, -1, 2, 2, 2, 2, 7, 7, 7, 7, 9, 10, 11, 12)
+WIND_AT = {(2, 0): 14.5, (2, 1): 16.5, (4, 0): 18, (4, 1): 18, (6, 0): 18, (6, 1): 18}
+FWD_AT = (0, 0, 3, 3, 3, 3, 8, 8)
 SPLIT0 = 1
-GROUPS = [(0, 1), (2, 3), (4, 5), (6,), (7,)]
+GROUPS = [(0, 1), (2, 3), (4, 5), (6, 7)]
 ON_POOL = [(0, 0), (0, 1)]
 WFS_ON_POOL = 1
 MOVES_ON_ACT = 0
-Q256_AT = (1, 2)
+Q256_AT = (1, 1)
 Q512_AT = (6, 6)
-CAST512_AT = (2, 2, 3, 5)
-CAST_HOLD = (0, 1)
-WIDE_ON_POOL = [(1, 0)]
-COPY_AT = (2, 2, 2, 5, 5, 5, 8, 8)
+CAST512_AT = (2, 2, 3, 4)
+CAST_HOLD = (1, 1)
+WIDE_ON_POOL = [(0, 1), (1, 0)]
+COPY_AT = (2, 2, 3, 3, 5, 5, 8, 8)
 TURN_AT = (6, 8)
-QE_AT = (9, 12)
+QE_AT = (11, 13)
 
 
 def tile_list_minmod_neighbour_fluxes_kernel(
@@ -45,11 +52,12 @@ def tile_list_minmod_neighbour_fluxes_kernel(
         keep = ctx.enter_context(tc.tile_pool(name="keep", bufs=1))
         shared = ctx.enter_context(tc.tile_pool(name="shared", bufs=1))
         psum = ctx.enter_context(tc.psum_pool(name="psum", bufs=1))
-        taken = []
+        order = ORDER.split()
 
         def bank_for(role, shape):
-            taken.append(role)
-            return psum.tile(shape, F32, name=role, tag="bank%d" % ((len(taken) - 1) % 8))
+            n = order.index(role)
+            number = HEAD_BANKS[n] if n < len(HEAD_BANKS) else RING[(n - len(HEAD_BANKS)) % 8]
+            return psum.tile(shape, F32, name=role, tag="bank%d" % number)
 
         def held(name, shape, dtype):
             return keep.tile(shape, dtype, name=name, tag=name, align_bytes=64)
@@ -60,14 +68,14 @@ def tile_list_minmod_neighbour_fluxes_kernel(
         offsets = keep.tile([P, S // 16], U16, name="offsets")
         nc.sync.dma_start(offsets[:], offs)
 
-        win = placed("win", [P, T], U8, 0)
+        win = placed("win", [P, T], U8, 30)
         by_row = tab_scales.bitcast(I32).rearrange("a q c -> q a c")
         for c in (0, 2):
             nc.sync.dma_start(win[:].bitcast(I32)[c:P:4, :], by_row)
         next_row = tab_scales.bitcast(I32).rearrange("a q c -> (a q) c")[1:17]
         nc.sync.dma_start(win[:].bitcast(I32)[1:P:2, :], next_row.unsqueeze(1).to_broadcast([16, 4, T // 4]))
 
-        tab = [placed("tab0", [P, T], I32, 14), held("tab1", [P, T], I32)]
+        tab = [placed("tab0", [P, T], I32, 14), placed("tab1", [P, T], I32, 75)]
 
         def load_tab(a):
             nc.sync.dma_start(tab[a][:], tab_words[a].rearrange("p t i -> p (t i)").bitcast(I32))
@@ -97,19 +105,19 @@ def tile_list_minmod_neighbour_fluxes_kernel(
                     plane[:].bitcast(I32)[r:P:32], scales.bitcast(I32)[:, r::4, :].rearrange("a d c -> d a c")
                 )
 
+        blank = placed("blank", [P, H // 2], I32, 74)
+        nc.vector.memset(blank[:], 0)
         wfs = held("wfs", [P, 2, H], U8)
-        nc.gpsimd.memset(wfs[:].bitcast(I32), 0)
-        load_plane(nc.gpsimd, wfs, wf_scales)
-        load_wf(0, held("wf0", [P, 2, H], U8))
+        nc.vector.tensor_copy(wfs[:].bitcast(I32).rearrange("p a c -> p (a c)"), blank[:])
+        load_plane(nc.sync, wfs, wf_scales)
+        load_wf(0, placed("wf0", [P, 2, H], U8, 73))
         load_tab(1)
 
-        vs = [held("vs0", [P, S], U8), placed("vs1", [P, S], U8, 1)]
+        vs = [held("vs%d" % a, [P, S], U8) for a in range(2)]
+        nc.vector.memset(vs[1][:].bitcast(I32), 0)
 
-        zero = placed("zero", [P, S // 4], I32, 29)
-        nc.vector.memset(zero[:], 0)
-        gs = placed("gs", [P, S], U8, 6)
+        gs = placed("gs", [P, S], U8, 45)
         nc.vector.tensor_copy(gs[:], win[:].indirect(offsets[:]))
-        nc.vector.tensor_copy(vs[1][:].bitcast(I32), zero[:])
         nc.vector.tensor_copy(vs[0][:].bitcast(I32), gs[:].bitcast(I32))
         mover = nc.scalar if MOVES_ON_ACT else nc.sync
         for a, r in [(1, 0), (1, 1), (1, 2), (1, 3), (0, 2), (0, 3)]:
@@ -137,7 +145,7 @@ def tile_list_minmod_neighbour_fluxes_kernel(
         grouped, wbq, wbs = {}, {}, {}
 
         def slot(step):
-            return 80 + 9 * step
+            return 88 + 9 * step
 
         def behind(step, side, name, shape, dtype, kib):
             return placed(name, shape, dtype, slot(step) + 1 if side else slot(step) + 1 - kib)
@@ -148,11 +156,9 @@ def tile_list_minmod_neighbour_fluxes_kernel(
             if (a, c0) == (0, 256):
                 grouped[a, c0] = held(name, shape, BF16)
             elif c0 == 256:
-                grouped[a, c0] = placed(name, shape, BF16, 15.5)
+                grouped[a, c0] = placed(name, shape, BF16, 39.5)
             else:
-                if a == 0:
-                    grouped["first"] = placed("grp_first", [P, 2048], BF16, 2.5)
-                grouped[a, c0] = grouped["first"][:, 1024 * a : 1024 * (a + 1)]
+                grouped[a, c0] = placed(name, shape, BF16, (43, 41)[a])
             dst = grouped[a, c0][:].rearrange("p (u m e i) -> p m i u e", u=2, e=2, i=4)
             src = raw[a, c0][:].rearrange("p i (m u e) -> p m i u e", u=2, e=2)
             if (a, c0) == (1, 256):
@@ -168,12 +174,12 @@ def tile_list_minmod_neighbour_fluxes_kernel(
                         ALU.add,
                     )
             else:
-                nc.vector.tensor_copy(dst, src)
+                (nc.vector.tensor_copy if a == 1 else nc.scalar.copy)(dst, src)
 
         def cast_wide(a, half):
             if half == 0:
                 name = "grp%d_512" % a
-                grouped[a, 512] = behind(CAST_HOLD[a], 1, name, [P, 2048], BF16, 4)
+                grouped[a, 512] = behind(CAST_HOLD[a], 1 - a, name, [P, 2048], BF16, 4)
             dst = grouped[a, 512][:].rearrange("p (t m i) -> p m i t", t=4, i=4)[:, 64 * half : 64 * (half + 1)]
             if (a, 768) in raw:
                 src = raw[a, 512 + 256 * half][:].rearrange("p i (m t) -> p m i t", t=4)
@@ -192,16 +198,13 @@ def tile_list_minmod_neighbour_fluxes_kernel(
             else:
                 nc.scalar.copy(dst, src)
 
-        def quant_first():
-            codes, scales = held("wbq_first", [P, 512], I32), held("wbs_first", [P, 512], U8)
-            nc.vector.quantize_mx(out=codes[:].bitcast(E4M3), scales=scales[:], in_=grouped["first"][:])
-            for a in range(2):
-                wbq[a, 0], wbs[a, 0] = codes[:, 256 * a : 256 * (a + 1)], scales[:, 256 * a : 256 * (a + 1)]
-
         def quant_wb(a, c0, width):
             name = "wbq%d_%d" % (a, c0)
-            step = (Q256_AT if c0 == 256 else Q512_AT)[a] - 1
-            wbq[a, c0] = behind(step, a if c0 == 512 else 0, name, [P, width], I32, width // 256)
+            if c0 == 0:
+                wbq[a, c0] = held(name, [P, width], I32)
+            else:
+                step = (Q256_AT if c0 == 256 else Q512_AT)[a] - 1
+                wbq[a, c0] = behind(step, a, name, [P, width], I32, width // 256)
             wbs[a, c0] = held("wbs%d_%d" % (a, c0), [P, width], U8)
             nc.vector.quantize_mx(out=wbq[a, c0][:].bitcast(E4M3), scales=wbs[a, c0][:], in_=grouped[a, c0][:])
 
@@ -220,7 +223,7 @@ def tile_list_minmod_neighbour_fluxes_kernel(
         def forward(a, jts):
             for jt in jts:
                 if a == 0:
-                    fwd_banks[jt] = bank_for("fwd", [P, 512])
+                    fwd_banks[jt] = bank_for("F%d" % jt, [P, 512])
                 nc.tensor.matmul_mx(
                     out=fwd_banks[jt][:],
                     lhsT=v_codes(a, jt),
@@ -231,8 +234,8 @@ def tile_list_minmod_neighbour_fluxes_kernel(
                     stop=(a == 1),
                 )
 
-        def empty_forward(jt):
-            for c0 in (0, 256):
+        def empty_forward(jt, chunks):
+            for c0 in chunks:
                 nc.scalar.copy(
                     f_sb[c0, jt // 2][:, 2 * (jt % 2) : 2 * (jt % 2) + 2, :].rearrange("p u (m e) -> p u m e", e=2),
                     fwd_banks[jt][:, c0 : c0 + 256].rearrange("p (m u e) -> p u m e", u=2, e=2),
@@ -252,7 +255,7 @@ def tile_list_minmod_neighbour_fluxes_kernel(
             return bank[:].rearrange("p (x c) -> p x c", c=128)
 
         def backward(c0, b):
-            bank = bank_for("back", [P, 512])
+            bank = bank_for("B%d" % units.index((c0, b)), [P, 512])
             backward_pass(bank, 0, c0, b)
             return backward_pass(bank, 1, c0, b)
 
@@ -260,15 +263,15 @@ def tile_list_minmod_neighbour_fluxes_kernel(
         h_late = [placed("hl%d" % b, [P, 2, 512], BF16, 48 + 8 * b) for b in range(4)]
 
         def deal_scales():
-            dealt["scales"] = placed("wfp", [P, 2, 4, 128], U8, 6.5)
+            dealt["scales"] = placed("wfp", [P, 2, 4, 128], U8, 45.5)
             nc.vector.tensor_copy(dealt["scales"][:], wfs[:, :, PASS:].rearrange("p a (m t) -> p a t m", t=4))
 
         def deal_codes():
-            dealt["codes"] = placed("wfd", [P, 2, 4, 128], U16, 4)
+            dealt["codes"] = placed("wfd", [P, 2, 4, 128], U16, 43)
             nc.vector.tensor_copy(dealt["codes"][:], wf[1][:].bitcast(U16).rearrange("p a (m t) -> p a t m", t=4))
 
         def slope(role, jt):
-            bank = bank_for(role, [P, 4, 128])
+            bank = bank_for("B%d" % units.index(jt) if role == "back" else "L%d" % jt, [P, 4, 128])
             for a in range(2):
                 for t in range(4):
                     cols = slice(128 * t, 128 * (t + 1))
@@ -292,8 +295,8 @@ def tile_list_minmod_neighbour_fluxes_kernel(
 
         def empty_late(jt):
             if jt == 0:
-                f_late["first"] = behind(2, 1, "fl_first", [P, 3, 128, 4], F32, 6)
-            f_late[jt] = f_late["first"][:, jt] if jt < 3 else held("fl%d" % jt, [P, 128, 4], F32)
+                f_late["first"] = behind(FL_HOLD, 1, "fl_first", [P, 2, 128, 4], F32, 4)
+            f_late[jt] = f_late["first"][:, jt] if jt < 2 else held("fl%d" % jt, [P, 128, 4], F32)
             nc.scalar.copy(f_late[jt][:], fwd_banks[8 + jt])
 
         def places(unit):
@@ -325,7 +328,7 @@ def tile_list_minmod_neighbour_fluxes_kernel(
             return slice(128 * jts[0], 128 * (jts[-1] + 1))
 
         def turn(b):
-            bank = bank_for("turn", [P, 4, P])
+            bank = bank_for("T%d" % b, [P, 4, P])
             for y in (1, 0):
                 for u in range(2):
                     nc.tensor.transpose(bank[:, 2 * y + u, :], h_sb[b][:, 2 * y + u, :].bitcast(F32), late["ident"][:])
@@ -350,7 +353,7 @@ def tile_list_minmod_neighbour_fluxes_kernel(
             cols = cells(jts)
             per_bank = 4 // groups
             for g in range(groups):
-                bank = bank_for("face", [P, per_bank, 128 * len(jts)])
+                bank = bank_for("X%d_%d" % (jts[0], g), [P, per_bank, 128 * len(jts)])
                 order = (0, 1) if jts == (7,) else (1, 0)
                 for s in order:
                     for y in range(per_bank):
@@ -391,35 +394,39 @@ def tile_list_minmod_neighbour_fluxes_kernel(
             nc.gpsimd.tensor_tensor(res[:], sums[:], factor(jts, 2 * which[0], count), ALU.mult)
             store(jts, 2 * which[0], count, res)
 
-        gather_words(0, 0, 8)
-        load_wb(1, 0, 256, placed("raw10", [P, 4, 256], F32, 10.5))
-        load_wf(1, placed("wf1", [P, 2, H], U8, 15.5))
-        load_wb(0, 256, 256, placed("raw0_256", [P, 4, 256], F32, 17.5))
-        load_wb(1, 256, 256, placed("raw1_256", [P, 4, 256], F32, 21.5))
+        gather_words(0, 0, 4)
+        gather_words(0, 4, 4)
+        load_wb(1, 0, 256, placed("raw10", [P, 4, 256], F32, 10.125))
+        load_wf(1, placed("wf1", [P, 2, H], U8, 15.75))
+        load_wb(0, 256, 256, placed("raw0_256", [P, 4, 256], F32, 17.75))
+        load_wb(1, 256, 256, placed("raw1_256", [P, 4, 256], F32, 21.75))
         gather_words(1, 0, 2)
-        gather_words(1, 2, 4)
+        gather_words(1, 2, 6)
         cast_narrow(0, 0)
         load_wb(0, 512, 256, placed("raw0_512", [P, 4, 256], F32, 26.5))
         load_wb(0, 768, 256, placed("raw0_768", [P, 4, 256], F32, 30.5))
         deal_scales()
         cast_narrow(1, 0)
-        load_wb(1, 512, 256, placed("raw1_512", [P, 4, 256], F32, 7.5))
-        load_wb(1, 768, 256, placed("raw1_768", [P, 4, 256], F32, 11.5))
-        quant_first()
-        gather_words(1, 6, 2, 3)
+        load_wb(1, 512, 256, placed("raw1_512", [P, 4, 256], F32, 6.25))
+        load_wb(1, 768, 256, placed("raw1_768", [P, 4, 256], F32, 10.25))
+        quant_wb(0, 0, 256)
+        quant_wb(1, 0, 256)
         deal_codes()
         sums_of = {}
         forward(0, (0, 1, 2, 3))
         forward(1, (0, 1))
-        forward(0, (4, 5, 6, 7))
+        forward(0, (4, 5))
         forward(1, (2, 3, 4, 5))
         for jt in range(6):
-            empty_forward(jt)
-        for b in range(2):
+            empty_forward(jt, (0, 256))
+        for b in range(3):
             sums_of[b] = backward(0, b)
-        forward(1, (6, 7))
         for jt in (6, 7):
-            empty_forward(jt)
+            forward(0, (jt,))
+            forward(1, (jt,))
+        for c0 in (0, 256):
+            for jt in (6, 7):
+                empty_forward(jt, (c0,))
 
         def load_wind(x):
             winds[x] = placed("wind%d" % x, [P, 4, 512], F32, (22.5, 30.5)[x])
@@ -431,7 +438,7 @@ def tile_list_minmod_neighbour_fluxes_kernel(
             load_plane(nc.sync, late["wxs"], wx_scales)
 
         def load_wx():
-            late["wx"] = placed("wx", [P, 2, N], I32, 17.5)
+            late["wx"] = placed("wx", [P, 2, N], I32, 17.75)
             nc.sync.dma_start(late["wx"][:], wx_words.rearrange("a p c i -> p a (c i)").bitcast(I32))
 
         before = {i: [] for i in range(-4, 25)}
@@ -440,7 +447,7 @@ def tile_list_minmod_neighbour_fluxes_kernel(
         early = {i: [] for i in before}
         for a in range(2):
             before[a - 1].append(lambda a=a: cast_narrow(a, 256))
-            after[Q256_AT[a] + 1].append(lambda a=a: quant_wb(a, 256, 256))
+            early[Q256_AT[a] + 1].append(lambda a=a: quant_wb(a, 256, 256))
             for half in range(2):
                 before[CAST512_AT[2 * a + half]].append(lambda a=a, half=half: cast_wide(a, half))
             after[Q512_AT[a] + 1].append(lambda a=a: quant_wb(a, 512, 512))
@@ -485,7 +492,7 @@ def tile_list_minmod_neighbour_fluxes_kernel(
                 upper(units[i - 1], sums_of[i - 1])
             for step in early[i]:
                 step()
-            for x in range(2, 16):
+            for x in range(3, 16):
                 if BACK_AT[x] == i:
                     sums_of[x] = slope("back", units[x]) if isinstance(units[x], int) else backward(*units[x])
             for step in last[i]:

@@ -19,19 +19,21 @@ ALU = mybir.AluOpType
 P = 128
 PASS = 512
 ORDER = (
-    "F0 F1 F2 F3 F4 F5 B0 B1 B2 F6 F7 B3 L0 L1 B4 B5 B6 B7 L2 L3 L4 L5 B8 B9 B10 B11 T0 T1 T2 T3"
+    "F0 F1 F2 F3 F4 F5 F6 F7 B0 B1 B2 B3 L0 L1 B4 B5 B6 B7 L2 L3 L4 L5 B8 B9 B10 B11 T0 T1 T2 T3"
     " B12 B13 B14 B15 L6 L7 X0_0 X0_1 - - - - X2_0 X2_1 X4_0 X4_1 X6_0 X6_1 X7_0 X7_1"
 )
+OPEN_FROM = 6
+WARM = 3
 EARLY = 4
 FL_HOLD = 2
-HEAD_BANKS = (0, 1, 2, 3, 4, 5, 6, 7, 0, 3, 4)
-RING = (1, 2, 5, 6, 7, 3, 4, 0)
+HEAD_BANKS = (0, 1, 2, 3, 4, 5, 6, 7, 0, 1, 2)
+RING = (3, 4, 5, 0, 1, 6, 7, 2)
 BACK_AT = (-3, -3, -1, -1, 2, 2, 2, 2, 7, 7, 7, 7, 9, 10, 11, 12)
-WIND_AT = {(2, 0): 14.5, (2, 1): 16.5, (4, 0): 18, (4, 1): 18, (6, 0): 18, (6, 1): 18}
+WIND_AT = {(2, 1): 14.5, (4, 0): 18, (4, 1): 18, (6, 0): 18, (6, 1): 18}
 FWD_AT = (0, 0, 3, 3, 3, 3, 8, 8)
 SPLIT0 = 1
 GROUPS = [(0, 1), (2, 3), (4, 5), (6, 7)]
-ON_POOL = [(0, 0), (0, 1)]
+ON_POOL = [(0, 0), (0, 1), (2, 0)]
 WFS_ON_POOL = 1
 MOVES_ON_ACT = 0
 Q256_AT = (1, 1)
@@ -69,11 +71,13 @@ def tile_list_minmod_neighbour_fluxes_kernel(
         nc.sync.dma_start(offsets[:], offs)
 
         win = placed("win", [P, T], U8, 30)
-        by_row = tab_scales.bitcast(I32).rearrange("a q c -> q a c")
-        for c in (0, 2):
-            nc.sync.dma_start(win[:].bitcast(I32)[c:P:4, :], by_row)
-        next_row = tab_scales.bitcast(I32).rearrange("a q c -> (a q) c")[1:17]
-        nc.sync.dma_start(win[:].bitcast(I32)[1:P:2, :], next_row.unsqueeze(1).to_broadcast([16, 4, T // 4]))
+        rows = tab_scales.bitcast(I32)
+        words = win[:].bitcast(I32)
+        nc.sync.dma_start(words[0:P:4, :], rows.rearrange("a q c -> q a c"))
+        nc.sync.dma_start(words[2:P:4, :], rows[0][0::2].unsqueeze(1).to_broadcast([8, 4, T // 4]))
+        flat = rows.rearrange("a q c -> (a q) c")
+        nc.sync.dma_start(words[1:P:4, :], flat[1:17].unsqueeze(1).to_broadcast([16, 2, T // 4]))
+        nc.sync.dma_start(words[3:P:4, :], flat[0:16].unsqueeze(1).to_broadcast([16, 2, T // 4]))
 
         tab = [placed("tab0", [P, T], I32, 14), placed("tab1", [P, T], I32, 75)]
 
@@ -114,16 +118,15 @@ def tile_list_minmod_neighbour_fluxes_kernel(
         load_tab(1)
 
         vs = [held("vs%d" % a, [P, S], U8) for a in range(2)]
-        nc.vector.memset(vs[1][:].bitcast(I32), 0)
+        for a in range(2):
+            nc.vector.memset(vs[a][:].bitcast(I32), 0)
 
-        gs = placed("gs", [P, S], U8, 45)
+        gs = placed("gs", [P, S], U8, 46)
         nc.vector.tensor_copy(gs[:], win[:].indirect(offsets[:]))
-        nc.vector.tensor_copy(vs[0][:].bitcast(I32), gs[:].bitcast(I32))
-        mover = nc.scalar if MOVES_ON_ACT else nc.sync
-        for a, r in [(1, 0), (1, 1), (1, 2), (1, 3), (0, 2), (0, 3)]:
-            first = 8 * r + 6 * a
-            mover.dma_start(vs[a][:].bitcast(I32)[r:P:32, :], gs[:].bitcast(I32)[first:P:32, :])
+        nc.sync.dma_start(vs[0][:].bitcast(I32)[0:112, :], gs[:].bitcast(I32)[14:126, :])
         load_wb(0, 0, 256, placed("raw00", [P, 4, 256], F32, 29))
+        for r in range(4):
+            nc.sync.dma_start(vs[1][:].bitcast(I32)[r:P:32, :], gs[:].bitcast(I32)[8 * r + 4 : P : 32, :])
 
         v = {}
 
@@ -201,7 +204,7 @@ def tile_list_minmod_neighbour_fluxes_kernel(
         def quant_wb(a, c0, width):
             name = "wbq%d_%d" % (a, c0)
             if c0 == 0:
-                wbq[a, c0] = held(name, [P, width], I32)
+                wbq[a, c0] = held(name, [P, width], I32) if a else placed(name, [P, width], I32, 10.25)
             else:
                 step = (Q256_AT if c0 == 256 else Q512_AT)[a] - 1
                 wbq[a, c0] = behind(step, a, name, [P, width], I32, width // 256)
@@ -222,7 +225,8 @@ def tile_list_minmod_neighbour_fluxes_kernel(
 
         def forward(a, jts):
             for jt in jts:
-                if a == 0:
+                first = jt not in fwd_banks
+                if first:
                     fwd_banks[jt] = bank_for("F%d" % jt, [P, 512])
                 nc.tensor.matmul_mx(
                     out=fwd_banks[jt][:],
@@ -230,8 +234,8 @@ def tile_list_minmod_neighbour_fluxes_kernel(
                     lhsT_scale=v_scales(a, jt),
                     rhs=wf[0][:, a, :].bitcast(E2M1),
                     rhs_scale=wfs[:, a, 0:PASS],
-                    start=(a == 0),
-                    stop=(a == 1),
+                    start=first,
+                    stop=not first,
                 )
 
         def empty_forward(jt, chunks):
@@ -263,11 +267,11 @@ def tile_list_minmod_neighbour_fluxes_kernel(
         h_late = [placed("hl%d" % b, [P, 2, 512], BF16, 48 + 8 * b) for b in range(4)]
 
         def deal_scales():
-            dealt["scales"] = placed("wfp", [P, 2, 4, 128], U8, 45.5)
+            dealt["scales"] = held("wfp", [P, 2, 4, 128], U8)
             nc.vector.tensor_copy(dealt["scales"][:], wfs[:, :, PASS:].rearrange("p a (m t) -> p a t m", t=4))
 
         def deal_codes():
-            dealt["codes"] = placed("wfd", [P, 2, 4, 128], U16, 43)
+            dealt["codes"] = placed("wfd", [P, 2, 4, 128], U16, 44)
             nc.vector.tensor_copy(dealt["codes"][:], wf[1][:].bitcast(U16).rearrange("p a (m t) -> p a t m", t=4))
 
         def slope(role, jt):
@@ -354,8 +358,8 @@ def tile_list_minmod_neighbour_fluxes_kernel(
             per_bank = 4 // groups
             for g in range(groups):
                 bank = bank_for("X%d_%d" % (jts[0], g), [P, per_bank, 128 * len(jts)])
-                order = (0, 1) if jts == (7,) else (1, 0)
-                for s in order:
+                passes = (0, 1) if jts[0] >= OPEN_FROM else (1, 0)
+                for s in passes:
                     for y in range(per_bank):
                         rows = slice(128 * (per_bank * g + y), 128 * (per_bank * g + y + 1))
                         nc.tensor.matmul_mx(
@@ -364,8 +368,8 @@ def tile_list_minmod_neighbour_fluxes_kernel(
                             lhsT_scale=late["wxs"][:, s, rows],
                             rhs=hq[s][:, cols].bitcast(E4M3),
                             rhs_scale=hs[s][:, cols],
-                            start=(s == order[0] and y == 0),
-                            stop=(s == order[1] and y == per_bank - 1),
+                            start=(s == passes[0] and y == 0),
+                            stop=(s == passes[1] and y == per_bank - 1),
                         )
                 faces[jts, g] = bank
 
@@ -400,30 +404,39 @@ def tile_list_minmod_neighbour_fluxes_kernel(
         load_wf(1, placed("wf1", [P, 2, H], U8, 15.75))
         load_wb(0, 256, 256, placed("raw0_256", [P, 4, 256], F32, 17.75))
         load_wb(1, 256, 256, placed("raw1_256", [P, 4, 256], F32, 21.75))
+        deal_scales()
         gather_words(1, 0, 2)
-        gather_words(1, 2, 6)
+        gather_words(1, 2, 4)
         cast_narrow(0, 0)
         load_wb(0, 512, 256, placed("raw0_512", [P, 4, 256], F32, 26.5))
         load_wb(0, 768, 256, placed("raw0_768", [P, 4, 256], F32, 30.5))
-        deal_scales()
         cast_narrow(1, 0)
         load_wb(1, 512, 256, placed("raw1_512", [P, 4, 256], F32, 6.25))
-        load_wb(1, 768, 256, placed("raw1_768", [P, 4, 256], F32, 10.25))
+        load_wb(1, 768, 256, placed("raw1_768", [P, 4, 256], F32, 11.25))
         quant_wb(0, 0, 256)
         quant_wb(1, 0, 256)
+        gather_words(1, 6, 2, 43)
         deal_codes()
         sums_of = {}
-        forward(0, (0, 1, 2, 3))
-        forward(1, (0, 1))
-        forward(0, (4, 5))
-        forward(1, (2, 3, 4, 5))
+        idle = psum.tile([P, 512], F32, name="idle", tag="bank7")
+        for x in range(WARM):
+            nc.tensor.matmul_mx(
+                out=idle[:],
+                lhsT=v_codes(0, x),
+                lhsT_scale=wfs[:, 0, 0:128],
+                rhs=wf[0][:, 0, :].bitcast(E2M1),
+                rhs_scale=wfs[:, 0, 0:PASS],
+                start=True,
+                stop=True,
+            )
+        forward(0, range(8))
+        forward(1, (0, 1, 2, 3, 4, 5))
         for jt in range(6):
             empty_forward(jt, (0, 256))
         for b in range(3):
             sums_of[b] = backward(0, b)
-        for jt in (6, 7):
-            forward(0, (jt,))
-            forward(1, (jt,))
+        forward(1, (6, 7))
+        cast_narrow(1, 256)
         for c0 in (0, 256):
             for jt in (6, 7):
                 empty_forward(jt, (c0,))
@@ -446,7 +459,6 @@ def tile_list_minmod_neighbour_fluxes_kernel(
         last = {i: [] for i in before}
         early = {i: [] for i in before}
         for a in range(2):
-            before[a - 1].append(lambda a=a: cast_narrow(a, 256))
             early[Q256_AT[a] + 1].append(lambda a=a: quant_wb(a, 256, 256))
             for half in range(2):
                 before[CAST512_AT[2 * a + half]].append(lambda a=a, half=half: cast_wide(a, half))
@@ -455,6 +467,7 @@ def tile_list_minmod_neighbour_fluxes_kernel(
             last[FWD_AT[jt]].append(lambda jt=jt: forward_late(jt))
         for jt in range(8):
             last[COPY_AT[jt]].append(lambda jt=jt: empty_late(jt))
+        before[-1].append(lambda: cast_narrow(0, 256))
         before[1].append(load_wx)
         before[5].append(make_ident)
         before[5].append(load_wxs)

@@ -18,32 +18,50 @@ ALU = mybir.AluOpType
 
 P = 128
 PASS = 512
-ORDER = (
-    "F0 F1 F2 F3 F4 F5 F6 F7 B0 B1 B2 B3 L0 L1 B4 B5 B6 B7 L2 L3 L4 L5 B8 B9 B10 B11 T0 T1 T2 T3"
-    " B12 B13 B14 B15 L6 L7 X0_0 X0_1 - - - - X2_0 X2_1 X4_0 X4_1 X6_0 X6_1 X7_0 X7_1"
-)
-OPEN_FROM = 6
+PART = 256
+SHIFT = 14
 WARM = 3
-EARLY = 4
-FL_HOLD = 2
-HEAD_BANKS = (0, 1, 2, 3, 4, 5, 6, 7, 0, 1, 2)
-RING = (3, 4, 5, 0, 1, 6, 7, 2)
-BACK_AT = (-3, -3, -1, -1, 2, 2, 2, 2, 7, 7, 7, 7, 9, 10, 11, 12)
-WIND_AT = {(2, 1): 14.5, (4, 0): 18, (4, 1): 18, (6, 0): 18, (6, 1): 18}
-FWD_AT = (0, 0, 3, 3, 3, 3, 8, 8)
-SPLIT0 = 1
-GROUPS = [(0, 1), (2, 3), (4, 5), (6, 7)]
-ON_POOL = [(0, 0), (0, 1), (2, 0)]
-WFS_ON_POOL = 1
-MOVES_ON_ACT = 0
-Q256_AT = (1, 1)
-Q512_AT = (6, 6)
-CAST512_AT = (2, 2, 3, 4)
-CAST_HOLD = (1, 1)
-WIDE_ON_POOL = [(0, 1), (1, 0)]
-COPY_AT = (2, 2, 3, 3, 5, 5, 8, 8)
-TURN_AT = (6, 8)
-QE_AT = (11, 13)
+
+SITE = {
+    "blank": 74,
+    "wf0": 73,
+    "tab1": 75,
+    "win": 30,
+    "raw0_0": 29,
+    "tab0": 14,
+    "raw1_0": 10.125,
+    "wf1": 15.75,
+    "raw0_256": 17.75,
+    "raw1_256": 21.75,
+    "raw0_512": 26.5,
+    "raw0_768": 30.5,
+    "raw1_512": 6.25,
+    "raw1_768": 11.25,
+    "wbq0_0": 10.25,
+    "grp0_0": 43,
+    "v1_6": 43,
+    "dealt_codes": 44,
+    "grp1_0": 41,
+    "grp1_256": 39.5,
+    "ident": 16,
+    "wx": 17.75,
+    "wind0": 22.5,
+    "wind1": 30.5,
+    "wxs": 8,
+    "f0": 88,
+    "wbq0_256": 88,
+    "wbq1_256": 89,
+    "f1": 97,
+    "grp0_512": 98,
+    "grp1_512": 94,
+    "f2": 106,
+    "f8_f9": 107,
+    "f5": 114,
+    "wbq0_512": 113,
+    "wbq1_512": 115,
+    "h_late1": 56,
+    "res_pool": 57,
+}
 
 
 def tile_list_minmod_neighbour_fluxes_kernel(
@@ -54,459 +72,396 @@ def tile_list_minmod_neighbour_fluxes_kernel(
         keep = ctx.enter_context(tc.tile_pool(name="keep", bufs=1))
         shared = ctx.enter_context(tc.tile_pool(name="shared", bufs=1))
         psum = ctx.enter_context(tc.psum_pool(name="psum", bufs=1))
-        order = ORDER.split()
 
-        def bank_for(role, shape):
-            n = order.index(role)
-            number = HEAD_BANKS[n] if n < len(HEAD_BANKS) else RING[(n - len(HEAD_BANKS)) % 8]
-            return psum.tile(shape, F32, name=role, tag="bank%d" % number)
-
-        def held(name, shape, dtype):
+        def sbuf(name, shape, dtype):
+            if name in SITE:
+                return shared.tile(shape, dtype, name=name, align_bytes=64, offset=int(1024 * SITE[name]))
             return keep.tile(shape, dtype, name=name, tag=name, align_bytes=64)
 
-        def placed(name, shape, dtype, kib):
-            return shared.tile(shape, dtype, name=name, align_bytes=64, offset=int(1024 * kib))
+        def bank(name, shape, number):
+            return psum.tile(shape, F32, name=name, tag="bank%d" % number)
+
+        upper_banks = []
+
+        def next_upper_bank(name, shape):
+            upper_banks.append(name)
+            return bank(name, shape, 4 + (len(upper_banks) - 1) % 4)
+
+        raw, wf, tab, winds, wx = {}, {}, {}, {}, {}
+
+        def load_tab(a):
+            tab[a] = sbuf("tab%d" % a, [P, T], I32)
+            nc.sync.dma_start(tab[a][:], tab_words[a].rearrange("p t i -> p (t i)").bitcast(I32))
+
+        def load_wb(a, c0):
+            raw[a, c0] = sbuf("raw%d_%d" % (a, c0), [P, 4, PART], F32)
+            rows = wb[PASS * a : PASS * (a + 1), c0 : c0 + PART]
+            nc.sync.dma_start(raw[a, c0][:], rows.rearrange("(p i) c -> p i c", i=4))
+
+        def load_wf(s):
+            wf[s] = sbuf("wf%d" % s, [P, 2, H], U8)
+            words = wf_words.bitcast(I32)[:, :, 256 * s : 256 * (s + 1)]
+            nc.sync.dma_start(wf[s][:].bitcast(I32), words.rearrange("a p c -> p a c"))
+
+        def load_plane(plane, scales):
+            for r in range(4):
+                rows = scales.bitcast(I32)[:, r::4, :].rearrange("a d c -> d a c")
+                nc.sync.dma_start(plane[:].bitcast(I32)[r:P:32], rows)
+
+        def load_wx():
+            wx["codes"] = sbuf("wx", [P, 2, N], I32)
+            nc.sync.dma_start(wx["codes"][:], wx_words.rearrange("a p c i -> p a (c i)").bitcast(I32))
+
+        def load_wx_scales():
+            wx["scales"] = sbuf("wxs", [P, 2, N], U8)
+            nc.gpsimd.memset(wx["scales"][:].bitcast(I32), 0)
+            load_plane(wx["scales"], wx_scales)
+
+        def load_wind(x):
+            winds[x] = sbuf("wind%d" % x, [P, 4, 512], F32)
+            nc.sync.dma_start(winds[x][:], wind[:, 512 * x : 512 * (x + 1)].rearrange("(y p) j -> p y j", p=P))
 
         offsets = keep.tile([P, S // 16], U16, name="offsets")
         nc.sync.dma_start(offsets[:], offs)
 
-        win = placed("win", [P, T], U8, 30)
-        rows = tab_scales.bitcast(I32)
-        words = win[:].bitcast(I32)
-        nc.sync.dma_start(words[0:P:4, :], rows.rearrange("a q c -> q a c"))
-        nc.sync.dma_start(words[2:P:4, :], rows[0][0::2].unsqueeze(1).to_broadcast([8, 4, T // 4]))
-        flat = rows.rearrange("a q c -> (a q) c")
-        nc.sync.dma_start(words[1:P:4, :], flat[1:17].unsqueeze(1).to_broadcast([16, 2, T // 4]))
-        nc.sync.dma_start(words[3:P:4, :], flat[0:16].unsqueeze(1).to_broadcast([16, 2, T // 4]))
-
-        tab = [placed("tab0", [P, T], I32, 14), placed("tab1", [P, T], I32, 75)]
-
-        def load_tab(a):
-            nc.sync.dma_start(tab[a][:], tab_words[a].rearrange("p t i -> p (t i)").bitcast(I32))
-
+        win = sbuf("win", [P, T], U8)
+        win_words = win[:].bitcast(I32)
+        by_pass = tab_scales.bitcast(I32)
+        all_rows = by_pass.rearrange("a q c -> (a q) c")
+        nc.sync.dma_start(win_words[0:P:4, :], by_pass.rearrange("a q c -> q a c"))
+        nc.sync.dma_start(win_words[2:P:4, :], by_pass[0][0::2].unsqueeze(1).to_broadcast([8, 4, T // 4]))
+        nc.sync.dma_start(win_words[1:P:4, :], all_rows[1:17].unsqueeze(1).to_broadcast([16, 2, T // 4]))
+        nc.sync.dma_start(win_words[3:P:4, :], all_rows[0:16].unsqueeze(1).to_broadcast([16, 2, T // 4]))
         load_tab(0)
 
-        raw = {}
-
-        def load_wb(a, c0, width, into):
-            raw[a, c0] = into
-            nc.sync.dma_start(
-                into[:], wb[PASS * a : PASS * (a + 1), c0 : c0 + width].rearrange("(p i) c -> p i c", i=4)
-            )
-
-        wf = {}
-
-        def load_wf(s, into):
-            wf[s] = into
-            nc.sync.dma_start(
-                into[:].bitcast(I32),
-                wf_words.bitcast(I32)[:, :, 256 * s : 256 * (s + 1)].rearrange("a p c -> p a c"),
-            )
-
-        def load_plane(queue, plane, scales):
-            for r in range(4):
-                queue.dma_start(
-                    plane[:].bitcast(I32)[r:P:32], scales.bitcast(I32)[:, r::4, :].rearrange("a d c -> d a c")
-                )
-
-        blank = placed("blank", [P, H // 2], I32, 74)
+        blank = sbuf("blank", [P, H // 2], I32)
         nc.vector.memset(blank[:], 0)
-        wfs = held("wfs", [P, 2, H], U8)
+        wfs = sbuf("wfs", [P, 2, H], U8)
         nc.vector.tensor_copy(wfs[:].bitcast(I32).rearrange("p a c -> p (a c)"), blank[:])
-        load_plane(nc.sync, wfs, wf_scales)
-        load_wf(0, placed("wf0", [P, 2, H], U8, 73))
+        load_plane(wfs, wf_scales)
+        load_wf(0)
         load_tab(1)
 
-        vs = [held("vs%d" % a, [P, S], U8) for a in range(2)]
+        vs = [sbuf("vs%d" % a, [P, S], U8) for a in range(2)]
         for a in range(2):
             nc.vector.memset(vs[a][:].bitcast(I32), 0)
-
-        gs = placed("gs", [P, S], U8, 46)
-        nc.vector.tensor_copy(gs[:], win[:].indirect(offsets[:]))
-        nc.sync.dma_start(vs[0][:].bitcast(I32)[0:112, :], gs[:].bitcast(I32)[14:126, :])
-        load_wb(0, 0, 256, placed("raw00", [P, 4, 256], F32, 29))
+        picked_rows = sbuf("picked_rows", [P, S], U8)
+        nc.vector.tensor_copy(picked_rows[:], win[:].indirect(offsets[:]))
+        nc.sync.dma_start(vs[0][:].bitcast(I32)[0:100, :], picked_rows[:].bitcast(I32)[SHIFT : SHIFT + 100, :])
+        load_wb(0, 0)
         for r in range(4):
-            nc.sync.dma_start(vs[1][:].bitcast(I32)[r:P:32, :], gs[:].bitcast(I32)[8 * r + 4 : P : 32, :])
+            nc.sync.dma_start(vs[1][:].bitcast(I32)[r:P:32, :], picked_rows[:].bitcast(I32)[8 * r + 4 : P : 32, :])
 
         v = {}
 
-        def gather_words(a, first, count, kib=None):
-            name, shape = "v%d_%d" % (a, first), [P, 128 * count]
-            picked = held(name, shape, I32) if kib is None else placed(name, shape, I32, kib)
-            nc.vector.tensor_copy(
-                picked[:].bitcast(U32), tab[a][:].bitcast(U32).indirect(offsets[:, 8 * first : 8 * (first + count)])
-            )
+        def gather_words(a, first, count):
+            picked = sbuf("v%d_%d" % (a, first), [P, P * count], I32)
+            window = tab[a][:].bitcast(U32).indirect(offsets[:, 8 * first : 8 * (first + count)])
+            nc.vector.tensor_copy(picked[:].bitcast(U32), window)
             for x in range(count):
-                v[a, first + x] = picked[:, 128 * x : 128 * (x + 1)]
-
-        def v_codes(a, jt):
-            return v[a, jt].bitcast(E4M3)
+                v[a, first + x] = picked[:, P * x : P * (x + 1)].bitcast(E4M3)
 
         def v_scales(a, jt):
-            return vs[a][:, 128 * jt : 128 * (jt + 1)]
+            return vs[a][:, P * jt : P * (jt + 1)]
 
         grouped, wbq, wbs = {}, {}, {}
 
-        def slot(step):
-            return 88 + 9 * step
-
-        def behind(step, side, name, shape, dtype, kib):
-            return placed(name, shape, dtype, slot(step) + 1 if side else slot(step) + 1 - kib)
-
-        def cast_narrow(a, c0):
-            name = "grp%d_%d" % (a, c0)
-            shape = [P, 1024]
-            if (a, c0) == (0, 256):
-                grouped[a, c0] = held(name, shape, BF16)
-            elif c0 == 256:
-                grouped[a, c0] = placed(name, shape, BF16, 39.5)
+        def cast(engine, dst, src):
+            if engine == "gpsimd":
+                for u in range(2):
+                    into = dst[:, :, :, u].rearrange("p m i e -> p m e i")
+                    values = src[:, :, :, u].rearrange("p m i e -> p m e i")
+                    nc.gpsimd.tensor_scalar(into, values, 1.0, 0.0, ALU.mult, ALU.add)
+            elif engine == "vector":
+                nc.vector.tensor_copy(dst, src)
             else:
-                grouped[a, c0] = placed(name, shape, BF16, (43, 41)[a])
+                nc.scalar.copy(dst, src)
+
+        def cast_first_half(engine, a, c0):
+            grouped[a, c0] = sbuf("grp%d_%d" % (a, c0), [P, 4 * PART], BF16)
             dst = grouped[a, c0][:].rearrange("p (u m e i) -> p m i u e", u=2, e=2, i=4)
-            src = raw[a, c0][:].rearrange("p i (m u e) -> p m i u e", u=2, e=2)
-            if (a, c0) == (1, 256):
-                nc.scalar.copy(dst, src)
-            elif c0 == 256:
-                for u in range(2):
-                    nc.gpsimd.tensor_scalar(
-                        dst[:, :, :, u, :].rearrange("p m i e -> p m e i"),
-                        src[:, :, :, u, :].rearrange("p m i e -> p m e i"),
-                        1.0,
-                        0.0,
-                        ALU.mult,
-                        ALU.add,
-                    )
-            else:
-                (nc.vector.tensor_copy if a == 1 else nc.scalar.copy)(dst, src)
+            cast(engine, dst, raw[a, c0][:].rearrange("p i (m u e) -> p m i u e", u=2, e=2))
 
-        def cast_wide(a, half):
-            if half == 0:
-                name = "grp%d_512" % a
-                grouped[a, 512] = behind(CAST_HOLD[a], 1 - a, name, [P, 2048], BF16, 4)
-            dst = grouped[a, 512][:].rearrange("p (t m i) -> p m i t", t=4, i=4)[:, 64 * half : 64 * (half + 1)]
-            if (a, 768) in raw:
-                src = raw[a, 512 + 256 * half][:].rearrange("p i (m t) -> p m i t", t=4)
-            else:
-                src = raw[a, 512][:].rearrange("p i (m t) -> p m i t", t=4)[:, 64 * half : 64 * (half + 1)]
-            if (a, half) in WIDE_ON_POOL:
-                for u in range(2):
-                    nc.gpsimd.tensor_scalar(
-                        dst[:, :, :, 2 * u : 2 * u + 2].rearrange("p m i e -> p m e i"),
-                        src[:, :, :, 2 * u : 2 * u + 2].rearrange("p m i e -> p m e i"),
-                        1.0,
-                        0.0,
-                        ALU.mult,
-                        ALU.add,
-                    )
-            else:
-                nc.scalar.copy(dst, src)
+        def cast_second_half(engine, a, x):
+            if x == 0:
+                grouped[a, PASS] = sbuf("grp%d_%d" % (a, PASS), [P, 4 * PASS], BF16)
+            dst = grouped[a, PASS][:].rearrange("p (u e m i) -> p m i u e", u=2, e=2, i=4)[:, 64 * x : 64 * (x + 1)]
+            cast(engine, dst, raw[a, PASS + PART * x][:].rearrange("p i (m u e) -> p m i u e", u=2, e=2))
 
-        def quant_wb(a, c0, width):
-            name = "wbq%d_%d" % (a, c0)
-            if c0 == 0:
-                wbq[a, c0] = held(name, [P, width], I32) if a else placed(name, [P, width], I32, 10.25)
-            else:
-                step = (Q256_AT if c0 == 256 else Q512_AT)[a] - 1
-                wbq[a, c0] = behind(step, a, name, [P, width], I32, width // 256)
-            wbs[a, c0] = held("wbs%d_%d" % (a, c0), [P, width], U8)
-            nc.vector.quantize_mx(out=wbq[a, c0][:].bitcast(E4M3), scales=wbs[a, c0][:], in_=grouped[a, c0][:])
+        def quantise_wb(c0, width):
+            for a in range(2):
+                wbq[a, c0] = sbuf("wbq%d_%d" % (a, c0), [P, width], I32)
+                wbs[a, c0] = sbuf("wbs%d_%d" % (a, c0), [P, width], U8)
+                nc.vector.quantize_mx(out=wbq[a, c0][:].bitcast(E4M3), scales=wbs[a, c0][:], in_=grouped[a, c0][:])
 
-        units = [(0, b) for b in range(4)] + [(256, b) for b in range(EARLY)]
-        rest = [(256, b) for b in range(EARLY, 4)]
-        units = units + [0, 1, 2, 3][: 2 * EARLY] + rest + list(range(min(4, 2 * EARLY), 8))
-        f_sb = {}
-        for step, unit in enumerate(units):
-            if not isinstance(unit, int):
-                name = "f%d_%d" % unit
-                f_sb[unit] = placed(name, [P, 4, 128], F32, slot(step)) if step < 8 else held(name, [P, 4, 128], F32)
-        h_sb = [held("h%d" % b, [P, 4, 256], BF16) for b in range(4)]
-
-        fwd_banks = {}
-
-        def forward(a, jts):
-            for jt in jts:
-                first = jt not in fwd_banks
-                if first:
-                    fwd_banks[jt] = bank_for("F%d" % jt, [P, 512])
-                nc.tensor.matmul_mx(
-                    out=fwd_banks[jt][:],
-                    lhsT=v_codes(a, jt),
-                    lhsT_scale=v_scales(a, jt),
-                    rhs=wf[0][:, a, :].bitcast(E2M1),
-                    rhs_scale=wfs[:, a, 0:PASS],
-                    start=first,
-                    stop=not first,
-                )
-
-        def empty_forward(jt, chunks):
-            for c0 in chunks:
-                nc.scalar.copy(
-                    f_sb[c0, jt // 2][:, 2 * (jt % 2) : 2 * (jt % 2) + 2, :].rearrange("p u (m e) -> p u m e", e=2),
-                    fwd_banks[jt][:, c0 : c0 + 256].rearrange("p (m u e) -> p u m e", u=2, e=2),
-                )
-
-        def backward_pass(bank, a, c0, b):
-            for x in range(2):
-                nc.tensor.matmul_mx(
-                    out=bank[:, 256 * x : 256 * (x + 1)],
-                    lhsT=v_codes(a, 2 * b + x),
-                    lhsT_scale=v_scales(a, 2 * b + x),
-                    rhs=wbq[a, c0][:].bitcast(E4M3),
-                    rhs_scale=wbs[a, c0][:],
-                    start=(a == 0 and x == 0),
-                    stop=(a == 1 and x == 1),
-                )
-            return bank[:].rearrange("p (x c) -> p x c", c=128)
-
-        def backward(c0, b):
-            bank = bank_for("B%d" % units.index((c0, b)), [P, 512])
-            backward_pass(bank, 0, c0, b)
-            return backward_pass(bank, 1, c0, b)
-
-        dealt, f_late = {}, {}
-        h_late = [placed("hl%d" % b, [P, 2, 512], BF16, 48 + 8 * b) for b in range(4)]
+        dealt = {}
 
         def deal_scales():
-            dealt["scales"] = held("wfp", [P, 2, 4, 128], U8)
+            dealt["scales"] = sbuf("dealt_scales", [P, 2, 4, P], U8)
             nc.vector.tensor_copy(dealt["scales"][:], wfs[:, :, PASS:].rearrange("p a (m t) -> p a t m", t=4))
 
         def deal_codes():
-            dealt["codes"] = placed("wfd", [P, 2, 4, 128], U16, 44)
+            dealt["codes"] = sbuf("dealt_codes", [P, 2, 4, P], U16)
             nc.vector.tensor_copy(dealt["codes"][:], wf[1][:].bitcast(U16).rearrange("p a (m t) -> p a t m", t=4))
 
-        def slope(role, jt):
-            bank = bank_for("B%d" % units.index(jt) if role == "back" else "L%d" % jt, [P, 4, 128])
+        f = {unit: sbuf("f%d" % unit, [P, 4, P], F32)[:] for unit in range(8)}
+        h_early = [sbuf("h_early%d" % b, [P, 4, 256], BF16) for b in range(4)]
+        h_late = [sbuf("h_late%d" % b, [P, 2, PASS], BF16) for b in range(4)]
+        fwd, back = {}, {}
+
+        def fwd_first_half(a, tiles):
+            for jt in tiles:
+                if a == 0:
+                    fwd[jt] = bank("fwd%d" % jt, [P, PASS], jt)
+                nc.tensor.matmul_mx(
+                    out=fwd[jt][:],
+                    lhsT=v[a, jt],
+                    lhsT_scale=v_scales(a, jt),
+                    rhs=wf[0][:, a, :].bitcast(E2M1),
+                    rhs_scale=wfs[:, a, 0:PASS],
+                    start=(a == 0),
+                    stop=(a == 1),
+                )
+
+        def empty_first_half(jt, part):
+            dst = f[4 * part + jt // 2][:, 2 * (jt % 2) : 2 * (jt % 2) + 2, :].rearrange("p u (m e) -> p u m e", e=2)
+            src = fwd[jt][:, PART * part : PART * (part + 1)].rearrange("p (m u e) -> p u m e", u=2, e=2)
+            nc.scalar.copy(dst, src)
+
+        def second_half_sums(sums, jt, weights):
             for a in range(2):
                 for t in range(4):
-                    cols = slice(128 * t, 128 * (t + 1))
-                    if role == "back":
-                        codes, scales = wbq[a, 512][:, cols].bitcast(E4M3), wbs[a, 512][:, cols]
-                    else:
-                        codes, scales = dealt["codes"][:, a, t, :].bitcast(E2M1), dealt["scales"][:, a, t, :]
+                    codes, scales = weights(a, t)
                     nc.tensor.matmul_mx(
-                        out=bank[:, t, :],
+                        out=sums[:, t, :],
                         lhsT=codes,
                         lhsT_scale=scales,
-                        rhs=v_codes(a, jt),
+                        rhs=v[a, jt],
                         rhs_scale=v_scales(a, jt),
                         start=(a == 0 and t == 0),
                         stop=(a == 1 and t == 3),
                     )
-            return bank[:].rearrange("p t c -> p c t")
+            return sums[:].rearrange("p t c -> p c t")
 
-        def forward_late(jt):
-            fwd_banks[8 + jt] = slope("fwd", jt)
+        def wf_run(a, t):
+            return dealt["codes"][:, a, t, :].bitcast(E2M1), dealt["scales"][:, a, t, :]
 
-        def empty_late(jt):
-            if jt == 0:
-                f_late["first"] = behind(FL_HOLD, 1, "fl_first", [P, 2, 128, 4], F32, 4)
-            f_late[jt] = f_late["first"][:, jt] if jt < 2 else held("fl%d" % jt, [P, 128, 4], F32)
-            nc.scalar.copy(f_late[jt][:], fwd_banks[8 + jt])
+        def wb_run(a, t):
+            return wbq[a, PASS][:, P * t : P * (t + 1)].bitcast(E4M3), wbs[a, PASS][:, P * t : P * (t + 1)]
 
-        def places(unit):
-            if isinstance(unit, int):
-                return f_late[unit][:], h_late[unit // 2][:, unit % 2, :].rearrange("p (c t) -> p c t", t=4)
-            c0, b = unit
-            cols = slice(c0 // 2, c0 // 2 + 128)
-            return f_sb[unit][:], h_sb[b][:, :, cols]
+        def fwd_second_half(units):
+            for unit in units:
+                fwd[unit] = second_half_sums(next_upper_bank("fwd%d" % unit, [P, 4, P]), unit - 8, wf_run)
 
-        def lower(unit, back):
-            f = places(unit)[0]
-            nc.vector.scalar_tensor_tensor(out=f, in0=back, scalar=0.0, in1=f, op0=ALU.min, op1=ALU.max)
+        def empty_second_half(units):
+            for unit in units:
+                if unit not in f:
+                    f[unit] = sbuf("f%d" % unit, [P, P, 4], F32)[:]
+                nc.scalar.copy(f[unit], fwd[unit])
 
-        def upper(unit, back):
-            f, h = places(unit)
-            nc.vector.scalar_tensor_tensor(out=h, in0=back, scalar=0.0, in1=f, op0=ALU.max, op1=ALU.min)
+        def back_sums(units):
+            for unit in units:
+                if unit >= 8:
+                    back[unit] = second_half_sums(bank("back%d" % unit, [P, 4, P], unit % 4), unit - 8, wb_run)
+                    continue
+                sums = bank("back%d" % unit, [P, 2 * PART], unit % 4)
+                c0, b = PART * (unit // 4), unit % 4
+                for a in range(2):
+                    for x in range(2):
+                        nc.tensor.matmul_mx(
+                            out=sums[:, PART * x : PART * (x + 1)],
+                            lhsT=v[a, 2 * b + x],
+                            lhsT_scale=v_scales(a, 2 * b + x),
+                            rhs=wbq[a, c0][:].bitcast(E4M3),
+                            rhs_scale=wbs[a, c0][:],
+                            start=(a == 0 and x == 0),
+                            stop=(a == 1 and x == 1),
+                        )
+                back[unit] = sums[:].rearrange("p (x c) -> p x c", c=P)
 
-        late = {}
-
-        def make_ident():
-            late["ident"] = behind(3, 0, "ident", [P, P], F32, 0.5)
-            make_identity(nc, late["ident"][:])
-
-        h_t = [held("ht%d" % x, [P, 2048], BF16) for x in range(2)]
-        hq = [held("hq%d" % s, [P, S], I32) for s in range(2)]
-        hs = [held("hs%d" % s, [P, S], U8) for s in range(2)]
-
-        def cells(jts):
-            return slice(128 * jts[0], 128 * (jts[-1] + 1))
-
-        def turn(b):
-            bank = bank_for("T%d" % b, [P, 4, P])
-            for y in (1, 0):
-                for u in range(2):
-                    nc.tensor.transpose(bank[:, 2 * y + u, :], h_sb[b][:, 2 * y + u, :].bitcast(F32), late["ident"][:])
-            nc.scalar.copy(
-                h_t[b // 2][:, 1024 * (b % 2) : 1024 * (b % 2 + 1)].bitcast(F32).rearrange("p (y j u) -> p y j u", y=2, u=2),
-                bank[:].rearrange("p (y u) j -> p y j u", u=2),
+        def lower(unit):
+            nc.vector.scalar_tensor_tensor(
+                out=f[unit], in0=back[unit], scalar=0.0, in1=f[unit], op0=ALU.min, op1=ALU.max
             )
 
-        def quant_early(x):
-            cols = slice(512 * x, 512 * (x + 1))
-            nc.vector.quantize_mx(out=hq[0][:, cols].bitcast(E4M3), scales=hs[0][:, cols], in_=h_t[x][:])
+        def upper(unit):
+            if unit >= 8:
+                h = h_late[(unit - 8) // 2][:, unit % 2, :].rearrange("p (c t) -> p c t", t=4)
+            else:
+                h = h_early[unit % 4][:, :, P * (unit // 4) : P * (unit // 4 + 1)]
+            nc.vector.scalar_tensor_tensor(out=h, in0=back[unit], scalar=0.0, in1=f[unit], op0=ALU.max, op1=ALU.min)
 
-        def quant_late(jts):
-            cols = cells(jts)
-            first = jts[0] % 2
-            values = h_late[jts[0] // 2][:, first : first + len(jts), :].rearrange("p x c -> p (x c)")
-            nc.vector.quantize_mx(out=hq[1][:, cols].bitcast(E4M3), scales=hs[1][:, cols], in_=values)
+        def limit(unit):
+            lower(unit)
+            upper(unit - 1)
 
+        h_turned = [sbuf("h_turned%d" % x, [P, 2048], BF16) for x in range(2)]
+        hq = [sbuf("hq%d" % s, [P, S], I32) for s in range(2)]
+        hs = [sbuf("hs%d" % s, [P, S], U8) for s in range(2)]
         faces = {}
 
-        def face(jts, groups):
-            cols = cells(jts)
-            per_bank = 4 // groups
-            for g in range(groups):
-                bank = bank_for("X%d_%d" % (jts[0], g), [P, per_bank, 128 * len(jts)])
-                passes = (0, 1) if jts[0] >= OPEN_FROM else (1, 0)
-                for s in passes:
-                    for y in range(per_bank):
-                        rows = slice(128 * (per_bank * g + y), 128 * (per_bank * g + y + 1))
+        def cells(b):
+            return slice(256 * b, 256 * (b + 1))
+
+        def turn(pairs):
+            for b in pairs:
+                turned = next_upper_bank("turned%d" % b, [P, 4, P])
+                for y in (1, 0):
+                    for u in range(2):
+                        nc.tensor.transpose(turned[:, 2 * y + u, :], h_early[b][:, 2 * y + u, :].bitcast(F32), ident[:])
+                dst = h_turned[b // 2][:, 1024 * (b % 2) : 1024 * (b % 2 + 1)].bitcast(F32)
+                nc.scalar.copy(
+                    dst.rearrange("p (y j u) -> p y j u", y=2, u=2), turned[:].rearrange("p (y u) j -> p y j u", u=2)
+                )
+
+        def quantise_first_half(x):
+            cols = slice(512 * x, 512 * (x + 1))
+            nc.vector.quantize_mx(out=hq[0][:, cols].bitcast(E4M3), scales=hs[0][:, cols], in_=h_turned[x][:])
+
+        def quantise_second_half(b):
+            values = h_late[b][:].rearrange("p x c -> p (x c)")
+            nc.vector.quantize_mx(out=hq[1][:, cells(b)].bitcast(E4M3), scales=hs[1][:, cells(b)], in_=values)
+
+        def face_sums(b, halves):
+            for g in range(2):
+                faces[b, g] = next_upper_bank("face%d_%d" % (b, g), [P, 2, 256])
+                for s in halves:
+                    for y in range(2):
+                        rows = slice(P * (2 * g + y), P * (2 * g + y + 1))
                         nc.tensor.matmul_mx(
-                            out=bank[:, y, :],
-                            lhsT=late["wx"][:, s, rows].bitcast(E4M3),
-                            lhsT_scale=late["wxs"][:, s, rows],
-                            rhs=hq[s][:, cols].bitcast(E4M3),
-                            rhs_scale=hs[s][:, cols],
-                            start=(s == passes[0] and y == 0),
-                            stop=(s == passes[1] and y == per_bank - 1),
+                            out=faces[b, g][:, y, :],
+                            lhsT=wx["codes"][:, s, rows].bitcast(E4M3),
+                            lhsT_scale=wx["scales"][:, s, rows],
+                            rhs=hq[s][:, cells(b)].bitcast(E4M3),
+                            rhs_scale=hs[s][:, cells(b)],
+                            start=(s == halves[0] and y == 0),
+                            stop=(s == halves[1] and y == 1),
                         )
-                faces[jts, g] = bank
 
-        winds = {}
+        def flux(b, g):
+            res = sbuf("res%d_%d" % (b, g), [P, 2, 256], F32)
+            factor = winds[b // 2][:, 2 * g : 2 * g + 2, cells(b % 2)]
+            nc.vector.tensor_tensor(res[:], faces[b, g][:], factor, ALU.mult)
+            nc.sync.dma_start(out[256 * g : 256 * (g + 1), cells(b)].rearrange("(y p) j -> p y j", p=P), res[:])
 
-        def store(jts, first, count, res):
-            rows = slice(128 * first, 128 * (first + count))
-            nc.sync.dma_start(out[rows, cells(jts)].rearrange("(y p) j -> p y j", p=P), res[:])
-
-        def factor(jts, first, count):
-            inside = 128 * (jts[0] % 4)
-            return winds[jts[0] // 4][:, first : first + count, inside : inside + 128 * len(jts)]
-
-        def flux(jts, groups, g):
-            per_bank = 4 // groups
-            res = held("res%d_%d" % (jts[0], g), [P, per_bank, 128 * len(jts)], F32)
-            nc.vector.tensor_tensor(res[:], faces[jts, g][:], factor(jts, per_bank * g, per_bank), ALU.mult)
-            store(jts, per_bank * g, per_bank, res)
-
-        def flux_on_pool(jts, which):
-            count = 2 * len(which)
-            sums = held("sums%d" % jts[0], [P, count, 256], F32)
-            for x, g in enumerate(which):
-                nc.scalar.copy(sums[:, 2 * x : 2 * x + 2, :], faces[jts, g][:])
-            res = placed("res%d_p" % jts[0], [P, count, 256], F32, 48 + 8 * (jts[0] // 2 + 1) + 1)
-            nc.gpsimd.tensor_tensor(res[:], sums[:], factor(jts, 2 * which[0], count), ALU.mult)
-            store(jts, 2 * which[0], count, res)
+        def first_flux_on_gpsimd():
+            sums = sbuf("face_sums", [P, 4, 256], F32)
+            for g in range(2):
+                nc.scalar.copy(sums[:, 2 * g : 2 * g + 2, :], faces[0, g][:])
+            res = sbuf("res_pool", [P, 4, 256], F32)
+            nc.gpsimd.tensor_tensor(res[:], sums[:], winds[0][:, :, cells(0)], ALU.mult)
+            nc.sync.dma_start(out[:, cells(0)].rearrange("(y p) j -> p y j", p=P), res[:])
 
         gather_words(0, 0, 4)
         gather_words(0, 4, 4)
-        load_wb(1, 0, 256, placed("raw10", [P, 4, 256], F32, 10.125))
-        load_wf(1, placed("wf1", [P, 2, H], U8, 15.75))
-        load_wb(0, 256, 256, placed("raw0_256", [P, 4, 256], F32, 17.75))
-        load_wb(1, 256, 256, placed("raw1_256", [P, 4, 256], F32, 21.75))
+        load_wb(1, 0)
+        load_wf(1)
+        load_wb(0, PART)
+        load_wb(1, PART)
         deal_scales()
         gather_words(1, 0, 2)
         gather_words(1, 2, 4)
-        cast_narrow(0, 0)
-        load_wb(0, 512, 256, placed("raw0_512", [P, 4, 256], F32, 26.5))
-        load_wb(0, 768, 256, placed("raw0_768", [P, 4, 256], F32, 30.5))
-        cast_narrow(1, 0)
-        load_wb(1, 512, 256, placed("raw1_512", [P, 4, 256], F32, 6.25))
-        load_wb(1, 768, 256, placed("raw1_768", [P, 4, 256], F32, 11.25))
-        quant_wb(0, 0, 256)
-        quant_wb(1, 0, 256)
-        gather_words(1, 6, 2, 43)
+        cast_first_half("scalar", 0, 0)
+        load_wb(0, PASS)
+        load_wb(0, PASS + PART)
+        cast_first_half("vector", 1, 0)
+        load_wb(1, PASS)
+        load_wb(1, PASS + PART)
+        quantise_wb(0, PART)
+        gather_words(1, 6, 2)
         deal_codes()
-        sums_of = {}
-        idle = psum.tile([P, 512], F32, name="idle", tag="bank7")
-        for x in range(WARM):
+
+        unread = bank("unread", [P, PASS], 7)
+        for jt in range(WARM):
             nc.tensor.matmul_mx(
-                out=idle[:],
-                lhsT=v_codes(0, x),
-                lhsT_scale=wfs[:, 0, 0:128],
+                out=unread[:],
+                lhsT=v[0, jt],
+                lhsT_scale=wfs[:, 0, 0:P],
                 rhs=wf[0][:, 0, :].bitcast(E2M1),
                 rhs_scale=wfs[:, 0, 0:PASS],
                 start=True,
                 stop=True,
             )
-        forward(0, range(8))
-        forward(1, (0, 1, 2, 3, 4, 5))
+
+        fwd_first_half(0, range(8))
+        fwd_first_half(1, range(6))
         for jt in range(6):
-            empty_forward(jt, (0, 256))
-        for b in range(3):
-            sums_of[b] = backward(0, b)
-        forward(1, (6, 7))
-        cast_narrow(1, 256)
-        for c0 in (0, 256):
+            for part in range(2):
+                empty_first_half(jt, part)
+        back_sums(range(3))
+        fwd_first_half(1, (6, 7))
+        cast_first_half("scalar", 1, PART)
+        for part in range(2):
             for jt in (6, 7):
-                empty_forward(jt, (c0,))
+                empty_first_half(jt, part)
+        cast_first_half("gpsimd", 0, PART)
+        back_sums([3])
+        ident = sbuf("ident", [P, P], F32)
+        make_identity(nc, ident[:])
 
-        def load_wind(x):
-            winds[x] = placed("wind%d" % x, [P, 4, 512], F32, (22.5, 30.5)[x])
-            nc.sync.dma_start(winds[x][:], wind[:, 512 * x : 512 * (x + 1)].rearrange("(m p) j -> p m j", p=P))
+        lower(0)
+        fwd_second_half((8, 9))
+        load_wx()
+        limit(1)
+        cast_second_half("scalar", 0, 0)
+        cast_second_half("gpsimd", 0, 1)
+        limit(2)
+        quantise_wb(PART, PART)
+        back_sums((4, 5))
+        f8_f9 = sbuf("f8_f9", [P, 2, P, 4], F32)
+        f[8], f[9] = f8_f9[:, 0], f8_f9[:, 1]
+        empty_second_half((8, 9))
+        cast_second_half("gpsimd", 1, 0)
+        limit(3)
+        back_sums([6])
+        load_wind(0)
+        load_wind(1)
+        limit(4)
+        back_sums([7])
+        fwd_second_half((10, 11, 12, 13))
+        empty_second_half((10, 11))
+        cast_second_half("scalar", 1, 1)
+        load_wx_scales()
+        limit(5)
+        empty_second_half((12, 13))
+        limit(6)
+        turn((0, 1))
+        lower(7)
+        quantise_wb(PASS, PASS)
+        upper(6)
+        back_sums((8, 9, 10))
 
-        def load_wxs():
-            late["wxs"] = placed("wxs", [P, 2, N], U8, 8)
-            nc.gpsimd.memset(late["wxs"][:].bitcast(I32), 0)
-            load_plane(nc.sync, late["wxs"], wx_scales)
-
-        def load_wx():
-            late["wx"] = placed("wx", [P, 2, N], I32, 17.75)
-            nc.sync.dma_start(late["wx"][:], wx_words.rearrange("a p c i -> p a (c i)").bitcast(I32))
-
-        before = {i: [] for i in range(-4, 25)}
-        after = {i: [] for i in before}
-        last = {i: [] for i in before}
-        early = {i: [] for i in before}
-        for a in range(2):
-            early[Q256_AT[a] + 1].append(lambda a=a: quant_wb(a, 256, 256))
-            for half in range(2):
-                before[CAST512_AT[2 * a + half]].append(lambda a=a, half=half: cast_wide(a, half))
-            after[Q512_AT[a] + 1].append(lambda a=a: quant_wb(a, 512, 512))
-        for jt in range(8):
-            last[FWD_AT[jt]].append(lambda jt=jt: forward_late(jt))
-        for jt in range(8):
-            last[COPY_AT[jt]].append(lambda jt=jt: empty_late(jt))
-        before[-1].append(lambda: cast_narrow(0, 256))
-        before[1].append(load_wx)
-        before[5].append(make_ident)
-        before[5].append(load_wxs)
-        before[4].append(lambda: load_wind(0))
-        before[4].append(lambda: load_wind(1))
-        turned = {}
-        for x in range(2):
-            early[TURN_AT[x]].append(lambda x=x: turn(2 * x))
-            early[TURN_AT[x]].append(lambda x=x: turn(2 * x + 1))
-            mid_at = QE_AT[x]
-            after[mid_at].append(lambda x=x: quant_early(x))
-            for jt in range(4 * x, 4 * x + 4):
-                turned[jt] = mid_at
-        for jts in GROUPS:
-            done = max(units.index(jts[-1]) + 2, turned[jts[-1]])
-            groups = 2 if jts == (7,) else len(jts)
-            after[done].append(lambda jts=jts: quant_late(jts))
-            after[done].append(lambda jts=jts, groups=groups: face(jts, groups))
-            pooled = [g for g in range(groups) if (jts[0], g) in ON_POOL]
-            if pooled:
-                after[done + 2].append(lambda jts=jts, pooled=pooled: flux_on_pool(jts, pooled))
-            for g in range(groups):
-                if g not in pooled:
-                    at = WIND_AT[jts[0], g]
-                    (after if at == int(at) else early)[int(at)].append(lambda jts=jts, groups=groups, g=g: flux(jts, groups, g))
-
-        for i in range(-4, 25):
-            for step in before[i]:
-                step()
-            if 0 <= i < 16:
-                lower(units[i], sums_of[i])
-            for step in after[i]:
-                step()
-            if 1 <= i <= 16:
-                upper(units[i - 1], sums_of[i - 1])
-            for step in early[i]:
-                step()
-            for x in range(3, 16):
-                if BACK_AT[x] == i:
-                    sums_of[x] = slope("back", units[x]) if isinstance(units[x], int) else backward(*units[x])
-            for step in last[i]:
-                step()
+        limit(8)
+        back_sums([11])
+        turn((2, 3))
+        fwd_second_half((14, 15))
+        empty_second_half((14, 15))
+        for unit in (9, 10):
+            limit(unit)
+            back_sums([unit + 3])
+        lower(11)
+        quantise_first_half(0)
+        quantise_second_half(0)
+        face_sums(0, (1, 0))
+        upper(10)
+        back_sums([14])
+        limit(12)
+        back_sums([15])
+        lower(13)
+        quantise_first_half(1)
+        first_flux_on_gpsimd()
+        quantise_second_half(1)
+        face_sums(1, (1, 0))
+        upper(12)
+        limit(14)
+        flux(1, 0)
+        limit(15)
+        quantise_second_half(2)
+        face_sums(2, (0, 1))
+        upper(15)
+        flux(1, 1)
+        quantise_second_half(3)
+        face_sums(3, (0, 1))
+        for b in (2, 3):
+            for g in range(2):
+                flux(b, g)

@@ -20,6 +20,8 @@ P = 128
 PASS = 512
 PART = 256
 SHIFT = 14
+BACK_RING = (6, 7, 2, 3)
+OTHER_RING = (4, 5, 0, 1)
 WARM = 3
 
 SITE = {
@@ -38,9 +40,8 @@ SITE = {
     "raw1_512": 6.25,
     "raw1_768": 11.25,
     "wbq0_0": 10.25,
-    "grp0_0": 43,
-    "v1_6": 43,
-    "dealt_codes": 44,
+    "grp0_0": 46,
+    "dealt_codes": 42.5,
     "grp1_0": 41,
     "grp1_256": 39.5,
     "ident": 16,
@@ -54,8 +55,8 @@ SITE = {
     "f1": 97,
     "grp0_512": 98,
     "grp1_512": 94,
-    "f2": 106,
-    "f8_f9": 107,
+    "f2": 46,
+    "f8_f9": 47,
     "f5": 114,
     "wbq0_512": 113,
     "wbq1_512": 115,
@@ -85,7 +86,7 @@ def tile_list_minmod_neighbour_fluxes_kernel(
 
         def next_upper_bank(name, shape):
             upper_banks.append(name)
-            return bank(name, shape, 4 + (len(upper_banks) - 1) % 4)
+            return bank(name, shape, OTHER_RING[(len(upper_banks) - 1) % 4])
 
         raw, wf, tab, winds, wx = {}, {}, {}, {}, {}
 
@@ -198,7 +199,7 @@ def tile_list_minmod_neighbour_fluxes_kernel(
 
         def deal_scales():
             dealt["scales"] = sbuf("dealt_scales", [P, 2, 4, P], U8)
-            nc.vector.tensor_copy(dealt["scales"][:], wfs[:, :, PASS:].rearrange("p a (m t) -> p a t m", t=4))
+            nc.gpsimd.tensor_copy(dealt["scales"][:], wfs[:, :, PASS:].rearrange("p a (m t) -> p a t m", t=4))
 
         def deal_codes():
             dealt["codes"] = sbuf("dealt_codes", [P, 2, 4, P], U16)
@@ -212,7 +213,8 @@ def tile_list_minmod_neighbour_fluxes_kernel(
         def fwd_first_half(a, tiles):
             for jt in tiles:
                 if a == 0:
-                    fwd[jt] = bank("fwd%d" % jt, [P, PASS], jt)
+                    name = "fwd%d" % jt
+                    fwd[jt] = bank(name, [P, PASS], jt) if jt < 6 else next_upper_bank(name, [P, PASS])
                 nc.tensor.matmul_mx(
                     out=fwd[jt][:],
                     lhsT=v[a, jt],
@@ -262,9 +264,9 @@ def tile_list_minmod_neighbour_fluxes_kernel(
         def back_sums(units):
             for unit in units:
                 if unit >= 8:
-                    back[unit] = second_half_sums(bank("back%d" % unit, [P, 4, P], unit % 4), unit - 8, wb_run)
+                    back[unit] = second_half_sums(bank("back%d" % unit, [P, 4, P], BACK_RING[unit % 4]), unit - 8, wb_run)
                     continue
-                sums = bank("back%d" % unit, [P, 2 * PART], unit % 4)
+                sums = bank("back%d" % unit, [P, 2 * PART], BACK_RING[unit % 4])
                 c0, b = PART * (unit // 4), unit % 4
                 for a in range(2):
                     for x in range(2):
@@ -344,6 +346,27 @@ def tile_list_minmod_neighbour_fluxes_kernel(
             nc.vector.tensor_tensor(res[:], faces[b, g][:], factor, ALU.mult)
             nc.sync.dma_start(out[256 * g : 256 * (g + 1), cells(b)].rearrange("(y p) j -> p y j", p=P), res[:])
 
+        def last_face_pass(s, cols, start, stop):
+            for y in range(4):
+                if start:
+                    name = "last_face%d" % y
+                    faces[y] = next_upper_bank(name, [P, 512]) if y < 2 else bank(name, [P, 512], BACK_RING[y - 2])
+                rows, these = slice(P * y, P * (y + 1)), slice(512 + cols.start, 512 + cols.stop)
+                nc.tensor.matmul_mx(
+                    out=faces[y][:, cols],
+                    lhsT=wx["codes"][:, s, rows].bitcast(E4M3),
+                    lhsT_scale=wx["scales"][:, s, rows],
+                    rhs=hq[s][:, these].bitcast(E4M3),
+                    rhs_scale=hs[s][:, these],
+                    start=start,
+                    stop=stop,
+                )
+
+        def last_flux(y):
+            res = sbuf("last_res%d" % y, [P, 512], F32)
+            nc.vector.tensor_tensor(res[:], faces[y][:], winds[1][:, y, :], ALU.mult)
+            nc.sync.dma_start(out[P * y : P * (y + 1), 512:], res[:])
+
         def first_flux_on_gpsimd():
             sums = sbuf("face_sums", [P, 4, 256], F32)
             for g in range(2):
@@ -360,7 +383,7 @@ def tile_list_minmod_neighbour_fluxes_kernel(
         load_wb(1, PART)
         deal_scales()
         gather_words(1, 0, 2)
-        gather_words(1, 2, 4)
+        gather_words(1, 2, 6)
         cast_first_half("scalar", 0, 0)
         load_wb(0, PASS)
         load_wb(0, PASS + PART)
@@ -368,7 +391,6 @@ def tile_list_minmod_neighbour_fluxes_kernel(
         load_wb(1, PASS)
         load_wb(1, PASS + PART)
         quantise_wb(0, PART)
-        gather_words(1, 6, 2)
         deal_codes()
 
         unread = bank("unread", [P, PASS], 7)
@@ -383,12 +405,13 @@ def tile_list_minmod_neighbour_fluxes_kernel(
                 stop=True,
             )
 
-        fwd_first_half(0, range(8))
+        fwd_first_half(0, range(6))
         fwd_first_half(1, range(6))
         for jt in range(6):
             for part in range(2):
                 empty_first_half(jt, part)
         back_sums(range(3))
+        fwd_first_half(0, (6, 7))
         fwd_first_half(1, (6, 7))
         cast_first_half("scalar", 1, PART)
         for part in range(2):
@@ -454,14 +477,14 @@ def tile_list_minmod_neighbour_fluxes_kernel(
         face_sums(1, (1, 0))
         upper(12)
         limit(14)
-        flux(1, 0)
         limit(15)
         quantise_second_half(2)
-        face_sums(2, (0, 1))
+        last_face_pass(0, slice(0, 512), True, False)
+        last_face_pass(1, slice(0, 256), False, False)
         upper(15)
-        flux(1, 1)
+        flux(1, 0)
         quantise_second_half(3)
-        face_sums(3, (0, 1))
-        for b in (2, 3):
-            for g in range(2):
-                flux(b, g)
+        last_face_pass(1, slice(256, 512), False, True)
+        flux(1, 1)
+        for y in range(4):
+            last_flux(y)

@@ -20,8 +20,8 @@ P = 128
 PASS = 512
 PART = 256
 SHIFT = 14
-BACK_RING = (6, 7, 2, 3)
-OTHER_RING = (4, 5, 0, 1)
+BACK_RING = (0, 1, 2, 3)
+OTHER_RING = (4, 5, 6, 7)
 WARM = 3
 
 SITE = {
@@ -40,14 +40,15 @@ SITE = {
     "raw1_512": 6.25,
     "raw1_768": 11.25,
     "wbq0_0": 10.25,
-    "grp0_0": 46,
-    "dealt_codes": 42.5,
+    "grp0_0": 43,
+    "v1_6": 43,
+    "dealt_codes": 44,
     "grp1_0": 41,
     "grp1_256": 39.5,
     "ident": 16,
     "wx": 17.75,
     "wind0": 22.5,
-    "wind1": 30.5,
+    "wind1": 101,
     "wxs": 8,
     "f0": 88,
     "wbq0_256": 88,
@@ -55,13 +56,15 @@ SITE = {
     "f1": 97,
     "grp0_512": 98,
     "grp1_512": 94,
-    "f2": 46,
-    "f8_f9": 47,
+    "f2": 110,
+    "f8_f9": 109,
     "f5": 114,
     "wbq0_512": 113,
     "wbq1_512": 115,
     "h_late1": 56,
-    "res_pool": 57,
+    "face_sums1": 62,
+    "hq1_1": 62,
+    "res_pool0": 57,
 }
 
 
@@ -199,7 +202,7 @@ def tile_list_minmod_neighbour_fluxes_kernel(
 
         def deal_scales():
             dealt["scales"] = sbuf("dealt_scales", [P, 2, 4, P], U8)
-            nc.gpsimd.tensor_copy(dealt["scales"][:], wfs[:, :, PASS:].rearrange("p a (m t) -> p a t m", t=4))
+            nc.vector.tensor_copy(dealt["scales"][:], wfs[:, :, PASS:].rearrange("p a (m t) -> p a t m", t=4))
 
         def deal_codes():
             dealt["codes"] = sbuf("dealt_codes", [P, 2, 4, P], U16)
@@ -213,8 +216,7 @@ def tile_list_minmod_neighbour_fluxes_kernel(
         def fwd_first_half(a, tiles):
             for jt in tiles:
                 if a == 0:
-                    name = "fwd%d" % jt
-                    fwd[jt] = bank(name, [P, PASS], jt) if jt < 6 else next_upper_bank(name, [P, PASS])
+                    fwd[jt] = bank("fwd%d" % jt, [P, PASS], jt)
                 nc.tensor.matmul_mx(
                     out=fwd[jt][:],
                     lhsT=v[a, jt],
@@ -298,8 +300,8 @@ def tile_list_minmod_neighbour_fluxes_kernel(
             upper(unit - 1)
 
         h_turned = [sbuf("h_turned%d" % x, [P, 2048], BF16) for x in range(2)]
-        hq = [sbuf("hq%d" % s, [P, S], I32) for s in range(2)]
-        hs = [sbuf("hs%d" % s, [P, S], U8) for s in range(2)]
+        hq = {(s, x): sbuf("hq%d_%d" % (s, x), [P, 512], I32) for s in range(2) for x in range(2)}
+        hs = {(s, x): sbuf("hs%d_%d" % (s, x), [P, 512], U8) for s in range(2) for x in range(2)}
         faces = {}
 
         def cells(b):
@@ -317,12 +319,12 @@ def tile_list_minmod_neighbour_fluxes_kernel(
                 )
 
         def quantise_first_half(x):
-            cols = slice(512 * x, 512 * (x + 1))
-            nc.vector.quantize_mx(out=hq[0][:, cols].bitcast(E4M3), scales=hs[0][:, cols], in_=h_turned[x][:])
+            nc.vector.quantize_mx(out=hq[0, x][:].bitcast(E4M3), scales=hs[0, x][:], in_=h_turned[x][:])
 
         def quantise_second_half(b):
             values = h_late[b][:].rearrange("p x c -> p (x c)")
-            nc.vector.quantize_mx(out=hq[1][:, cells(b)].bitcast(E4M3), scales=hs[1][:, cells(b)], in_=values)
+            codes, scales = hq[1, b // 2][:, cells(b % 2)], hs[1, b // 2][:, cells(b % 2)]
+            nc.vector.quantize_mx(out=codes.bitcast(E4M3), scales=scales, in_=values)
 
         def face_sums(b, halves):
             for g in range(2):
@@ -334,8 +336,8 @@ def tile_list_minmod_neighbour_fluxes_kernel(
                             out=faces[b, g][:, y, :],
                             lhsT=wx["codes"][:, s, rows].bitcast(E4M3),
                             lhsT_scale=wx["scales"][:, s, rows],
-                            rhs=hq[s][:, cells(b)].bitcast(E4M3),
-                            rhs_scale=hs[s][:, cells(b)],
+                            rhs=hq[s, 0][:, cells(b)].bitcast(E4M3),
+                            rhs_scale=hs[s, 0][:, cells(b)],
                             start=(s == halves[0] and y == 0),
                             stop=(s == halves[1] and y == 1),
                         )
@@ -346,20 +348,19 @@ def tile_list_minmod_neighbour_fluxes_kernel(
             nc.vector.tensor_tensor(res[:], faces[b, g][:], factor, ALU.mult)
             nc.sync.dma_start(out[256 * g : 256 * (g + 1), cells(b)].rearrange("(y p) j -> p y j", p=P), res[:])
 
-        def last_face_pass(s, cols, start, stop):
+        def last_face_pass(s):
             for y in range(4):
-                if start:
-                    name = "last_face%d" % y
-                    faces[y] = next_upper_bank(name, [P, 512]) if y < 2 else bank(name, [P, 512], BACK_RING[y - 2])
-                rows, these = slice(P * y, P * (y + 1)), slice(512 + cols.start, 512 + cols.stop)
+                if s == 0:
+                    faces[y] = bank("last_face%d" % y, [P, 512], BACK_RING[y])
+                rows = slice(P * y, P * (y + 1))
                 nc.tensor.matmul_mx(
-                    out=faces[y][:, cols],
+                    out=faces[y][:],
                     lhsT=wx["codes"][:, s, rows].bitcast(E4M3),
                     lhsT_scale=wx["scales"][:, s, rows],
-                    rhs=hq[s][:, these].bitcast(E4M3),
-                    rhs_scale=hs[s][:, these],
-                    start=start,
-                    stop=stop,
+                    rhs=hq[s, 1][:].bitcast(E4M3),
+                    rhs_scale=hs[s, 1][:],
+                    start=(s == 0),
+                    stop=(s == 1),
                 )
 
         def last_flux(y):
@@ -367,13 +368,13 @@ def tile_list_minmod_neighbour_fluxes_kernel(
             nc.vector.tensor_tensor(res[:], faces[y][:], winds[1][:, y, :], ALU.mult)
             nc.sync.dma_start(out[P * y : P * (y + 1), 512:], res[:])
 
-        def first_flux_on_gpsimd():
-            sums = sbuf("face_sums", [P, 4, 256], F32)
-            for g in range(2):
-                nc.scalar.copy(sums[:, 2 * g : 2 * g + 2, :], faces[0, g][:])
-            res = sbuf("res_pool", [P, 4, 256], F32)
-            nc.gpsimd.tensor_tensor(res[:], sums[:], winds[0][:, :, cells(0)], ALU.mult)
-            nc.sync.dma_start(out[:, cells(0)].rearrange("(y p) j -> p y j", p=P), res[:])
+        def flux_on_gpsimd(b, banks):
+            sums = sbuf("face_sums%d" % b, [P, 2 * banks, 256], F32)
+            for g in range(banks):
+                nc.scalar.copy(sums[:, 2 * g : 2 * g + 2, :], faces[b, g][:])
+            res = sbuf("res_pool%d" % b, [P, 2 * banks, 256], F32)
+            nc.gpsimd.tensor_tensor(res[:], sums[:], winds[0][:, : 2 * banks, cells(b)], ALU.mult)
+            nc.sync.dma_start(out[: 256 * banks, cells(b)].rearrange("(y p) j -> p y j", p=P), res[:])
 
         gather_words(0, 0, 4)
         gather_words(0, 4, 4)
@@ -383,7 +384,7 @@ def tile_list_minmod_neighbour_fluxes_kernel(
         load_wb(1, PART)
         deal_scales()
         gather_words(1, 0, 2)
-        gather_words(1, 2, 6)
+        gather_words(1, 2, 4)
         cast_first_half("scalar", 0, 0)
         load_wb(0, PASS)
         load_wb(0, PASS + PART)
@@ -391,6 +392,7 @@ def tile_list_minmod_neighbour_fluxes_kernel(
         load_wb(1, PASS)
         load_wb(1, PASS + PART)
         quantise_wb(0, PART)
+        gather_words(1, 6, 2)
         deal_codes()
 
         unread = bank("unread", [P, PASS], 7)
@@ -405,13 +407,12 @@ def tile_list_minmod_neighbour_fluxes_kernel(
                 stop=True,
             )
 
-        fwd_first_half(0, range(6))
+        fwd_first_half(0, range(8))
         fwd_first_half(1, range(6))
         for jt in range(6):
             for part in range(2):
                 empty_first_half(jt, part)
         back_sums(range(3))
-        fwd_first_half(0, (6, 7))
         fwd_first_half(1, (6, 7))
         cast_first_half("scalar", 1, PART)
         for part in range(2):
@@ -438,7 +439,6 @@ def tile_list_minmod_neighbour_fluxes_kernel(
         limit(3)
         back_sums([6])
         load_wind(0)
-        load_wind(1)
         limit(4)
         back_sums([7])
         fwd_second_half((10, 11, 12, 13))
@@ -451,6 +451,7 @@ def tile_list_minmod_neighbour_fluxes_kernel(
         turn((0, 1))
         lower(7)
         quantise_wb(PASS, PASS)
+        load_wind(1)
         upper(6)
         back_sums((8, 9, 10))
 
@@ -459,32 +460,31 @@ def tile_list_minmod_neighbour_fluxes_kernel(
         turn((2, 3))
         fwd_second_half((14, 15))
         empty_second_half((14, 15))
-        for unit in (9, 10):
-            limit(unit)
-            back_sums([unit + 3])
-        lower(11)
+        limit(9)
         quantise_first_half(0)
+        back_sums([12])
+        limit(10)
+        lower(11)
         quantise_second_half(0)
-        face_sums(0, (1, 0))
+        face_sums(0, (0, 1))
+        back_sums([13])
         upper(10)
         back_sums([14])
-        limit(12)
+        upper(11)
         back_sums([15])
-        lower(13)
         quantise_first_half(1)
-        first_flux_on_gpsimd()
+        flux_on_gpsimd(0, 2)
         quantise_second_half(1)
         face_sums(1, (1, 0))
-        upper(12)
-        limit(14)
-        limit(15)
-        quantise_second_half(2)
-        last_face_pass(0, slice(0, 512), True, False)
-        last_face_pass(1, slice(0, 256), False, False)
+        flux_on_gpsimd(1, 1)
+        lower(12)
+        for unit in (13, 14, 15):
+            limit(unit)
+        last_face_pass(0)
         upper(15)
-        flux(1, 0)
+        quantise_second_half(2)
         quantise_second_half(3)
-        last_face_pass(1, slice(256, 512), False, True)
+        last_face_pass(1)
         flux(1, 1)
         for y in range(4):
             last_flux(y)

from contextlib import ExitStack

import concourse.mybir as mybir
from concourse.masks import make_identity

K, T, S, H, N = 1024, 2048, 1024, 1024, 512
FLOPS = 2 * K * H * S * 2 + 2 * H * N * S

F32 = mybir.dt.float32
BF16 = mybir.dt.bfloat16
I32 = mybir.dt.int32
U32 = mybir.dt.uint32
U16 = mybir.dt.uint16
U8 = mybir.dt.uint8
E4M3 = mybir.dt.float8_e4m3fn_x4
E2M1 = mybir.dt.float4_e2m1fn_x4
ALU = mybir.AluOpType

P = 128
PASS = 512
PART = 256
SHIFT = 14
BACK_RING = (0, 1, 2, 3)
OTHER_RING = (4, 5, 6, 7)
WARM = 3

SITE = {
    "blank": 74,
    "wf0": 73,
    "tab1": 75,
    "win": 30,
    "raw0_0": 29,
    "tab0": 14,
    "raw1_0": 10.125,
    "wf1": 15.75,
    "raw0_256": 17.75,
    "raw1_256": 21.75,
    "raw0_512": 26.5,
    "raw0_768": 30.5,
    "raw1_512": 6.25,
    "raw1_768": 11.25,
    "wbq0_0": 10.25,
    "grp0_0": 43,
    "v1_6": 43,
    "dealt_codes": 44,
    "grp1_0": 41,
    "grp1_256": 39.5,
    "ident": 16,
    "wx": 17.75,
    "wind0": 22.5,
    "wind1": 101,
    "wxs": 8,
    "f0": 88,
    "wbq0_256": 88,
    "wbq1_256": 89,
    "f1": 97,
    "grp0_512": 98,
    "grp1_512": 94,
    "f2": 110,
    "f8_f9": 109,
    "f5": 114,
    "wbq0_512": 113,
    "wbq1_512": 115,
    "h_late1": 56,
    "face_sums1": 62,
    "hq1_1": 62,
    "res_pool0": 57,
}


def tile_list_minmod_neighbour_fluxes_kernel(
    tc, tab_words, tab_scales, offs, wb, wf_words, wf_scales, wx_words, wx_scales, wind, out
):
    nc = tc.nc
    with ExitStack() as ctx:
        keep = ctx.enter_context(tc.tile_pool(name="keep", bufs=1))
        shared = ctx.enter_context(tc.tile_pool(name="shared", bufs=1))
        psum = ctx.enter_context(tc.psum_pool(name="psum", bufs=1))

        def sbuf(name, shape, dtype):
            if name in SITE:
                return shared.tile(shape, dtype, name=name, align_bytes=64, offset=int(1024 * SITE[name]))
            return keep.tile(shape, dtype, name=name, tag=name, align_bytes=64)

        def bank(name, shape, number):
            return psum.tile(shape, F32, name=name, tag="bank%d" % number)

        upper_banks = []

        def next_upper_bank(name, shape):
            upper_banks.append(name)
            return bank(name, shape, OTHER_RING[(len(upper_banks) - 1) % 4])

        raw, wf, tab, winds, wx = {}, {}, {}, {}, {}

        def load_tab(a):
            tab[a] = sbuf("tab%d" % a, [P, T], I32)
            nc.sync.dma_start(tab[a][:], tab_words[a].rearrange("p t i -> p (t i)").bitcast(I32))

        def load_wb(a, c0):
            raw[a, c0] = sbuf("raw%d_%d" % (a, c0), [P, 4, PART], F32)
            rows = wb[PASS * a : PASS * (a + 1), c0 : c0 + PART]
            nc.sync.dma_start(raw[a, c0][:], rows.rearrange("(p i) c -> p i c", i=4))

        def load_wf(s):
            wf[s] = sbuf("wf%d" % s, [P, 2, H], U8)
            words = wf_words.bitcast(I32)[:, :, 256 * s : 256 * (s + 1)]
            nc.sync.dma_start(wf[s][:].bitcast(I32), words.rearrange("a p c -> p a c"))

        def load_plane(plane, scales):
            for r in range(4):
                rows = scales.bitcast(I32)[:, r::4, :].rearrange("a d c -> d a c")
                nc.sync.dma_start(plane[:].bitcast(I32)[r:P:32], rows)

        def load_wx():
            wx["codes"] = sbuf("wx", [P, 2, N], I32)
            nc.sync.dma_start(wx["codes"][:], wx_words.rearrange("a p c i -> p a (c i)").bitcast(I32))

        def load_wx_scales():
            wx["scales"] = sbuf("wxs", [P, 2, N], U8)
            nc.gpsimd.memset(wx["scales"][:].bitcast(I32), 0)
            load_plane(wx["scales"], wx_scales)

        def load_wind(x):
            winds[x] = sbuf("wind%d" % x, [P, 4, 512], F32)
            nc.sync.dma_start(winds[x][:], wind[:, 512 * x : 512 * (x + 1)].rearrange("(y p) j -> p y j", p=P))

        offsets = keep.tile([P, S // 16], U16, name="offsets")
        nc.sync.dma_start(offsets[:], offs)

        win = sbuf("win", [P, T], U8)
        win_words = win[:].bitcast(I32)
        by_pass = tab_scales.bitcast(I32)
        all_rows = by_pass.rearrange("a q c -> (a q) c")
        nc.sync.dma_start(win_words[0:P:4, :], by_pass.rearrange("a q c -> q a c"))
        nc.sync.dma_start(win_words[2:P:4, :], by_pass[0][0::2].unsqueeze(1).to_broadcast([8, 4, T // 4]))
        nc.sync.dma_start(win_words[1:P:4, :], all_rows[1:17].unsqueeze(1).to_broadcast([16, 2, T // 4]))
        nc.sync.dma_start(win_words[3:P:4, :], all_rows[0:16].unsqueeze(1).to_broadcast([16, 2, T // 4]))
        load_tab(0)

        blank = sbuf("blank", [P, H // 2], I32)
        nc.vector.memset(blank[:], 0)
        wfs = sbuf("wfs", [P, 2, H], U8)
        nc.vector.tensor_copy(wfs[:].bitcast(I32).rearrange("p a c -> p (a c)"), blank[:])
        load_plane(wfs, wf_scales)
        load_wf(0)
        load_tab(1)

        vs = [sbuf("vs%d" % a, [P, S], U8) for a in range(2)]
        for a in range(2):
            nc.vector.memset(vs[a][:].bitcast(I32), 0)
        picked_rows = sbuf("picked_rows", [P, S], U8)
        nc.vector.tensor_copy(picked_rows[:], win[:].indirect(offsets[:]))
        nc.sync.dma_start(vs[0][:].bitcast(I32)[0:100, :], picked_rows[:].bitcast(I32)[SHIFT : SHIFT + 100, :])
        load_wb(0, 0)
        for r in range(4):
            nc.sync.dma_start(vs[1][:].bitcast(I32)[r:P:32, :], picked_rows[:].bitcast(I32)[8 * r + 4 : P : 32, :])

        v = {}

        def gather_words(a, first, count):
            picked = sbuf("v%d_%d" % (a, first), [P, P * count], I32)
            window = tab[a][:].bitcast(U32).indirect(offsets[:, 8 * first : 8 * (first + count)])
            nc.vector.tensor_copy(picked[:].bitcast(U32), window)
            for x in range(count):
                v[a, first + x] = picked[:, P * x : P * (x + 1)].bitcast(E4M3)

        def v_scales(a, jt):
            return vs[a][:, P * jt : P * (jt + 1)]

        grouped, wbq, wbs = {}, {}, {}

        def cast(engine, dst, src):
            if engine == "gpsimd":
                for u in range(2):
                    into = dst[:, :, :, u].rearrange("p m i e -> p m e i")
                    values = src[:, :, :, u].rearrange("p m i e -> p m e i")
                    nc.gpsimd.tensor_scalar(into, values, 1.0, 0.0, ALU.mult, ALU.add)
            elif engine == "vector":
                nc.vector.tensor_copy(dst, src)
            else:
                nc.scalar.copy(dst, src)

        def cast_first_half(engine, a, c0):
            grouped[a, c0] = sbuf("grp%d_%d" % (a, c0), [P, 4 * PART], BF16)
            dst = grouped[a, c0][:].rearrange("p (u m e i) -> p m i u e", u=2, e=2, i=4)
            cast(engine, dst, raw[a, c0][:].rearrange("p i (m u e) -> p m i u e", u=2, e=2))

        def cast_second_half(engine, a, x):
            if x == 0:
                grouped[a, PASS] = sbuf("grp%d_%d" % (a, PASS), [P, 4 * PASS], BF16)
            dst = grouped[a, PASS][:].rearrange("p (u e m i) -> p m i u e", u=2, e=2, i=4)[:, 64 * x : 64 * (x + 1)]
            cast(engine, dst, raw[a, PASS + PART * x][:].rearrange("p i (m u e) -> p m i u e", u=2, e=2))

        def quantise_wb(c0, width):
            for a in range(2):
                wbq[a, c0] = sbuf("wbq%d_%d" % (a, c0), [P, width], I32)
                wbs[a, c0] = sbuf("wbs%d_%d" % (a, c0), [P, width], U8)
                nc.vector.quantize_mx(out=wbq[a, c0][:].bitcast(E4M3), scales=wbs[a, c0][:], in_=grouped[a, c0][:])

        dealt = {}

        def deal_scales():
            dealt["scales"] = sbuf("dealt_scales", [P, 2, 4, P], U8)
            nc.vector.tensor_copy(dealt["scales"][:], wfs[:, :, PASS:].rearrange("p a (m t) -> p a t m", t=4))

        def deal_codes():
            dealt["codes"] = sbuf("dealt_codes", [P, 2, 4, P], U16)
            nc.vector.tensor_copy(dealt["codes"][:], wf[1][:].bitcast(U16).rearrange("p a (m t) -> p a t m", t=4))

        f = {unit: sbuf("f%d" % unit, [P, 4, P], F32)[:] for unit in range(8)}
        h_early = [sbuf("h_early%d" % b, [P, 4, 256], BF16) for b in range(4)]
        h_late = [sbuf("h_late%d" % b, [P, 2, PASS], BF16) for b in range(4)]
        fwd, back = {}, {}

        def fwd_first_half(a, tiles):
            for jt in tiles:
                if a == 0:
                    fwd[jt] = bank("fwd%d" % jt, [P, PASS], jt)
                nc.tensor.matmul_mx(
                    out=fwd[jt][:],
                    lhsT=v[a, jt],
                    lhsT_scale=v_scales(a, jt),
                    rhs=wf[0][:, a, :].bitcast(E2M1),
                    rhs_scale=wfs[:, a, 0:PASS],
                    start=(a == 0),
                    stop=(a == 1),
                )

        def empty_first_half(jt, part):
            dst = f[4 * part + jt // 2][:, 2 * (jt % 2) : 2 * (jt % 2) + 2, :].rearrange("p u (m e) -> p u m e", e=2)
            src = fwd[jt][:, PART * part : PART * (part + 1)].rearrange("p (m u e) -> p u m e", u=2, e=2)
            nc.scalar.copy(dst, src)

        def second_half_sums(sums, jt, weights):
            for a in range(2):
                for t in range(4):
                    codes, scales = weights(a, t)
                    nc.tensor.matmul_mx(
                        out=sums[:, t, :],
                        lhsT=codes,
                        lhsT_scale=scales,
                        rhs=v[a, jt],
                        rhs_scale=v_scales(a, jt),
                        start=(a == 0 and t == 0),
                        stop=(a == 1 and t == 3),
                    )
            return sums[:].rearrange("p t c -> p c t")

        def wf_run(a, t):
            return dealt["codes"][:, a, t, :].bitcast(E2M1), dealt["scales"][:, a, t, :]

        def wb_run(a, t):
            return wbq[a, PASS][:, P * t : P * (t + 1)].bitcast(E4M3), wbs[a, PASS][:, P * t : P * (t + 1)]

        def fwd_second_half(units):
            for unit in units:
                fwd[unit] = second_half_sums(next_upper_bank("fwd%d" % unit, [P, 4, P]), unit - 8, wf_run)

        def empty_second_half(units):
            for unit in units:
                if unit not in f:
                    f[unit] = sbuf("f%d" % unit, [P, P, 4], F32)[:]
                nc.scalar.copy(f[unit], fwd[unit])

        def back_sums(units):
            for unit in units:
                if unit >= 8:
                    back[unit] = second_half_sums(bank("back%d" % unit, [P, 4, P], BACK_RING[unit % 4]), unit - 8, wb_run)
                    continue
                sums = bank("back%d" % unit, [P, 2 * PART], BACK_RING[unit % 4])
                c0, b = PART * (unit // 4), unit % 4
                for a in range(2):
                    for x in range(2):
                        nc.tensor.matmul_mx(
                            out=sums[:, PART * x : PART * (x + 1)],
                            lhsT=v[a, 2 * b + x],
                            lhsT_scale=v_scales(a, 2 * b + x),
                            rhs=wbq[a, c0][:].bitcast(E4M3),
                            rhs_scale=wbs[a, c0][:],
                            start=(a == 0 and x == 0),
                            stop=(a == 1 and x == 1),
                        )
                back[unit] = sums[:].rearrange("p (x c) -> p x c", c=P)

        def lower(unit):
            nc.vector.scalar_tensor_tensor(
                out=f[unit], in0=back[unit], scalar=0.0, in1=f[unit], op0=ALU.min, op1=ALU.max
            )

        def upper(unit):
            if unit >= 8:
                h = h_late[(unit - 8) // 2][:, unit % 2, :].rearrange("p (c t) -> p c t", t=4)
            else:
                h = h_early[unit % 4][:, :, P * (unit // 4) : P * (unit // 4 + 1)]
            nc.vector.scalar_tensor_tensor(out=h, in0=back[unit], scalar=0.0, in1=f[unit], op0=ALU.max, op1=ALU.min)

        def limit(unit):
            lower(unit)
            upper(unit - 1)

        h_turned = [sbuf("h_turned%d" % x, [P, 2048], BF16) for x in range(2)]
        hq = {(s, x): sbuf("hq%d_%d" % (s, x), [P, 512], I32) for s in range(2) for x in range(2)}
        hs = {(s, x): sbuf("hs%d_%d" % (s, x), [P, 512], U8) for s in range(2) for x in range(2)}
        faces = {}

        def cells(b):
            return slice(256 * b, 256 * (b + 1))

        def turn(pairs):
            for b in pairs:
                turned = next_upper_bank("turned%d" % b, [P, 4, P])
                for y in (1, 0):
                    for u in range(2):
                        nc.tensor.transpose(turned[:, 2 * y + u, :], h_early[b][:, 2 * y + u, :].bitcast(F32), ident[:])
                dst = h_turned[b // 2][:, 1024 * (b % 2) : 1024 * (b % 2 + 1)].bitcast(F32)
                nc.scalar.copy(
                    dst.rearrange("p (y j u) -> p y j u", y=2, u=2), turned[:].rearrange("p (y u) j -> p y j u", u=2)
                )

        def quantise_first_half(x):
            nc.vector.quantize_mx(out=hq[0, x][:].bitcast(E4M3), scales=hs[0, x][:], in_=h_turned[x][:])

        def quantise_second_half(b):
            values = h_late[b][:].rearrange("p x c -> p (x c)")
            codes, scales = hq[1, b // 2][:, cells(b % 2)], hs[1, b // 2][:, cells(b % 2)]
            nc.vector.quantize_mx(out=codes.bitcast(E4M3), scales=scales, in_=values)

        def face_sums(b, halves):
            for g in range(2):
                faces[b, g] = next_upper_bank("face%d_%d" % (b, g), [P, 2, 256])
                for s in halves:
                    for y in range(2):
                        rows = slice(P * (2 * g + y), P * (2 * g + y + 1))
                        nc.tensor.matmul_mx(
                            out=faces[b, g][:, y, :],
                            lhsT=wx["codes"][:, s, rows].bitcast(E4M3),
                            lhsT_scale=wx["scales"][:, s, rows],
                            rhs=hq[s, 0][:, cells(b)].bitcast(E4M3),
                            rhs_scale=hs[s, 0][:, cells(b)],
                            start=(s == halves[0] and y == 0),
                            stop=(s == halves[1] and y == 1),
                        )

        def flux(b, g):
            res = sbuf("res%d_%d" % (b, g), [P, 2, 256], F32)
            factor = winds[b // 2][:, 2 * g : 2 * g + 2, cells(b % 2)]
            nc.vector.tensor_tensor(res[:], faces[b, g][:], factor, ALU.mult)
            nc.sync.dma_start(out[256 * g : 256 * (g + 1), cells(b)].rearrange("(y p) j -> p y j", p=P), res[:])

        def last_face_pass(s):
            for y in range(4):
                if s == 0:
                    faces[y] = bank("last_face%d" % y, [P, 512], BACK_RING[y])
                rows = slice(P * y, P * (y + 1))
                nc.tensor.matmul_mx(
                    out=faces[y][:],
                    lhsT=wx["codes"][:, s, rows].bitcast(E4M3),
                    lhsT_scale=wx["scales"][:, s, rows],
                    rhs=hq[s, 1][:].bitcast(E4M3),
                    rhs_scale=hs[s, 1][:],
                    start=(s == 0),
                    stop=(s == 1),
                )

        def last_flux(y):
            res = sbuf("last_res%d" % y, [P, 512], F32)
            nc.vector.tensor_tensor(res[:], faces[y][:], winds[1][:, y, :], ALU.mult)
            nc.sync.dma_start(out[P * y : P * (y + 1), 512:], res[:])

        def flux_on_gpsimd(b, banks):
            sums = sbuf("face_sums%d" % b, [P, 2 * banks, 256], F32)
            for g in range(banks):
                nc.scalar.copy(sums[:, 2 * g : 2 * g + 2, :], faces[b, g][:])
            res = sbuf("res_pool%d" % b, [P, 2 * banks, 256], F32)
            nc.gpsimd.tensor_tensor(res[:], sums[:], winds[0][:, : 2 * banks, cells(b)], ALU.mult)
            nc.sync.dma_start(out[: 256 * banks, cells(b)].rearrange("(y p) j -> p y j", p=P), res[:])

        gather_words(0, 0, 4)
        gather_words(0, 4, 4)
        load_wb(1, 0)
        load_wf(1)
        load_wb(0, PART)
        load_wb(1, PART)
        deal_scales()
        gather_words(1, 0, 2)
        gather_words(1, 2, 4)
        cast_first_half("scalar", 0, 0)
        load_wb(0, PASS)
        load_wb(0, PASS + PART)
        cast_first_half("vector", 1, 0)
        load_wb(1, PASS)
        load_wb(1, PASS + PART)
        quantise_wb(0, PART)
        gather_words(1, 6, 2)
        deal_codes()

        unread = bank("unread", [P, PASS], 7)
        for jt in range(WARM):
            nc.tensor.matmul_mx(
                out=unread[:],
                lhsT=v[0, jt],
                lhsT_scale=wfs[:, 0, 0:P],
                rhs=wf[0][:, 0, :].bitcast(E2M1),
                rhs_scale=wfs[:, 0, 0:PASS],
                start=True,
                stop=True,
            )

        fwd_first_half(0, range(8))
        fwd_first_half(1, range(6))
        for jt in range(6):
            for part in range(2):
                empty_first_half(jt, part)
        back_sums(range(3))
        fwd_first_half(1, (6, 7))
        cast_first_half("scalar", 1, PART)
        for part in range(2):
            for jt in (6, 7):
                empty_first_half(jt, part)
        cast_first_half("gpsimd", 0, PART)
        back_sums([3])
        ident = sbuf("ident", [P, P], F32)
        make_identity(nc, ident[:])

        lower(0)
        fwd_second_half((8, 9))
        load_wx()
        limit(1)
        cast_second_half("scalar", 0, 0)
        cast_second_half("gpsimd", 0, 1)
        limit(2)
        quantise_wb(PART, PART)
        back_sums((4, 5))
        f8_f9 = sbuf("f8_f9", [P, 2, P, 4], F32)
        f[8], f[9] = f8_f9[:, 0], f8_f9[:, 1]
        empty_second_half((8, 9))
        cast_second_half("gpsimd", 1, 0)
        limit(3)
        back_sums([6])
        load_wind(0)
        limit(4)
        back_sums([7])
        fwd_second_half((10, 11, 12, 13))
        empty_second_half((10, 11))
        cast_second_half("scalar", 1, 1)
        load_wx_scales()
        limit(5)
        empty_second_half((12, 13))
        limit(6)
        turn((0, 1))
        lower(7)
        quantise_wb(PASS, PASS)
        load_wind(1)
        upper(6)
        back_sums((8, 9, 10))

        limit(8)
        back_sums([11])
        turn((2, 3))
        fwd_second_half((14, 15))
        empty_second_half((14, 15))
        limit(9)
        quantise_first_half(0)
        back_sums([12])
        limit(10)
        lower(11)
        quantise_second_half(0)
        face_sums(0, (0, 1))
        back_sums([13])
        upper(10)
        back_sums([14])
        upper(11)
        back_sums([15])
        quantise_first_half(1)
        flux_on_gpsimd(0, 2)
        quantise_second_half(1)
        face_sums(1, (1, 0))
        flux_on_gpsimd(1, 1)
        lower(12)
        for unit in (13, 14, 15):
            limit(unit)
        last_face_pass(0)
        upper(15)
        quantise_second_half(2)
        quantise_second_half(3)
        last_face_pass(1)
        flux(1, 1)
        for y in range(4):
            last_flux(y)
